import numpy as np
import ml_dtypes


def mxq(x, axis, fmt="e4m3"):
    dtype, down = {"e4m3": (ml_dtypes.float8_e4m3fn, 7), "e5m2": (ml_dtypes.float8_e5m2, 14)}[fmt]
    v = np.moveaxis(np.asarray(x, np.float32).astype(ml_dtypes.bfloat16).astype(np.float64), axis, -1)
    blocks = v.reshape(v.shape[:-1] + (-1, 32))
    amax = np.abs(blocks).max(-1, keepdims=True)
    byte = np.maximum(np.where(amax > 0, np.frexp(amax)[1] - 1 + 127, 0) - down, 1)
    scale = np.exp2(byte - 127.0)
    codes = (blocks / scale).astype(np.float32).astype(dtype).astype(np.float64)
    return np.moveaxis((codes * scale).reshape(v.shape), -1, axis)


WIDE = False


def mx_kscale(k):
    if not WIDE:
        return np.ones(k)
    levels = np.array([24, -24, 12, -12, 0])
    if k % 512:
        return np.exp2(np.random.permutation(np.resize(levels, k // 32))).repeat(32)
    a = np.empty((k // 512, 16))
    for p in range(k // 512):
        a[p, :8] = np.random.permutation(np.resize(levels, 8))
        for g in range(8):
            far = levels[np.abs(levels - a[p, g]) >= 10]
            a[p, g + 8] = far[np.random.randint(len(far))]
    return np.exp2(a.ravel()).repeat(32)


def f64(x):
    return np.asarray(x).astype(np.float64)


def striped(idx):
    return np.tile(idx.reshape(-1, 16).T, (8, 1)).astype(np.uint16)


def unstriped(offs):
    return offs[:16].T.reshape(-1).astype(np.int64)


E2M1 = np.array([0.0, 0.5, 1.0, 1.5, 2.0, 3.0, 4.0, 6.0, -0.0, -0.5, -1.0, -1.5, -2.0, -3.0, -4.0, -6.0])


def pack_weight(w, fmt):
    k, n = w.shape
    w = f64(np.asarray(w, np.float32).astype(ml_dtypes.bfloat16)).reshape(k // 32, 32, n)
    amax = np.abs(w).max(1)
    if fmt == "e4m3":
        byte = np.frexp(amax)[1] - 1 + 127 - 7
    else:
        mant, ex = np.frexp(amax / 6.0)
        byte = np.where(mant > 0.5, ex, ex - 1) + 127
    byte = np.clip(np.where(amax > 0, byte, 1), 1, 254)
    scaled = (w * np.exp2(127.0 - byte)[:, None, :]).reshape(k, n).astype(np.float32)
    by_word = np.ascontiguousarray(scaled.reshape(k // 512, 128, 4, n).transpose(0, 1, 3, 2))
    if fmt == "e4m3":
        words = by_word.astype(ml_dtypes.float8_e4m3fn).view(np.uint8)
    else:
        c = by_word.astype(ml_dtypes.float4_e2m1fn).view(np.uint8) & 0xF
        words = (c[..., 0::2] | (c[..., 1::2] << 4)).reshape(k // 512, 128, 2 * n)
    return np.ascontiguousarray(words), np.ascontiguousarray(byte.astype(np.uint8).reshape(k // 512, 16, n))


def unpack_weight(words, scales, fmt):
    g, _, n = scales.shape
    words = np.ascontiguousarray(words).reshape(g, 128, n, -1)
    if fmt == "e4m3":
        vals = words.view(ml_dtypes.float8_e4m3fn).astype(np.float64)
    else:
        nib = np.empty((g, 128, n, 4), np.uint8)
        nib[..., 0::2] = words & 0xF
        nib[..., 1::2] = words >> 4
        vals = E2M1[nib]
    vals = vals * np.repeat(np.exp2(scales.astype(np.float64) - 127.0), 8, axis=1)[..., None]
    return vals.transpose(0, 1, 3, 2).reshape(g * 512, n)


K, R, N, T, J = 512, 1024, 256, 4096, 512


def setup_inputs():
    n = np.random.standard_normal
    s = mx_kscale(K)[:, None]
    u = mx_kscale(R)[:, None]
    wd = n((R, N)) / np.sqrt(R) / u
    p_tab = pack_weight(n((K, T)) * s, "e4m3")
    p_w = pack_weight(n((K, R)) / np.sqrt(K) / s * u.T, "e4m3")
    p_wd8 = pack_weight(wd[:512], "e4m3")
    p_wd4 = pack_weight(wd[512:], "e2m1")
    return {
        "tab_words": p_tab[0],
        "tab_scales": p_tab[1],
        "c": (n((K, J)) * s).astype(np.float32),
        "w_words": p_w[0],
        "w_scales": p_w[1],
        "wc": (n((K, R)) / np.sqrt(K) / s * u.T).astype(np.float32),
        "wd8_words": p_wd8[0],
        "wd8_scales": p_wd8[1],
        "wd4_words": p_wd4[0],
        "wd4_scales": p_wd4[1],
        "offs": striped(np.concatenate([np.random.permutation(T)[:J] for _ in range(2)])),
    }


def reference(tab_words, tab_scales, c, w_words, w_scales, wc, wd8_words, wd8_scales, wd4_words, wd4_scales, offs):
    idx = unstriped(offs).reshape(2, J)
    tab_ = unpack_weight(tab_words, tab_scales, "e4m3")[:, idx]
    c_ = mxq(f64(c), 0, "e4m3")
    w_ = unpack_weight(w_words, w_scales, "e4m3")
    a0 = w_.T @ tab_[:, 0]
    a1 = w_.T @ tab_[:, 1]
    wc_ = mxq(f64(wc), 0, "e4m3")
    ac = wc_.T @ c_
    h = np.maximum(np.maximum(a0, a1) + ac, 0.0)
    h_ = mxq(h, 0, "e4m3")
    wd8_ = unpack_weight(wd8_words, wd8_scales, "e4m3")
    wd4_ = unpack_weight(wd4_words, wd4_scales, "e2m1")
    y = wd8_.T @ h_[:512] + wd4_.T @ h_[512:]
    return y

@@ -1,0 +1,260 @@
+from contextlib import ExitStack
+
+import concourse.mybir as mybir
+
+K, R, N, T, J = 512, 1024, 256, 4096, 512
+FLOPS = 3 * 2 * K * R * J + 2 * R * N * J
+
+F32 = mybir.dt.float32
+BF16 = mybir.dt.bfloat16
+I32 = mybir.dt.int32
+U32 = mybir.dt.uint32
+U16 = mybir.dt.uint16
+U8 = mybir.dt.uint8
+FP8X4 = mybir.dt.float8_e4m3fn_x4
+FP4X4 = mybir.dt.float4_e2m1fn_x4
+ALU = mybir.AluOpType
+
+P = 128
+PACK = 4
+HALF = P * PACK
+JB = 128
+N_JB = J // JB
+FUSED = ((1, 2), (1, 3))
+
+
+def load_scale_rows(queue, plane, rows):
+    for q in range(4):
+        queue.dma_start(out=plane[32 * q : 32 * q + 4, :].bitcast(I32), in_=rows[4 * q : 4 * q + 4, :].bitcast(I32))
+
+
+def tile_list_pnet_mix_none_kernel(
+    tc, tab_words, tab_scales, c, w_words, w_scales, wc, wd8_words, wd8_scales, wd4_words, wd4_scales, offs, out
+):
+    nc = tc.nc
+    with ExitStack() as ctx:
+        keep = ctx.enter_context(tc.tile_pool(name="keep", bufs=1))
+        ring = ctx.enter_context(tc.tile_pool(name="ring", bufs=3))
+        shared = ctx.enter_context(tc.tile_pool(name="shared", bufs=1))
+        psum = ctx.enter_context(tc.psum_pool(name="psum", bufs=2))
+
+        offsets = keep.tile([P, 2 * J // 16], U16, name="offsets")
+        tab_w = keep.tile([P, T], U32, name="tab_w", align_bytes=64)
+        ws_raw = shared.tile([P, HALF], U8, name="ws_raw", align_bytes=64, offset=3840)
+        tab_s = shared.tile([P, T], U8, name="tab_s", align_bytes=64, offset=8192)
+        w_raw = shared.tile([P, R], I32, name="w_raw", align_bytes=64, offset=33280)
+
+        nc.vector.memset(tab_s[:].bitcast(I32), 0)
+        nc.gpsimd.memset(ws_raw[:].bitcast(I32), 0)
+
+        nc.sync.dma_start(offsets[:], offs)
+        nc.sync.dma_start(out=tab_w[:].bitcast(I32), in_=tab_words[0].rearrange("p t i -> p (t i)").bitcast(I32))
+        nc.sync.dma_start(out=w_raw[:], in_=w_words[0].rearrange("p r i -> p (r i)").bitcast(I32))
+        load_scale_rows(nc.scalar, tab_s, tab_scales[0])
+        ws_rows = w_scales[0].bitcast(I32).rearrange("q (g r) -> g q r", g=2)
+        for q in range(4):
+            nc.gpsimd.dma_start(out=ws_raw[32 * q : 32 * q + 8, :].bitcast(I32), in_=ws_rows[:, 4 * q : 4 * q + 4, :])
+
+        nb_s = keep.tile([P, 2 * J], U8, name="nb_s", align_bytes=64)
+        nc.vector.tensor_copy(nb_s[:], tab_s[:].indirect(offsets[:]))
+
+        raw = shared.tile([P, 6, PACK, 256], F32, name="raw", align_bytes=64, offset=8704)
+        c_raw = [raw[:, 2 + u] for u in range(2)]
+        wc_raw = [raw[:, slot] for slot in (0, 1, 4, 5)]
+        c_rows = c.rearrange("(p i) j -> p i j", i=PACK)
+        wc_rows = wc.rearrange("(p i) r -> p i r", i=PACK)
+        for u in range(2):
+            nc.sync.dma_start(out=wc_raw[u], in_=wc_rows[:, :, 256 * u : 256 * (u + 1)])
+        for u in range(2):
+            nc.sync.dma_start(out=c_raw[u], in_=c_rows[:, :, 256 * u : 256 * (u + 1)])
+        for u in range(2, 4):
+            nc.sync.dma_start(out=wc_raw[u], in_=wc_rows[:, :, 256 * u : 256 * (u + 1)])
+
+        w_s = shared.tile([P, HALF], U8, name="w_s", align_bytes=64, offset=8192)
+        nc.vector.tensor_copy(
+            w_s[:].rearrange("p (t m e) -> p m t e", t=PACK, e=16),
+            ws_raw[:].rearrange("p (m e t) -> p m t e", t=PACK, e=16),
+        )
+        nb_all = shared.tile([P, 2 * J], U32, name="nb_all", align_bytes=64, offset=0)
+        w_all = shared.tile([P, R], I32, name="w_all", align_bytes=64, offset=4096)
+        nb_w = [nb_all[:, J * a : J * (a + 1)] for a in range(2)]
+        w_w = [w_all[:, HALF * g : HALF * (g + 1)] for g in range(2)]
+
+        def gather_words(a):
+            nc.vector.tensor_copy(nb_w[a], tab_w[:].indirect(offsets[:, 32 * a : 32 * (a + 1)]))
+
+        def order_w(g):
+            nc.vector.tensor_copy(
+                w_w[g].rearrange("p (t m e) -> p m t e", t=PACK, e=4),
+                w_raw[:, HALF * g : HALF * (g + 1)].rearrange("p (m e t) -> p m t e", t=PACK, e=4),
+            )
+
+        gather_words(0)
+        order_w(0)
+        gather_words(1)
+        order_w(1)
+
+        wd8_w = shared.tile([P, N], U32, name="wd8_w", align_bytes=64, offset=33280)
+        wd4_w = shared.tile([P, 2 * N], U8, name="wd4_w", align_bytes=64, offset=34304)
+        wd_s = shared.tile([P, 2 * N], U8, name="wd_s", align_bytes=64, offset=34816)
+        nc.sync.dma_start(out=wd8_w[:].bitcast(I32), in_=wd8_words[0].rearrange("p n i -> p (n i)").bitcast(I32))
+        nc.sync.dma_start(out=wd4_w[:].bitcast(I32), in_=wd4_words[0].bitcast(I32))
+        load_scale_rows(nc.sync, wd_s[:, 0:N], wd8_scales[0])
+        load_scale_rows(nc.sync, wd_s[:, N : 2 * N], wd4_scales[0])
+
+        def neighbour_passes(bank, a, g, b, closed):
+            for t in range(PACK):
+                nc.tensor.matmul_mx(
+                    out=bank[:, t, :],
+                    lhsT=w_w[g][:, P * t : P * (t + 1)].bitcast(FP8X4),
+                    lhsT_scale=w_s[4 * g : P, P * t : P * (t + 1)],
+                    rhs=nb_w[a][:, JB * b : JB * (b + 1)].bitcast(FP8X4),
+                    rhs_scale=nb_s[:, J * a + JB * b : J * a + JB * (b + 1)],
+                    start=closed or t == 0,
+                    stop=closed,
+                )
+
+        c_bf = [keep.tile([P, J // 2, PACK], BF16, name=f"c_bf{u}", align_bytes=64) for u in range(2)]
+        c_w = [keep.tile([P, J // 2], U32, name=f"c_w{u}", align_bytes=64) for u in range(2)]
+        c_s = [keep.tile([P, J // 2], U8, name=f"c_s{u}", align_bytes=64) for u in range(2)]
+        wc_bf = [keep.tile([P, PACK, P, PACK], BF16, name=f"wc_bf{g}", align_bytes=64) for g in range(2)]
+        wc_w = [keep.tile([P, HALF], U32, name=f"wc_w{g}", align_bytes=64) for g in range(2)]
+        wc_s = [keep.tile([P, HALF], U8, name=f"wc_s{g}", align_bytes=64) for g in range(2)]
+
+        def round_c(u):
+            nc.scalar.copy(
+                c_bf[u][:].rearrange("p (q e) i -> p q i e", e=4),
+                c_raw[u].rearrange("p i (q e) -> p q i e", e=4),
+            )
+
+        def round_wc(u):
+            g, v = divmod(u, 2)
+            nc.scalar.copy(
+                wc_bf[g][:, :, 64 * v : 64 * (v + 1), :].rearrange("p t m i -> p m i t"),
+                wc_raw[u].rearrange("p i (m t) -> p m i t", t=PACK),
+            )
+
+        def quantize_c(u):
+            nc.vector.quantize_mx(out=c_w[u][:].bitcast(FP8X4), scales=c_s[u][:], in_=c_bf[u][:].rearrange("p j i -> p (j i)"))
+
+        def quantize_wc(g):
+            nc.vector.quantize_mx(out=wc_w[g][:].bitcast(FP8X4), scales=wc_s[g][:], in_=wc_bf[g][:].rearrange("p t m i -> p (t m i)"))
+
+        def own_passes(bank, g, b, closed):
+            u, v = divmod(b, 2)
+            for t in range(PACK):
+                nc.tensor.matmul_mx(
+                    out=bank[:, t, :],
+                    lhsT=wc_w[g][:, P * t : P * (t + 1)].bitcast(FP8X4),
+                    lhsT_scale=wc_s[g][:, P * t : P * (t + 1)],
+                    rhs=c_w[u][:, JB * v : JB * (v + 1)].bitcast(FP8X4),
+                    rhs_scale=c_s[u][:, JB * v : JB * (v + 1)],
+                    start=closed,
+                    stop=closed or t == PACK - 1,
+                )
+
+        def by_point(bank):
+            return bank[:].rearrange("p t j -> p j t")
+
+        blocks = [(g, b) for g in range(2) for b in range(N_JB)]
+        pooled = {}
+        for g, b in blocks:
+            if (g, b) in FUSED:
+                continue
+            a0 = psum.tile([P, PACK, JB], F32, tag="a0", name="a0")
+            a1 = psum.tile([P, PACK, JB], F32, tag="a1", name="a1")
+            neighbour_passes(a0, 0, g, b, True)
+            first = ring.tile([P, JB, PACK], F32, tag="first", name="first")
+            nc.scalar.copy(first[:], by_point(a0))
+            neighbour_passes(a1, 1, g, b, True)
+            pooled[(g, b)] = keep.tile([P, JB, PACK], F32, name=f"pooled{g}{b}")
+            nc.vector.tensor_tensor(pooled[(g, b)][:], by_point(a1), first[:], ALU.max)
+
+        round_wc(0)
+        round_wc(1)
+        round_c(0)
+        round_c(1)
+        round_wc(2)
+        round_wc(3)
+        quantize_wc(0)
+        quantize_c(0)
+
+        h_bf = {gb: keep.tile([P, JB * PACK], BF16, name=f"h_bf{gb[0]}{gb[1]}", align_bytes=64) for gb in blocks}
+        h_w = {gb: keep.tile([P, JB], U32, name=f"h_w{gb[0]}{gb[1]}", align_bytes=64) for gb in blocks}
+        h_s = {gb: keep.tile([P, JB], U8, name=f"h_s{gb[0]}{gb[1]}", align_bytes=64) for gb in blocks}
+        pre = {}
+        sums = {}
+
+        def open_sums(gb):
+            s0 = psum.tile([P, PACK, JB], F32, tag="a0", name="s0")
+            s1 = psum.tile([P, PACK, JB], F32, tag="a1", name="s1")
+            neighbour_passes(s0, 0, gb[0], gb[1], False)
+            neighbour_passes(s1, 1, gb[0], gb[1], False)
+            sums[gb] = (s0, s1)
+
+        def combine(gb):
+            g, b = gb
+            if gb in FUSED:
+                s0, s1 = sums[gb]
+                own_passes(s0, g, b, False)
+                first = ring.tile([P, JB, PACK], F32, tag="first", name="first")
+                nc.scalar.copy(first[:], by_point(s0))
+                own_passes(s1, g, b, False)
+                nc.vector.scalar_tensor_tensor(
+                    h_bf[gb][:].rearrange("p (j t) -> p j t", t=PACK), by_point(s1), 0.0, first[:], ALU.max, ALU.max
+                )
+            else:
+                ac = psum.tile([P, PACK, JB], F32, tag="ac", name="ac")
+                own_passes(ac, g, b, True)
+                pre[gb] = ring.tile([P, JB, PACK], BF16, tag="pre", name="pre")
+                nc.vector.tensor_tensor(pre[gb][:], by_point(ac), pooled[gb][:], ALU.add)
+
+        def relu(gb):
+            if gb not in FUSED:
+                nc.vector.tensor_scalar_max(h_bf[gb][:], pre[gb][:].rearrange("p j t -> p (j t)"), 0.0)
+
+        def quantize_h(gb):
+            nc.vector.quantize_mx(out=h_w[gb][:].bitcast(FP8X4), scales=h_s[gb][:], in_=h_bf[gb][:])
+
+        out_rows = out.rearrange("(x p) j -> p x j", p=P)
+
+        def second_layer(b):
+            y = psum.tile([P, 2, JB], F32, tag="y", name="y")
+            for x in range(2):
+                nc.tensor.matmul_mx(
+                    out=y[:, x, :],
+                    lhsT=wd8_w[:, P * x : P * (x + 1)].bitcast(FP8X4),
+                    lhsT_scale=wd_s[:, P * x : P * (x + 1)],
+                    rhs=h_w[(0, b)][:].bitcast(FP8X4),
+                    rhs_scale=h_s[(0, b)][:],
+                    start=True,
+                    stop=False,
+                )
+                nc.tensor.matmul_mx(
+                    out=y[:, x, :],
+                    lhsT=wd4_w[:, 2 * P * x : 2 * P * (x + 1)].bitcast(FP4X4),
+                    lhsT_scale=wd_s[:, N + P * x : N + P * (x + 1)],
+                    rhs=h_w[(1, b)][:].bitcast(FP8X4),
+                    rhs_scale=h_s[(1, b)][:],
+                    start=False,
+                    stop=True,
+                )
+            res = ring.tile([P, 2, JB], F32, tag="res", name="res")
+            nc.scalar.copy(res[:], y[:])
+            nc.sync.dma_start(out=out_rows[:, :, JB * b : JB * (b + 1)], in_=res[:])
+
+        for s in range(len(blocks) + 2):
+            if s < len(blocks):
+                combine(blocks[s])
+            if s == 0:
+                quantize_c(1)
+            if s == 2:
+                quantize_wc(1)
+            if s == 2 or s == 3:
+                open_sums(FUSED[s - 2])
+            if 1 <= s <= len(blocks):
+                relu(blocks[s - 1])
+            if s >= 2:
+                quantize_h(blocks[s - 2])
+                if blocks[s - 2][0] == 1:
+                    second_layer(blocks[s - 2][1])

@@ -20,6 +20,7 @@ PACK = 4
 HALF = P * PACK
 JB = 128
 N_JB = J // JB
+TAB_HEAD = 1024
 FUSED = ((1, 2), (1, 3))
 
 
@@ -35,72 +36,64 @@ def tile_list_pnet_mix_none_kernel(
     with ExitStack() as ctx:
         keep = ctx.enter_context(tc.tile_pool(name="keep", bufs=1))
         ring = ctx.enter_context(tc.tile_pool(name="ring", bufs=3))
-        shared = ctx.enter_context(tc.tile_pool(name="shared", bufs=1))
         psum = ctx.enter_context(tc.psum_pool(name="psum", bufs=2))
 
         offsets = keep.tile([P, 2 * J // 16], U16, name="offsets")
         tab_w = keep.tile([P, T], U32, name="tab_w", align_bytes=64)
-        ws_raw = shared.tile([P, HALF], U8, name="ws_raw", align_bytes=64, offset=3840)
-        tab_s = shared.tile([P, T], U8, name="tab_s", align_bytes=64, offset=8192)
-        w_raw = shared.tile([P, R], I32, name="w_raw", align_bytes=64, offset=33280)
+        tab_s = keep.tile([P, T], U8, name="tab_s", align_bytes=64)
+        ws_raw = keep.tile([P, HALF], U8, name="ws_raw", tag="ws_raw", align_bytes=64)
+        w_raw = keep.tile([P, R], I32, name="w_raw", align_bytes=64)
+        wd8_w = keep.tile([P, N], U32, name="wd8_w", align_bytes=64)
+        wd4_w = keep.tile([P, 2 * N], U8, name="wd4_w", align_bytes=64)
+        wd_s = keep.tile([P, 2 * N], U8, name="wd_s", align_bytes=64)
+        c_raw = keep.tile([P, PACK, J], F32, name="c_raw")
+        wc_raw = [keep.tile([P, PACK, HALF], F32, name=f"wc_raw{g}") for g in range(2)]
 
         nc.vector.memset(tab_s[:].bitcast(I32), 0)
-        nc.gpsimd.memset(ws_raw[:].bitcast(I32), 0)
+        nc.vector.memset(ws_raw[:].bitcast(I32), 0)
 
+        tab_rows = tab_words[0].rearrange("p t i -> p (t i)").bitcast(I32)
         nc.sync.dma_start(offsets[:], offs)
-        nc.sync.dma_start(out=tab_w[:].bitcast(I32), in_=tab_words[0].rearrange("p t i -> p (t i)").bitcast(I32))
         nc.sync.dma_start(out=w_raw[:], in_=w_words[0].rearrange("p r i -> p (r i)").bitcast(I32))
-        load_scale_rows(nc.scalar, tab_s, tab_scales[0])
+        nc.sync.dma_start(out=tab_w[:, 0:TAB_HEAD].bitcast(I32), in_=tab_rows[:, 0:TAB_HEAD])
+        load_scale_rows(nc.sync, tab_s, tab_scales[0])
+        nc.sync.dma_start(out=tab_w[:, TAB_HEAD:T].bitcast(I32), in_=tab_rows[:, TAB_HEAD:T])
         ws_rows = w_scales[0].bitcast(I32).rearrange("q (g r) -> g q r", g=2)
         for q in range(4):
-            nc.gpsimd.dma_start(out=ws_raw[32 * q : 32 * q + 8, :].bitcast(I32), in_=ws_rows[:, 4 * q : 4 * q + 4, :])
-
-        nb_s = keep.tile([P, 2 * J], U8, name="nb_s", align_bytes=64)
-        nc.vector.tensor_copy(nb_s[:], tab_s[:].indirect(offsets[:]))
-
-        raw = shared.tile([P, 6, PACK, 256], F32, name="raw", align_bytes=64, offset=8704)
-        c_raw = [raw[:, 2 + u] for u in range(2)]
-        wc_raw = [raw[:, slot] for slot in (0, 1, 4, 5)]
-        c_rows = c.rearrange("(p i) j -> p i j", i=PACK)
+            nc.sync.dma_start(out=ws_raw[32 * q : 32 * q + 8, :].bitcast(I32), in_=ws_rows[:, 4 * q : 4 * q + 4, :])
         wc_rows = wc.rearrange("(p i) r -> p i r", i=PACK)
-        for u in range(2):
-            nc.sync.dma_start(out=wc_raw[u], in_=wc_rows[:, :, 256 * u : 256 * (u + 1)])
-        for u in range(2):
-            nc.sync.dma_start(out=c_raw[u], in_=c_rows[:, :, 256 * u : 256 * (u + 1)])
-        for u in range(2, 4):
-            nc.sync.dma_start(out=wc_raw[u], in_=wc_rows[:, :, 256 * u : 256 * (u + 1)])
-
-        w_s = shared.tile([P, HALF], U8, name="w_s", align_bytes=64, offset=8192)
-        nc.vector.tensor_copy(
-            w_s[:].rearrange("p (t m e) -> p m t e", t=PACK, e=16),
-            ws_raw[:].rearrange("p (m e t) -> p m t e", t=PACK, e=16),
-        )
-        nb_all = shared.tile([P, 2 * J], U32, name="nb_all", align_bytes=64, offset=0)
-        w_all = shared.tile([P, R], I32, name="w_all", align_bytes=64, offset=4096)
-        nb_w = [nb_all[:, J * a : J * (a + 1)] for a in range(2)]
-        w_w = [w_all[:, HALF * g : HALF * (g + 1)] for g in range(2)]
-
-        def gather_words(a):
-            nc.vector.tensor_copy(nb_w[a], tab_w[:].indirect(offsets[:, 32 * a : 32 * (a + 1)]))
-
-        def order_w(g):
-            nc.vector.tensor_copy(
-                w_w[g].rearrange("p (t m e) -> p m t e", t=PACK, e=4),
-                w_raw[:, HALF * g : HALF * (g + 1)].rearrange("p (m e t) -> p m t e", t=PACK, e=4),
-            )
-
-        gather_words(0)
-        order_w(0)
-        gather_words(1)
-        order_w(1)
-
-        wd8_w = shared.tile([P, N], U32, name="wd8_w", align_bytes=64, offset=33280)
-        wd4_w = shared.tile([P, 2 * N], U8, name="wd4_w", align_bytes=64, offset=34304)
-        wd_s = shared.tile([P, 2 * N], U8, name="wd_s", align_bytes=64, offset=34816)
+        nc.sync.dma_start(out=wc_raw[0][:], in_=wc_rows[:, :, 0:HALF])
+        nc.sync.dma_start(out=c_raw[:], in_=c.rearrange("(p i) j -> p i j", i=PACK))
+        nc.sync.dma_start(out=wc_raw[1][:], in_=wc_rows[:, :, HALF:R])
         nc.sync.dma_start(out=wd8_w[:].bitcast(I32), in_=wd8_words[0].rearrange("p n i -> p (n i)").bitcast(I32))
         nc.sync.dma_start(out=wd4_w[:].bitcast(I32), in_=wd4_words[0].bitcast(I32))
         load_scale_rows(nc.sync, wd_s[:, 0:N], wd8_scales[0])
         load_scale_rows(nc.sync, wd_s[:, N : 2 * N], wd4_scales[0])
+
+        nb_s = keep.tile([P, 2 * J], U8, name="nb_s", align_bytes=64)
+        nc.vector.tensor_copy(nb_s[:], tab_s[:].indirect(offsets[:]))
+        w_s = keep.tile([P, HALF], U8, name="w_s", align_bytes=64)
+        nb_w = {}
+        w_w = [keep.tile([P, HALF], I32, name=f"w_w{g}", align_bytes=64) for g in range(2)]
+
+        def gather_words(a, tag):
+            nb_w[a] = keep.tile([P, J], U32, name=f"nb_w{a}", tag=tag, align_bytes=64)
+            nc.vector.tensor_copy(nb_w[a][:], tab_w[:].indirect(offsets[:, 32 * a : 32 * (a + 1)]))
+
+        def order_w(g):
+            nc.vector.tensor_copy(
+                w_w[g][:].rearrange("p (t m e) -> p m t e", t=PACK, e=4),
+                w_raw[:, HALF * g : HALF * (g + 1)].rearrange("p (m e t) -> p m t e", t=PACK, e=4),
+            )
+
+        order_w(0)
+        order_w(1)
+        gather_words(0, "nb_w0")
+        nc.vector.tensor_copy(
+            w_s[:].rearrange("p (t m e) -> p m t e", t=PACK, e=16),
+            ws_raw[:].rearrange("p (m e t) -> p m t e", t=PACK, e=16),
+        )
+        gather_words(1, "ws_raw")
 
         def neighbour_passes(bank, a, g, b, closed):
             for t in range(PACK):
@@ -122,16 +115,14 @@ def tile_list_pnet_mix_none_kernel(
         wc_s = [keep.tile([P, HALF], U8, name=f"wc_s{g}", align_bytes=64) for g in range(2)]
 
         def round_c(u):
-            nc.scalar.copy(
-                c_bf[u][:].rearrange("p (q e) i -> p q i e", e=4),
-                c_raw[u].rearrange("p i (q e) -> p q i e", e=4),
-            )
+            src = c_raw[:, :, 256 * u : 256 * (u + 1)].rearrange("p i j -> p j i")
+            nc.gpsimd.tensor_scalar(c_bf[u][:], src, 1.0, 0.0, ALU.mult, ALU.add)
 
         def round_wc(u):
             g, v = divmod(u, 2)
             nc.scalar.copy(
-                wc_bf[g][:, :, 64 * v : 64 * (v + 1), :].rearrange("p t m i -> p m i t"),
-                wc_raw[u].rearrange("p i (m t) -> p m i t", t=PACK),
+                wc_bf[g][:, :, 64 * v : 64 * (v + 1), :].rearrange("p t m i -> p m t i"),
+                wc_raw[g][:, :, 256 * v : 256 * (v + 1)].rearrange("p i (m t) -> p m t i", t=PACK),
             )
 
         def quantize_c(u):
@@ -157,27 +148,40 @@ def tile_list_pnet_mix_none_kernel(
             return bank[:].rearrange("p t j -> p j t")
 
         blocks = [(g, b) for g in range(2) for b in range(N_JB)]
+        plain = [gb for gb in blocks if gb not in FUSED]
+        firsts = {}
         pooled = {}
-        for g, b in blocks:
-            if (g, b) in FUSED:
-                continue
+
+        def first_neighbour(gb):
             a0 = psum.tile([P, PACK, JB], F32, tag="a0", name="a0")
+            neighbour_passes(a0, 0, gb[0], gb[1], True)
+            firsts[gb] = keep.tile([P, JB, PACK], F32, name=f"first{gb[0]}{gb[1]}")
+            nc.scalar.copy(firsts[gb][:], by_point(a0))
+
+        def second_neighbour(gb):
             a1 = psum.tile([P, PACK, JB], F32, tag="a1", name="a1")
-            neighbour_passes(a0, 0, g, b, True)
-            first = ring.tile([P, JB, PACK], F32, tag="first", name="first")
-            nc.scalar.copy(first[:], by_point(a0))
-            neighbour_passes(a1, 1, g, b, True)
-            pooled[(g, b)] = keep.tile([P, JB, PACK], F32, name=f"pooled{g}{b}")
-            nc.vector.tensor_tensor(pooled[(g, b)][:], by_point(a1), first[:], ALU.max)
+            neighbour_passes(a1, 1, gb[0], gb[1], True)
+            pooled[gb] = keep.tile([P, JB, PACK], F32, name=f"pooled{gb[0]}{gb[1]}")
+            nc.vector.tensor_tensor(pooled[gb][:], by_point(a1), firsts[gb][:], ALU.max)
+
+        for s in range(N_JB + 2):
+            if s < N_JB:
+                first_neighbour(plain[s])
+            if s >= 2:
+                second_neighbour(plain[s - 2])
 
         round_wc(0)
         round_wc(1)
         round_c(0)
         round_c(1)
+        quantize_c(0)
+        quantize_wc(0)
+        for gb in plain[N_JB:]:
+            first_neighbour(gb)
         round_wc(2)
         round_wc(3)
-        quantize_wc(0)
-        quantize_c(0)
+        for gb in plain[N_JB:]:
+            second_neighbour(gb)
 
         h_bf = {gb: keep.tile([P, JB * PACK], BF16, name=f"h_bf{gb[0]}{gb[1]}", align_bytes=64) for gb in blocks}
         h_w = {gb: keep.tile([P, JB], U32, name=f"h_w{gb[0]}{gb[1]}", align_bytes=64) for gb in blocks}
@@ -210,8 +214,11 @@ def tile_list_pnet_mix_none_kernel(
                 nc.vector.tensor_tensor(pre[gb][:], by_point(ac), pooled[gb][:], ALU.add)
 
         def relu(gb):
-            if gb not in FUSED:
-                nc.vector.tensor_scalar_max(h_bf[gb][:], pre[gb][:].rearrange("p j t -> p (j t)"), 0.0)
+            src = pre[gb][:].rearrange("p j t -> p (j t)")
+            if gb in ((0, 0), (0, 1)):
+                nc.vector.tensor_scalar_max(h_bf[gb][:], src, 0.0)
+            else:
+                nc.scalar.activation(h_bf[gb][:], src, mybir.ActivationFunctionType.Relu)
 
         def quantize_h(gb):
             nc.vector.quantize_mx(out=h_w[gb][:].bitcast(FP8X4), scales=h_s[gb][:], in_=h_bf[gb][:])
@@ -239,22 +246,31 @@ def tile_list_pnet_mix_none_kernel(
                     start=False,
                     stop=True,
                 )
-            res = ring.tile([P, 2, JB], F32, tag="res", name="res")
+            res = keep.tile([P, 2, JB], F32, name=f"res{b}")
             nc.scalar.copy(res[:], y[:])
             nc.sync.dma_start(out=out_rows[:, :, JB * b : JB * (b + 1)], in_=res[:])
 
-        for s in range(len(blocks) + 2):
-            if s < len(blocks):
-                combine(blocks[s])
+        def finish(gb):
+            quantize_h(gb)
+            if gb[0] == 1:
+                second_layer(gb[1])
+
+        for s in range(len(plain)):
+            combine(plain[s])
             if s == 0:
                 quantize_c(1)
             if s == 2:
                 quantize_wc(1)
             if s == 2 or s == 3:
                 open_sums(FUSED[s - 2])
-            if 1 <= s <= len(blocks):
-                relu(blocks[s - 1])
+            if s >= 1:
+                relu(plain[s - 1])
             if s >= 2:
-                quantize_h(blocks[s - 2])
-                if blocks[s - 2][0] == 1:
-                    second_layer(blocks[s - 2][1])
+                finish(plain[s - 2])
+        combine(FUSED[0])
+        relu(plain[-1])
+        finish(plain[-2])
+        finish(FUSED[0])
+        finish(plain[-1])
+        combine(FUSED[1])
+        finish(FUSED[1])

@@ -14,19 +14,20 @@ U8 = mybir.dt.uint8
 FP8X4 = mybir.dt.float8_e4m3fn_x4
 FP4X4 = mybir.dt.float4_e2m1fn_x4
 ALU = mybir.AluOpType
+RELU = mybir.ActivationFunctionType.Relu
 
 P = 128
 PACK = 4
 HALF = P * PACK
 JB = 128
 N_JB = J // JB
-TAB_HEAD = 1024
-FUSED = ((1, 2), (1, 3))
+TAB_CUTS = (0, 1536, T)
+FUSED = ((0, 3), (1, 3))
 
 
 def load_scale_rows(queue, plane, rows):
-    for q in range(4):
-        queue.dma_start(out=plane[32 * q : 32 * q + 4, :].bitcast(I32), in_=rows[4 * q : 4 * q + 4, :].bitcast(I32))
+    for r in range(4):
+        queue.dma_start(out=plane[r:P:32, :].bitcast(I32), in_=rows[r:16:4, :].bitcast(I32))
 
 
 def tile_list_pnet_mix_none_kernel(
@@ -35,71 +36,79 @@ def tile_list_pnet_mix_none_kernel(
     nc = tc.nc
     with ExitStack() as ctx:
         keep = ctx.enter_context(tc.tile_pool(name="keep", bufs=1))
-        ring = ctx.enter_context(tc.tile_pool(name="ring", bufs=3))
+        head = ctx.enter_context(tc.tile_pool(name="head", bufs=1))
         psum = ctx.enter_context(tc.psum_pool(name="psum", bufs=2))
 
         offsets = keep.tile([P, 2 * J // 16], U16, name="offsets")
         tab_w = keep.tile([P, T], U32, name="tab_w", align_bytes=64)
         tab_s = keep.tile([P, T], U8, name="tab_s", align_bytes=64)
-        ws_raw = keep.tile([P, HALF], U8, name="ws_raw", tag="ws_raw", align_bytes=64)
-        w_raw = keep.tile([P, R], I32, name="w_raw", align_bytes=64)
-        wd8_w = keep.tile([P, N], U32, name="wd8_w", align_bytes=64)
-        wd4_w = keep.tile([P, 2 * N], U8, name="wd4_w", align_bytes=64)
-        wd_s = keep.tile([P, 2 * N], U8, name="wd_s", align_bytes=64)
-        c_raw = keep.tile([P, PACK, J], F32, name="c_raw")
-        wc_raw = [keep.tile([P, PACK, HALF], F32, name=f"wc_raw{g}") for g in range(2)]
+        w_raw = head.tile([P, R], I32, name="w_raw", align_bytes=64, offset=0)
+        ws_raw = head.tile([P, HALF], U8, name="ws_raw", align_bytes=64, offset=8 * HALF)
 
         nc.vector.memset(tab_s[:].bitcast(I32), 0)
         nc.vector.memset(ws_raw[:].bitcast(I32), 0)
 
         tab_rows = tab_words[0].rearrange("p t i -> p (t i)").bitcast(I32)
+        w_rows = w_words[0].rearrange("p r i -> p (r i)").bitcast(I32)
+        wc_rows = wc.rearrange("(p i) r -> p i r", i=PACK)
+        c_rows = c.rearrange("(p i) j -> p i j", i=PACK)
         nc.sync.dma_start(offsets[:], offs)
-        nc.sync.dma_start(out=w_raw[:], in_=w_words[0].rearrange("p r i -> p (r i)").bitcast(I32))
-        nc.sync.dma_start(out=tab_w[:, 0:TAB_HEAD].bitcast(I32), in_=tab_rows[:, 0:TAB_HEAD])
+
+        def load_table(n):
+            cols = slice(TAB_CUTS[n], TAB_CUTS[n + 1])
+            nc.sync.dma_start(out=tab_w[:, cols].bitcast(I32), in_=tab_rows[:, cols])
+
+        load_table(0)
         load_scale_rows(nc.sync, tab_s, tab_scales[0])
-        nc.sync.dma_start(out=tab_w[:, TAB_HEAD:T].bitcast(I32), in_=tab_rows[:, TAB_HEAD:T])
+        load_table(1)
         ws_rows = w_scales[0].bitcast(I32).rearrange("q (g r) -> g q r", g=2)
         for q in range(4):
             nc.sync.dma_start(out=ws_raw[32 * q : 32 * q + 8, :].bitcast(I32), in_=ws_rows[:, 4 * q : 4 * q + 4, :])
-        wc_rows = wc.rearrange("(p i) r -> p i r", i=PACK)
-        nc.sync.dma_start(out=wc_raw[0][:], in_=wc_rows[:, :, 0:HALF])
-        nc.sync.dma_start(out=c_raw[:], in_=c.rearrange("(p i) j -> p i j", i=PACK))
-        nc.sync.dma_start(out=wc_raw[1][:], in_=wc_rows[:, :, HALF:R])
+        nc.sync.dma_start(out=w_raw[:], in_=w_rows)
+
+        nb_s = keep.tile([P, 2 * J], U8, name="nb_s", align_bytes=64)
+        nc.vector.tensor_copy(nb_s[:], tab_s[:].indirect(offsets[:]))
+
+        wd8_w = keep.tile([P, N], U32, name="wd8_w", align_bytes=64)
+        wd4_w = keep.tile([P, 2 * N], U8, name="wd4_w", align_bytes=64)
+        wd_s = keep.tile([P, 2 * N], U8, name="wd_s", align_bytes=64)
+        c_raw = [keep.tile([P, PACK, 256], F32, name=f"c_raw{u}")[:] for u in range(2)]
+        wc_raw = [[keep.tile([P, PACK, 256], F32, name=f"wc_raw{g}{v}", tag=f"wc_raw{g}{v}", align_bytes=64)[:] for v in range(2)] for g in range(2)]
+        nc.sync.dma_start(out=c_raw[0], in_=c_rows[:, :, 0 : J // 2])
+        for g in range(2):
+            for v in range(2):
+                nc.sync.dma_start(out=wc_raw[g][v], in_=wc_rows[:, :, HALF * g + 256 * v : HALF * g + 256 * (v + 1)])
+        nc.sync.dma_start(out=c_raw[1], in_=c_rows[:, :, J // 2 : J])
         nc.sync.dma_start(out=wd8_w[:].bitcast(I32), in_=wd8_words[0].rearrange("p n i -> p (n i)").bitcast(I32))
         nc.sync.dma_start(out=wd4_w[:].bitcast(I32), in_=wd4_words[0].bitcast(I32))
         load_scale_rows(nc.sync, wd_s[:, 0:N], wd8_scales[0])
         load_scale_rows(nc.sync, wd_s[:, N : 2 * N], wd4_scales[0])
 
-        nb_s = keep.tile([P, 2 * J], U8, name="nb_s", align_bytes=64)
-        nc.vector.tensor_copy(nb_s[:], tab_s[:].indirect(offsets[:]))
         w_s = keep.tile([P, HALF], U8, name="w_s", align_bytes=64)
-        nb_w = {}
-        w_w = [keep.tile([P, HALF], I32, name=f"w_w{g}", align_bytes=64) for g in range(2)]
+        w_w = keep.tile([P, R], I32, name="w_w", align_bytes=64)
 
-        def gather_words(a, tag):
-            nb_w[a] = keep.tile([P, J], U32, name=f"nb_w{a}", tag=tag, align_bytes=64)
-            nc.vector.tensor_copy(nb_w[a][:], tab_w[:].indirect(offsets[:, 32 * a : 32 * (a + 1)]))
+        def gather_words(dst, a):
+            nc.vector.tensor_copy(dst[:], tab_w[:].indirect(offsets[:, 32 * a : 32 * (a + 1)]))
 
-        def order_w(g):
-            nc.vector.tensor_copy(
-                w_w[g][:].rearrange("p (t m e) -> p m t e", t=PACK, e=4),
-                w_raw[:, HALF * g : HALF * (g + 1)].rearrange("p (m e t) -> p m t e", t=PACK, e=4),
-            )
-
-        order_w(0)
-        order_w(1)
-        gather_words(0, "nb_w0")
+        nb_w0 = keep.tile([P, J], U32, name="nb_w0", align_bytes=64)
+        gather_words(nb_w0, 0)
         nc.vector.tensor_copy(
             w_s[:].rearrange("p (t m e) -> p m t e", t=PACK, e=16),
             ws_raw[:].rearrange("p (m e t) -> p m t e", t=PACK, e=16),
         )
-        gather_words(1, "ws_raw")
+        nc.vector.tensor_copy(
+            w_w[:].rearrange("p (g t m e) -> p g m t e", g=2, t=PACK, e=4),
+            w_raw[:].rearrange("p (g m e t) -> p g m t e", g=2, t=PACK, e=4),
+        )
+        nb_w1 = head.tile([P, J], U32, name="nb_w1", align_bytes=64, offset=5 * HALF)
+        gather_words(nb_w1, 1)
+        nb_w = [nb_w0, nb_w1]
 
         def neighbour_passes(bank, a, g, b, closed):
             for t in range(PACK):
                 nc.tensor.matmul_mx(
                     out=bank[:, t, :],
-                    lhsT=w_w[g][:, P * t : P * (t + 1)].bitcast(FP8X4),
+                    lhsT=w_w[:, HALF * g + P * t : HALF * g + P * (t + 1)].bitcast(FP8X4),
                     lhsT_scale=w_s[4 * g : P, P * t : P * (t + 1)],
                     rhs=nb_w[a][:, JB * b : JB * (b + 1)].bitcast(FP8X4),
                     rhs_scale=nb_s[:, J * a + JB * b : J * a + JB * (b + 1)],
@@ -107,23 +116,65 @@ def tile_list_pnet_mix_none_kernel(
                     stop=closed,
                 )
 
-        c_bf = [keep.tile([P, J // 2, PACK], BF16, name=f"c_bf{u}", align_bytes=64) for u in range(2)]
-        c_w = [keep.tile([P, J // 2], U32, name=f"c_w{u}", align_bytes=64) for u in range(2)]
+        def by_point(bank):
+            return bank[:].rearrange("p t j -> p j t")
+
+        order = [(0, 0), (0, 1), (1, 0), (1, 1), (0, 2), (1, 2), (0, 3), (1, 3)]
+        plain = [gb for gb in order if gb not in FUSED]
+        firsts = {}
+        pooled = {}
+
+        def first_neighbour(gb):
+            a0 = psum.tile([P, PACK, JB], F32, tag=("a0", "ac")[plain.index(gb) % 2], name="a0")
+            neighbour_passes(a0, 0, gb[0], gb[1], True)
+            firsts[gb] = keep.tile([P, JB, PACK], F32, name=f"first{gb[0]}{gb[1]}", tag=f"first{gb[0]}{gb[1]}", align_bytes=64)
+            nc.scalar.copy(firsts[gb][:], by_point(a0))
+
+        def second_neighbour(gb):
+            a1 = psum.tile([P, PACK, JB], F32, tag=("a1", "y")[plain.index(gb) % 2], name="a1")
+            neighbour_passes(a1, 1, gb[0], gb[1], True)
+            pooled[gb] = keep.tile([P, JB, PACK], F32, name=f"pooled{gb[0]}{gb[1]}")
+            nc.vector.tensor_tensor(pooled[gb][:], by_point(a1), firsts[gb][:], ALU.max)
+
+        for s in range(len(plain) + 1):
+            if s < len(plain):
+                first_neighbour(plain[s])
+            if s >= 1:
+                second_neighbour(plain[s - 1])
+
+        sums = {}
+        for gb in FUSED:
+            s0 = psum.tile([P, PACK, JB], F32, tag="a0", name="s0")
+            s1 = psum.tile([P, PACK, JB], F32, tag="a1", name="s1")
+            neighbour_passes(s0, 0, gb[0], gb[1], False)
+            neighbour_passes(s1, 1, gb[0], gb[1], False)
+            sums[gb] = (s0, s1)
+
+        c_bf = [head.tile([P, J // 2, PACK], BF16, name="c_bf0", align_bytes=64, offset=0)]
+        last = plain[-2]
+        c_w = [
+            keep.tile([P, J // 2], U32, name="c_w0", tag=f"first{last[0]}{last[1]}", align_bytes=64),
+            keep.tile([P, J // 2], U32, name="c_w1", align_bytes=64),
+        ]
         c_s = [keep.tile([P, J // 2], U8, name=f"c_s{u}", align_bytes=64) for u in range(2)]
-        wc_bf = [keep.tile([P, PACK, P, PACK], BF16, name=f"wc_bf{g}", align_bytes=64) for g in range(2)]
+        wc_bf = [keep.tile([P, PACK, P, PACK], BF16, name="wc_bf0", tag="staged", align_bytes=64)]
         wc_w = [keep.tile([P, HALF], U32, name=f"wc_w{g}", align_bytes=64) for g in range(2)]
         wc_s = [keep.tile([P, HALF], U8, name=f"wc_s{g}", align_bytes=64) for g in range(2)]
 
-        def round_c(u):
-            src = c_raw[:, :, 256 * u : 256 * (u + 1)].rearrange("p i j -> p j i")
-            nc.gpsimd.tensor_scalar(c_bf[u][:], src, 1.0, 0.0, ALU.mult, ALU.add)
+        def round_c(u, engine):
+            src = c_raw[u].rearrange("p i j -> p j i")
+            if engine == "gpsimd":
+                nc.gpsimd.tensor_scalar(c_bf[u][:], src, 1.0, 0.0, ALU.mult, ALU.add)
+            else:
+                nc.scalar.copy(c_bf[u][:], src)
 
-        def round_wc(u):
-            g, v = divmod(u, 2)
-            nc.scalar.copy(
-                wc_bf[g][:, :, 64 * v : 64 * (v + 1), :].rearrange("p t m i -> p m t i"),
-                wc_raw[g][:, :, 256 * v : 256 * (v + 1)].rearrange("p i (m t) -> p m t i", t=PACK),
-            )
+        def round_wc(g, v, engine):
+            dst = wc_bf[g][:, :, 64 * v : 64 * (v + 1), :].rearrange("p t m i -> p m t i")
+            src = wc_raw[g][v].rearrange("p i (m t) -> p m t i", t=PACK)
+            if engine == "gpsimd":
+                nc.gpsimd.tensor_scalar(dst, src, 1.0, 0.0, ALU.mult, ALU.add)
+            else:
+                nc.scalar.copy(dst, src)
 
         def quantize_c(u):
             nc.vector.quantize_mx(out=c_w[u][:].bitcast(FP8X4), scales=c_s[u][:], in_=c_bf[u][:].rearrange("p j i -> p (j i)"))
@@ -144,133 +195,120 @@ def tile_list_pnet_mix_none_kernel(
                     stop=closed or t == PACK - 1,
                 )
 
-        def by_point(bank):
-            return bank[:].rearrange("p t j -> p j t")
+        pairs = [order[0:2], order[2:4], order[4:6], order[6:7], order[7:8]]
+        place = {gb: (n, pair.index(gb)) for n, pair in enumerate(pairs) for gb in pair}
+        pre = [keep.tile([P, len(pair), HALF], BF16, name=f"pre{n}") for n, pair in enumerate(pairs[:3])]
+        h_bf = {n: keep.tile([P, len(pair), HALF], BF16, name=f"h_bf{n}", align_bytes=64) for n, pair in enumerate(pairs)}
+        h_w = [keep.tile([P, len(pair) * JB], U32, name=f"h_w{n}", align_bytes=64) for n, pair in enumerate(pairs)]
+        h_s = [keep.tile([P, len(pair) * JB], U8, name=f"h_s{n}", align_bytes=64) for n, pair in enumerate(pairs)]
 
-        blocks = [(g, b) for g in range(2) for b in range(N_JB)]
-        plain = [gb for gb in blocks if gb not in FUSED]
-        firsts = {}
-        pooled = {}
+        def add_own(gb):
+            n, e = place[gb]
+            ac = psum.tile([P, PACK, JB], F32, tag="ac", name="ac")
+            own_passes(ac, gb[0], gb[1], True)
+            nc.vector.tensor_tensor(pre[n][:, e, :].rearrange("p (j t) -> p j t", t=PACK), by_point(ac), pooled[gb][:], ALU.add)
 
-        def first_neighbour(gb):
-            a0 = psum.tile([P, PACK, JB], F32, tag="a0", name="a0")
-            neighbour_passes(a0, 0, gb[0], gb[1], True)
+        def close_first(gb):
+            s0 = sums[gb][0]
+            own_passes(s0, gb[0], gb[1], False)
             firsts[gb] = keep.tile([P, JB, PACK], F32, name=f"first{gb[0]}{gb[1]}")
-            nc.scalar.copy(firsts[gb][:], by_point(a0))
+            nc.scalar.copy(firsts[gb][:], by_point(s0))
 
-        def second_neighbour(gb):
-            a1 = psum.tile([P, PACK, JB], F32, tag="a1", name="a1")
-            neighbour_passes(a1, 1, gb[0], gb[1], True)
-            pooled[gb] = keep.tile([P, JB, PACK], F32, name=f"pooled{gb[0]}{gb[1]}")
-            nc.vector.tensor_tensor(pooled[gb][:], by_point(a1), firsts[gb][:], ALU.max)
+        def close_second(gb):
+            n, e = place[gb]
+            s1 = sums[gb][1]
+            own_passes(s1, gb[0], gb[1], False)
+            nc.vector.scalar_tensor_tensor(
+                h_bf[n][:, e, :].rearrange("p (j t) -> p j t", t=PACK), by_point(s1), 0.0, firsts[gb][:], ALU.max, ALU.max
+            )
 
-        for s in range(N_JB + 2):
-            if s < N_JB:
-                first_neighbour(plain[s])
-            if s >= 2:
-                second_neighbour(plain[s - 2])
+        def relu_pair_on_vector(n):
+            nc.vector.tensor_scalar_max(h_bf[n][:].rearrange("p e x -> p (e x)"), pre[n][:].rearrange("p e x -> p (e x)"), 0.0)
 
-        round_wc(0)
-        round_wc(1)
-        round_c(0)
-        round_c(1)
-        quantize_c(0)
-        quantize_wc(0)
-        for gb in plain[N_JB:]:
-            first_neighbour(gb)
-        round_wc(2)
-        round_wc(3)
-        for gb in plain[N_JB:]:
-            second_neighbour(gb)
+        def relu_on_scalar(gb):
+            n, e = place[gb]
+            nc.scalar.activation(h_bf[n][:, e, :], pre[n][:, e, :], RELU)
 
-        h_bf = {gb: keep.tile([P, JB * PACK], BF16, name=f"h_bf{gb[0]}{gb[1]}", align_bytes=64) for gb in blocks}
-        h_w = {gb: keep.tile([P, JB], U32, name=f"h_w{gb[0]}{gb[1]}", align_bytes=64) for gb in blocks}
-        h_s = {gb: keep.tile([P, JB], U8, name=f"h_s{gb[0]}{gb[1]}", align_bytes=64) for gb in blocks}
-        pre = {}
-        sums = {}
-
-        def open_sums(gb):
-            s0 = psum.tile([P, PACK, JB], F32, tag="a0", name="s0")
-            s1 = psum.tile([P, PACK, JB], F32, tag="a1", name="s1")
-            neighbour_passes(s0, 0, gb[0], gb[1], False)
-            neighbour_passes(s1, 1, gb[0], gb[1], False)
-            sums[gb] = (s0, s1)
-
-        def combine(gb):
-            g, b = gb
-            if gb in FUSED:
-                s0, s1 = sums[gb]
-                own_passes(s0, g, b, False)
-                first = ring.tile([P, JB, PACK], F32, tag="first", name="first")
-                nc.scalar.copy(first[:], by_point(s0))
-                own_passes(s1, g, b, False)
-                nc.vector.scalar_tensor_tensor(
-                    h_bf[gb][:].rearrange("p (j t) -> p j t", t=PACK), by_point(s1), 0.0, first[:], ALU.max, ALU.max
-                )
-            else:
-                ac = psum.tile([P, PACK, JB], F32, tag="ac", name="ac")
-                own_passes(ac, g, b, True)
-                pre[gb] = ring.tile([P, JB, PACK], BF16, tag="pre", name="pre")
-                nc.vector.tensor_tensor(pre[gb][:], by_point(ac), pooled[gb][:], ALU.add)
-
-        def relu(gb):
-            src = pre[gb][:].rearrange("p j t -> p (j t)")
-            if gb in ((0, 0), (0, 1)):
-                nc.vector.tensor_scalar_max(h_bf[gb][:], src, 0.0)
-            else:
-                nc.scalar.activation(h_bf[gb][:], src, mybir.ActivationFunctionType.Relu)
-
-        def quantize_h(gb):
-            nc.vector.quantize_mx(out=h_w[gb][:].bitcast(FP8X4), scales=h_s[gb][:], in_=h_bf[gb][:])
+        def quantize_h(n):
+            nc.vector.quantize_mx(out=h_w[n][:].bitcast(FP8X4), scales=h_s[n][:], in_=h_bf[n][:].rearrange("p e x -> p (e x)"))
 
         out_rows = out.rearrange("(x p) j -> p x j", p=P)
 
+        def second_passes(y, x, g, b, start, stop):
+            n, e = place[(g, b)]
+            if g == 0:
+                lhsT = wd8_w[:, P * x : P * (x + 1)].bitcast(FP8X4)
+            else:
+                lhsT = wd4_w[:, 2 * P * x : 2 * P * (x + 1)].bitcast(FP4X4)
+            nc.tensor.matmul_mx(
+                out=y,
+                lhsT=lhsT,
+                lhsT_scale=wd_s[:, N * g + P * x : N * g + P * (x + 1)],
+                rhs=h_w[n][:, JB * e : JB * (e + 1)].bitcast(FP8X4),
+                rhs_scale=h_s[n][:, JB * e : JB * (e + 1)],
+                start=start,
+                stop=stop,
+            )
+
         def second_layer(b):
             y = psum.tile([P, 2, JB], F32, tag="y", name="y")
-            for x in range(2):
-                nc.tensor.matmul_mx(
-                    out=y[:, x, :],
-                    lhsT=wd8_w[:, P * x : P * (x + 1)].bitcast(FP8X4),
-                    lhsT_scale=wd_s[:, P * x : P * (x + 1)],
-                    rhs=h_w[(0, b)][:].bitcast(FP8X4),
-                    rhs_scale=h_s[(0, b)][:],
-                    start=True,
-                    stop=False,
-                )
-                nc.tensor.matmul_mx(
-                    out=y[:, x, :],
-                    lhsT=wd4_w[:, 2 * P * x : 2 * P * (x + 1)].bitcast(FP4X4),
-                    lhsT_scale=wd_s[:, N + P * x : N + P * (x + 1)],
-                    rhs=h_w[(1, b)][:].bitcast(FP8X4),
-                    rhs_scale=h_s[(1, b)][:],
-                    start=False,
-                    stop=True,
-                )
+            for g in range(2):
+                for x in range(2):
+                    second_passes(y[:, x, :], x, g, b, g == 0 and x == 0, g == 1 and x == 1)
             res = keep.tile([P, 2, JB], F32, name=f"res{b}")
             nc.scalar.copy(res[:], y[:])
             nc.sync.dma_start(out=out_rows[:, :, JB * b : JB * (b + 1)], in_=res[:])
 
-        def finish(gb):
-            quantize_h(gb)
-            if gb[0] == 1:
-                second_layer(gb[1])
+        last_y = []
 
-        for s in range(len(plain)):
-            combine(plain[s])
-            if s == 0:
-                quantize_c(1)
-            if s == 2:
-                quantize_wc(1)
-            if s == 2 or s == 3:
-                open_sums(FUSED[s - 2])
-            if s >= 1:
-                relu(plain[s - 1])
-            if s >= 2:
-                finish(plain[s - 2])
-        combine(FUSED[0])
-        relu(plain[-1])
-        finish(plain[-2])
-        finish(FUSED[0])
-        finish(plain[-1])
-        combine(FUSED[1])
-        finish(FUSED[1])
+        def open_last(b):
+            for x in range(2):
+                last_y.append(psum.tile([P, JB], F32, tag="ac", name="last_y"))
+                second_passes(last_y[x][:], x, 0, b, True, False)
+
+        def close_last(b):
+            for x in range(2):
+                second_passes(last_y[x][:], x, 1, b, False, True)
+            res = [keep.tile([P, JB], F32, name=f"last_res{x}") for x in range(2)]
+            nc.scalar.copy(res[0][:], last_y[0][:])
+            nc.sync.dma_start(out=out_rows[:, 0, JB * b : JB * (b + 1)], in_=res[0][:])
+            nc.vector.tensor_copy(res[1][:], last_y[1][:])
+            nc.scalar.dma_start(out=out_rows[:, 1, JB * b : JB * (b + 1)], in_=res[1][:])
+
+        round_c(0, "gpsimd")
+        round_wc(0, 0, "gpsimd")
+        round_wc(0, 1, "gpsimd")
+        quantize_c(0)
+        quantize_wc(0)
+        wc_bf.append(keep.tile([P, PACK, P, PACK], BF16, name="wc_bf1", tag="staged", align_bytes=64))
+        round_wc(1, 0, "scalar")
+        round_wc(1, 1, "gpsimd")
+        add_own(order[0])
+        add_own(order[1])
+        quantize_wc(1)
+        relu_pair_on_vector(0)
+        c_bf.append(keep.tile([P, J // 2, PACK], BF16, name="c_bf1", tag="wc_raw10", align_bytes=64))
+        round_c(1, "scalar")
+        quantize_c(1)
+        add_own(order[2])
+        close_first(order[6])
+        add_own(order[3])
+        close_first(order[7])
+        add_own(order[4])
+        relu_on_scalar(order[2])
+        relu_on_scalar(order[3])
+        quantize_h(0)
+        add_own(order[5])
+        relu_on_scalar(order[4])
+        relu_on_scalar(order[5])
+        close_second(order[6])
+        quantize_h(1)
+        second_layer(0)
+        second_layer(1)
+        close_second(order[7])
+        quantize_h(2)
+        second_layer(2)
+        quantize_h(3)
+        open_last(3)
+        quantize_h(4)
+        close_last(3)

@@ -21,7 +21,7 @@ PACK = 4
 HALF = P * PACK
 JB = 128
 N_JB = J // JB
-TAB_CUTS = (0, 1536, T)
+TAB_CUTS = (0, 512, 1280, 3072, T)
 FUSED = ((0, 3), (1, 3))
 
 
@@ -36,14 +36,14 @@ def tile_list_pnet_mix_none_kernel(
     nc = tc.nc
     with ExitStack() as ctx:
         keep = ctx.enter_context(tc.tile_pool(name="keep", bufs=1))
-        head = ctx.enter_context(tc.tile_pool(name="head", bufs=1))
+        stage = ctx.enter_context(tc.tile_pool(name="stage", bufs=1))
         psum = ctx.enter_context(tc.psum_pool(name="psum", bufs=2))
 
         offsets = keep.tile([P, 2 * J // 16], U16, name="offsets")
         tab_w = keep.tile([P, T], U32, name="tab_w", align_bytes=64)
-        tab_s = keep.tile([P, T], U8, name="tab_s", align_bytes=64)
-        w_raw = head.tile([P, R], I32, name="w_raw", align_bytes=64, offset=0)
-        ws_raw = head.tile([P, HALF], U8, name="ws_raw", align_bytes=64, offset=8 * HALF)
+        tab_s = keep.tile([P, T], U8, name="tab_s", tag="tab_s", align_bytes=64)
+        w_raw = stage.tile([P, R], I32, name="w_raw", align_bytes=64, offset=10048)
+        ws_raw = keep.tile([P, HALF], U8, name="ws_raw", align_bytes=64)
 
         nc.vector.memset(tab_s[:].bitcast(I32), 0)
         nc.vector.memset(ws_raw[:].bitcast(I32), 0)
@@ -52,18 +52,20 @@ def tile_list_pnet_mix_none_kernel(
         w_rows = w_words[0].rearrange("p r i -> p (r i)").bitcast(I32)
         wc_rows = wc.rearrange("(p i) r -> p i r", i=PACK)
         c_rows = c.rearrange("(p i) j -> p i j", i=PACK)
-        nc.sync.dma_start(offsets[:], offs)
 
         def load_table(n):
             cols = slice(TAB_CUTS[n], TAB_CUTS[n + 1])
             nc.sync.dma_start(out=tab_w[:, cols].bitcast(I32), in_=tab_rows[:, cols])
 
         load_table(0)
-        load_scale_rows(nc.sync, tab_s, tab_scales[0])
+        nc.sync.dma_start(offsets[:], offs)
         load_table(1)
+        load_scale_rows(nc.sync, tab_s, tab_scales[0])
+        load_table(2)
         ws_rows = w_scales[0].bitcast(I32).rearrange("q (g r) -> g q r", g=2)
         for q in range(4):
             nc.sync.dma_start(out=ws_raw[32 * q : 32 * q + 8, :].bitcast(I32), in_=ws_rows[:, 4 * q : 4 * q + 4, :])
+        load_table(3)
         nc.sync.dma_start(out=w_raw[:], in_=w_rows)
 
         nb_s = keep.tile([P, 2 * J], U8, name="nb_s", align_bytes=64)
@@ -84,7 +86,11 @@ def tile_list_pnet_mix_none_kernel(
         load_scale_rows(nc.sync, wd_s[:, 0:N], wd8_scales[0])
         load_scale_rows(nc.sync, wd_s[:, N : 2 * N], wd4_scales[0])
 
-        w_s = keep.tile([P, HALF], U8, name="w_s", align_bytes=64)
+        w_s = keep.tile([P, HALF], U8, name="w_s", tag="tab_s", align_bytes=64)
+        nc.vector.tensor_copy(
+            w_s[:].rearrange("p (t m e) -> p m t e", t=PACK, e=16),
+            ws_raw[:].rearrange("p (m e t) -> p m t e", t=PACK, e=16),
+        )
         w_w = keep.tile([P, R], I32, name="w_w", align_bytes=64)
 
         def gather_words(dst, a):
@@ -92,15 +98,12 @@ def tile_list_pnet_mix_none_kernel(
 
         nb_w0 = keep.tile([P, J], U32, name="nb_w0", align_bytes=64)
         gather_words(nb_w0, 0)
-        nc.vector.tensor_copy(
-            w_s[:].rearrange("p (t m e) -> p m t e", t=PACK, e=16),
-            ws_raw[:].rearrange("p (m e t) -> p m t e", t=PACK, e=16),
-        )
-        nc.vector.tensor_copy(
-            w_w[:].rearrange("p (g t m e) -> p g m t e", g=2, t=PACK, e=4),
-            w_raw[:].rearrange("p (g m e t) -> p g m t e", g=2, t=PACK, e=4),
-        )
-        nb_w1 = head.tile([P, J], U32, name="nb_w1", align_bytes=64, offset=5 * HALF)
+        for g in range(2):
+            nc.vector.tensor_copy(
+                w_w[:, HALF * g : HALF * (g + 1)].rearrange("p (t m e) -> p m t e", t=PACK, e=4),
+                w_raw[:, HALF * g : HALF * (g + 1)].rearrange("p (m e t) -> p m t e", t=PACK, e=4),
+            )
+        nb_w1 = stage.tile([P, J], U32, name="nb_w1", align_bytes=64, offset=12096)
         gather_words(nb_w1, 1)
         nb_w = [nb_w0, nb_w1]
 
@@ -125,39 +128,35 @@ def tile_list_pnet_mix_none_kernel(
         pooled = {}
 
         def first_neighbour(gb):
-            a0 = psum.tile([P, PACK, JB], F32, tag=("a0", "ac")[plain.index(gb) % 2], name="a0")
+            a0 = psum.tile([P, PACK, JB], F32, tag=("a0", "ac")[plain.index(gb) // 2 % 2], name="a0")
             neighbour_passes(a0, 0, gb[0], gb[1], True)
             firsts[gb] = keep.tile([P, JB, PACK], F32, name=f"first{gb[0]}{gb[1]}", tag=f"first{gb[0]}{gb[1]}", align_bytes=64)
             nc.scalar.copy(firsts[gb][:], by_point(a0))
 
-        def second_neighbour(gb):
-            a1 = psum.tile([P, PACK, JB], F32, tag=("a1", "y")[plain.index(gb) % 2], name="a1")
-            neighbour_passes(a1, 1, gb[0], gb[1], True)
-            pooled[gb] = keep.tile([P, JB, PACK], F32, name=f"pooled{gb[0]}{gb[1]}")
-            nc.vector.tensor_tensor(pooled[gb][:], by_point(a1), firsts[gb][:], ALU.max)
+        seconds = {}
+        sums = {}
 
-        for s in range(len(plain) + 1):
-            if s < len(plain):
-                first_neighbour(plain[s])
+        def pool_neighbours(gb, tile):
+            pooled[gb] = tile
+            nc.vector.tensor_tensor(tile[:], by_point(seconds[gb]), firsts[gb][:], ALU.max)
+
+        def second_neighbour(gb):
+            a1 = psum.tile([P, PACK, JB], F32, tag=("y", "a1")[plain.index(gb) // 2 % 2], name="a1")
+            neighbour_passes(a1, 1, gb[0], gb[1], True)
+            seconds[gb] = a1
+            if gb not in plain[-2:]:
+                pool_neighbours(gb, keep.tile([P, JB, PACK], F32, name=f"pooled{gb[0]}{gb[1]}"))
+
+        for s in range(len(plain)):
+            first_neighbour(plain[s])
             if s >= 1:
                 second_neighbour(plain[s - 1])
+        second_neighbour(plain[-1])
 
-        sums = {}
-        for gb in FUSED:
-            s0 = psum.tile([P, PACK, JB], F32, tag="a0", name="s0")
-            s1 = psum.tile([P, PACK, JB], F32, tag="a1", name="s1")
-            neighbour_passes(s0, 0, gb[0], gb[1], False)
-            neighbour_passes(s1, 1, gb[0], gb[1], False)
-            sums[gb] = (s0, s1)
-
-        c_bf = [head.tile([P, J // 2, PACK], BF16, name="c_bf0", align_bytes=64, offset=0)]
-        last = plain[-2]
-        c_w = [
-            keep.tile([P, J // 2], U32, name="c_w0", tag=f"first{last[0]}{last[1]}", align_bytes=64),
-            keep.tile([P, J // 2], U32, name="c_w1", align_bytes=64),
-        ]
+        c_bf = [stage.tile([P, J // 2, PACK], BF16, name="c_bf0", align_bytes=64, offset=8064)]
+        c_w = [keep.tile([P, J // 2], U32, name=f"c_w{u}", align_bytes=64) for u in range(2)]
         c_s = [keep.tile([P, J // 2], U8, name=f"c_s{u}", align_bytes=64) for u in range(2)]
-        wc_bf = [keep.tile([P, PACK, P, PACK], BF16, name="wc_bf0", tag="staged", align_bytes=64)]
+        wc_bf = []
         wc_w = [keep.tile([P, HALF], U32, name=f"wc_w{g}", align_bytes=64) for g in range(2)]
         wc_s = [keep.tile([P, HALF], U8, name=f"wc_s{g}", align_bytes=64) for g in range(2)]
 
@@ -204,7 +203,7 @@ def tile_list_pnet_mix_none_kernel(
 
         def add_own(gb):
             n, e = place[gb]
-            ac = psum.tile([P, PACK, JB], F32, tag="ac", name="ac")
+            ac = psum.tile([P, PACK, JB], F32, tag="a0" if gb in order[:2] else "ac", name="ac")
             own_passes(ac, gb[0], gb[1], True)
             nc.vector.tensor_tensor(pre[n][:, e, :].rearrange("p (j t) -> p j t", t=PACK), by_point(ac), pooled[gb][:], ALU.add)
 
@@ -251,7 +250,7 @@ def tile_list_pnet_mix_none_kernel(
             )
 
         def second_layer(b):
-            y = psum.tile([P, 2, JB], F32, tag="y", name="y")
+            y = psum.tile([P, 2, JB], F32, tag="a1" if b < 2 else "ac", name="y")
             for g in range(2):
                 for x in range(2):
                     second_passes(y[:, x, :], x, g, b, g == 0 and x == 0, g == 1 and x == 1)
@@ -263,7 +262,7 @@ def tile_list_pnet_mix_none_kernel(
 
         def open_last(b):
             for x in range(2):
-                last_y.append(psum.tile([P, JB], F32, tag="ac", name="last_y"))
+                last_y.append(psum.tile([P, JB], F32, tag="a0", name="last_y"))
                 second_passes(last_y[x][:], x, 0, b, True, False)
 
         def close_last(b):
@@ -276,38 +275,48 @@ def tile_list_pnet_mix_none_kernel(
             nc.scalar.dma_start(out=out_rows[:, 1, JB * b : JB * (b + 1)], in_=res[1][:])
 
         round_c(0, "gpsimd")
+        quantize_c(0)
+        wc_bf.append(stage.tile([P, PACK, P, PACK], BF16, name="wc_bf0", align_bytes=64, offset=4032))
         round_wc(0, 0, "gpsimd")
         round_wc(0, 1, "gpsimd")
-        quantize_c(0)
         quantize_wc(0)
-        wc_bf.append(keep.tile([P, PACK, P, PACK], BF16, name="wc_bf1", tag="staged", align_bytes=64))
+        for n, gb in enumerate(plain[-2:]):
+            pool_neighbours(gb, stage.tile([P, JB, PACK], F32, name=f"pooled_late{n}", align_bytes=64, offset=4096 + 2048 * n))
+        wc_bf.append(stage.tile([P, PACK, P, PACK], BF16, name="wc_bf1", align_bytes=64, offset=0))
         round_wc(1, 0, "scalar")
         round_wc(1, 1, "gpsimd")
         add_own(order[0])
-        add_own(order[1])
         quantize_wc(1)
-        relu_pair_on_vector(0)
+        add_own(order[1])
+        for gb in FUSED:
+            s0 = psum.tile([P, PACK, JB], F32, tag="a0", name="s0")
+            s1 = psum.tile([P, PACK, JB], F32, tag="y", name="s1")
+            neighbour_passes(s0, 0, gb[0], gb[1], False)
+            neighbour_passes(s1, 1, gb[0], gb[1], False)
+            sums[gb] = (s0, s1)
+
         c_bf.append(keep.tile([P, J // 2, PACK], BF16, name="c_bf1", tag="wc_raw10", align_bytes=64))
         round_c(1, "scalar")
         quantize_c(1)
+        relu_on_scalar(order[0])
+        relu_on_scalar(order[1])
         add_own(order[2])
-        close_first(order[6])
         add_own(order[3])
-        close_first(order[7])
-        add_own(order[4])
         relu_on_scalar(order[2])
         relu_on_scalar(order[3])
+        add_own(order[4])
+        close_first(order[6])
         quantize_h(0)
         add_own(order[5])
-        relu_on_scalar(order[4])
-        relu_on_scalar(order[5])
-        close_second(order[6])
+        close_first(order[7])
         quantize_h(1)
         second_layer(0)
         second_layer(1)
-        close_second(order[7])
+        relu_pair_on_vector(2)
+        close_second(order[6])
         quantize_h(2)
         second_layer(2)
+        close_second(order[7])
         quantize_h(3)
         open_last(3)
         quantize_h(4)

@@ -21,7 +21,7 @@ PACK = 4
 HALF = P * PACK
 JB = 128
 N_JB = J // JB
-TAB_CUTS = (0, 512, 1280, 3072, T)
+TAB_CUTS = (0, 256, 512, 1792, T)
 FUSED = ((0, 3), (1, 3))
 
 
@@ -60,7 +60,7 @@ def tile_list_pnet_mix_none_kernel(
         load_table(0)
         nc.sync.dma_start(offsets[:], offs)
         load_table(1)
-        load_scale_rows(nc.sync, tab_s, tab_scales[0])
+        nc.sync.dma_start(out=tab_s[0:P:8, :].bitcast(I32), in_=tab_scales[0].bitcast(I32))
         load_table(2)
         ws_rows = w_scales[0].bitcast(I32).rearrange("q (g r) -> g q r", g=2)
         for q in range(4):
@@ -69,7 +69,10 @@ def tile_list_pnet_mix_none_kernel(
         nc.sync.dma_start(out=w_raw[:], in_=w_rows)
 
         nb_s = keep.tile([P, 2 * J], U8, name="nb_s", align_bytes=64)
-        nc.vector.tensor_copy(nb_s[:], tab_s[:].indirect(offsets[:]))
+        picked_s = keep.tile([P, 2 * J], U8, name="picked_s", align_bytes=64)
+        nc.vector.tensor_copy(picked_s[:], tab_s[:].indirect(offsets[:]))
+        for r in range(4):
+            nc.scalar.dma_start(out=nb_s[r:P:32, :].bitcast(I32), in_=picked_s[8 * r : P : 32, :].bitcast(I32))
 
         wd8_w = keep.tile([P, N], U32, name="wd8_w", align_bytes=64)
         wd4_w = keep.tile([P, 2 * N], U8, name="wd4_w", align_bytes=64)

@@ -21,7 +21,9 @@ PACK = 4
 HALF = P * PACK
 JB = 128
 N_JB = J // JB
-TAB_CUTS = (0, 256, 512, 1792, T)
+TAB_CUTS = (0, 768, T)
+SCALE_ROWS = 48
+NB_PLANE = 12
 FUSED = ((0, 3), (1, 3))
 
 
@@ -41,12 +43,13 @@ def tile_list_pnet_mix_none_kernel(
 
         offsets = keep.tile([P, 2 * J // 16], U16, name="offsets")
         tab_w = keep.tile([P, T], U32, name="tab_w", align_bytes=64)
-        tab_s = keep.tile([P, T], U8, name="tab_s", tag="tab_s", align_bytes=64)
+        tab_s = stage.tile([P, T], U8, name="tab_s", align_bytes=64, offset=14080)
         w_raw = stage.tile([P, R], I32, name="w_raw", align_bytes=64, offset=10048)
         ws_raw = keep.tile([P, HALF], U8, name="ws_raw", align_bytes=64)
 
-        nc.vector.memset(tab_s[:].bitcast(I32), 0)
         nc.vector.memset(ws_raw[:].bitcast(I32), 0)
+        nc.vector.memset(tab_s[0:SCALE_ROWS, :].bitcast(I32), 0)
+        nc.vector.memset(tab_s[SCALE_ROWS + 16 : P, :].bitcast(I32), 0)
 
         tab_rows = tab_words[0].rearrange("p t i -> p (t i)").bitcast(I32)
         w_rows = w_words[0].rearrange("p r i -> p (r i)").bitcast(I32)
@@ -57,39 +60,30 @@ def tile_list_pnet_mix_none_kernel(
             cols = slice(TAB_CUTS[n], TAB_CUTS[n + 1])
             nc.sync.dma_start(out=tab_w[:, cols].bitcast(I32), in_=tab_rows[:, cols])
 
-        load_table(0)
+        nc.sync.dma_start(out=tab_s[SCALE_ROWS : SCALE_ROWS + 16, :].bitcast(I32), in_=tab_scales[0].bitcast(I32))
         nc.sync.dma_start(offsets[:], offs)
-        load_table(1)
-        nc.sync.dma_start(out=tab_s[0:P:8, :].bitcast(I32), in_=tab_scales[0].bitcast(I32))
-        load_table(2)
+        load_table(0)
         ws_rows = w_scales[0].bitcast(I32).rearrange("q (g r) -> g q r", g=2)
         for q in range(4):
             nc.sync.dma_start(out=ws_raw[32 * q : 32 * q + 8, :].bitcast(I32), in_=ws_rows[:, 4 * q : 4 * q + 4, :])
-        load_table(3)
-        nc.sync.dma_start(out=w_raw[:], in_=w_rows)
+        load_table(1)
 
         nb_s = keep.tile([P, 2 * J], U8, name="nb_s", align_bytes=64)
-        picked_s = keep.tile([P, 2 * J], U8, name="picked_s", align_bytes=64)
+        picked_s = stage.tile([P, 2 * J], U8, name="picked_s", align_bytes=64, offset=30336)
         nc.vector.tensor_copy(picked_s[:], tab_s[:].indirect(offsets[:]))
         for r in range(4):
-            nc.scalar.dma_start(out=nb_s[r:P:32, :].bitcast(I32), in_=picked_s[8 * r : P : 32, :].bitcast(I32))
+            nc.scalar.dma_start(out=nb_s[NB_PLANE + r : P : 32, :].bitcast(I32), in_=picked_s[SCALE_ROWS + r : SCALE_ROWS + 16 : 4, :].bitcast(I32))
+        nc.sync.dma_start(out=w_raw[:], in_=w_rows)
 
-        wd8_w = keep.tile([P, N], U32, name="wd8_w", align_bytes=64)
-        wd4_w = keep.tile([P, 2 * N], U8, name="wd4_w", align_bytes=64)
-        wd_s = keep.tile([P, 2 * N], U8, name="wd_s", align_bytes=64)
-        c_raw = [keep.tile([P, PACK, 256], F32, name=f"c_raw{u}")[:] for u in range(2)]
-        wc_raw = [[keep.tile([P, PACK, 256], F32, name=f"wc_raw{g}{v}", tag=f"wc_raw{g}{v}", align_bytes=64)[:] for v in range(2)] for g in range(2)]
+        c_raw = [stage.tile([P, PACK, 256], F32, name="c_raw0", align_bytes=64, offset=18112)[:]]
+        wc_half = [stage.tile([P, 2, PACK, 256], F32, name=f"wc_raw{g}", align_bytes=64, offset=(22208, 31296)[g]) for g in range(2)]
+        wc_raw = [[wc_half[g][:, v, :, :] for v in range(2)] for g in range(2)]
         nc.sync.dma_start(out=c_raw[0], in_=c_rows[:, :, 0 : J // 2])
         for g in range(2):
             for v in range(2):
                 nc.sync.dma_start(out=wc_raw[g][v], in_=wc_rows[:, :, HALF * g + 256 * v : HALF * g + 256 * (v + 1)])
-        nc.sync.dma_start(out=c_raw[1], in_=c_rows[:, :, J // 2 : J])
-        nc.sync.dma_start(out=wd8_w[:].bitcast(I32), in_=wd8_words[0].rearrange("p n i -> p (n i)").bitcast(I32))
-        nc.sync.dma_start(out=wd4_w[:].bitcast(I32), in_=wd4_words[0].bitcast(I32))
-        load_scale_rows(nc.sync, wd_s[:, 0:N], wd8_scales[0])
-        load_scale_rows(nc.sync, wd_s[:, N : 2 * N], wd4_scales[0])
 
-        w_s = keep.tile([P, HALF], U8, name="w_s", tag="tab_s", align_bytes=64)
+        w_s = stage.tile([P, HALF], U8, name="w_s", align_bytes=64, offset=14208)
         nc.vector.tensor_copy(
             w_s[:].rearrange("p (t m e) -> p m t e", t=PACK, e=16),
             ws_raw[:].rearrange("p (m e t) -> p m t e", t=PACK, e=16),
@@ -117,7 +111,7 @@ def tile_list_pnet_mix_none_kernel(
                     lhsT=w_w[:, HALF * g + P * t : HALF * g + P * (t + 1)].bitcast(FP8X4),
                     lhsT_scale=w_s[4 * g : P, P * t : P * (t + 1)],
                     rhs=nb_w[a][:, JB * b : JB * (b + 1)].bitcast(FP8X4),
-                    rhs_scale=nb_s[:, J * a + JB * b : J * a + JB * (b + 1)],
+                    rhs_scale=nb_s[NB_PLANE:P, J * a + JB * b : J * a + JB * (b + 1)],
                     start=closed or t == 0,
                     stop=closed,
                 )
@@ -278,7 +272,16 @@ def tile_list_pnet_mix_none_kernel(
             nc.scalar.dma_start(out=out_rows[:, 1, JB * b : JB * (b + 1)], in_=res[1][:])
 
         round_c(0, "gpsimd")
+        c_raw.append(stage.tile([P, PACK, 256], F32, name="c_raw1", align_bytes=64, offset=18112)[:])
+        nc.sync.dma_start(out=c_raw[1], in_=c_rows[:, :, J // 2 : J])
         quantize_c(0)
+        wd8_w = stage.tile([P, N], U32, name="wd8_w", align_bytes=64, offset=8192)
+        wd4_w = stage.tile([P, 2 * N], U8, name="wd4_w", align_bytes=64, offset=9216)
+        wd_s = stage.tile([P, 2 * N], U8, name="wd_s", align_bytes=64, offset=9728)
+        nc.sync.dma_start(out=wd8_w[:].bitcast(I32), in_=wd8_words[0].rearrange("p n i -> p (n i)").bitcast(I32))
+        nc.sync.dma_start(out=wd4_w[:].bitcast(I32), in_=wd4_words[0].bitcast(I32))
+        load_scale_rows(nc.sync, wd_s[:, 0:N], wd8_scales[0])
+        load_scale_rows(nc.sync, wd_s[:, N : 2 * N], wd4_scales[0])
         wc_bf.append(stage.tile([P, PACK, P, PACK], BF16, name="wc_bf0", align_bytes=64, offset=4032))
         round_wc(0, 0, "gpsimd")
         round_wc(0, 1, "gpsimd")
@@ -298,7 +301,7 @@ def tile_list_pnet_mix_none_kernel(
             neighbour_passes(s1, 1, gb[0], gb[1], False)
             sums[gb] = (s0, s1)
 
-        c_bf.append(keep.tile([P, J // 2, PACK], BF16, name="c_bf1", tag="wc_raw10", align_bytes=64))
+        c_bf.append(keep.tile([P, J // 2, PACK], BF16, name="c_bf1", align_bytes=64))
         round_c(1, "scalar")
         quantize_c(1)
         relu_on_scalar(order[0])

@@ -43,9 +43,9 @@ def tile_list_pnet_mix_none_kernel(
 
         offsets = keep.tile([P, 2 * J // 16], U16, name="offsets")
         tab_w = keep.tile([P, T], U32, name="tab_w", align_bytes=64)
-        tab_s = stage.tile([P, T], U8, name="tab_s", align_bytes=64, offset=14080)
+        tab_s = stage.tile([P, T], U8, name="tab_s", align_bytes=64, offset=18368)
         w_raw = stage.tile([P, R], I32, name="w_raw", align_bytes=64, offset=10048)
-        ws_raw = keep.tile([P, HALF], U8, name="ws_raw", align_bytes=64)
+        ws_raw = stage.tile([P, HALF], U8, name="ws_raw", align_bytes=64, offset=30528)
 
         nc.vector.memset(ws_raw[:].bitcast(I32), 0)
         nc.vector.memset(tab_s[0:SCALE_ROWS, :].bitcast(I32), 0)
@@ -67,27 +67,29 @@ def tile_list_pnet_mix_none_kernel(
         for q in range(4):
             nc.sync.dma_start(out=ws_raw[32 * q : 32 * q + 8, :].bitcast(I32), in_=ws_rows[:, 4 * q : 4 * q + 4, :])
         load_table(1)
-
-        nb_s = keep.tile([P, 2 * J], U8, name="nb_s", align_bytes=64)
-        picked_s = stage.tile([P, 2 * J], U8, name="picked_s", align_bytes=64, offset=30336)
-        nc.vector.tensor_copy(picked_s[:], tab_s[:].indirect(offsets[:]))
-        for r in range(4):
-            nc.scalar.dma_start(out=nb_s[NB_PLANE + r : P : 32, :].bitcast(I32), in_=picked_s[SCALE_ROWS + r : SCALE_ROWS + 16 : 4, :].bitcast(I32))
         nc.sync.dma_start(out=w_raw[:], in_=w_rows)
 
-        c_raw = [stage.tile([P, PACK, 256], F32, name="c_raw0", align_bytes=64, offset=18112)[:]]
-        wc_half = [stage.tile([P, 2, PACK, 256], F32, name=f"wc_raw{g}", align_bytes=64, offset=(22208, 31296)[g]) for g in range(2)]
-        wc_raw = [[wc_half[g][:, v, :, :] for v in range(2)] for g in range(2)]
-        nc.sync.dma_start(out=c_raw[0], in_=c_rows[:, :, 0 : J // 2])
-        for g in range(2):
-            for v in range(2):
-                nc.sync.dma_start(out=wc_raw[g][v], in_=wc_rows[:, :, HALF * g + 256 * v : HALF * g + 256 * (v + 1)])
+        nb_s = keep.tile([P, 2 * J], U8, name="nb_s", align_bytes=64)
+        picked_s = stage.tile([P, 2 * J], U8, name="picked_s", align_bytes=64, offset=39104)
+        nc.vector.tensor_copy(picked_s[:], tab_s[:].indirect(offsets[:]))
+        for r in range(4):
+            nc.sync.dma_start(out=nb_s[NB_PLANE + r : P : 32, :].bitcast(I32), in_=picked_s[SCALE_ROWS + r : SCALE_ROWS + 16 : 4, :].bitcast(I32))
 
-        w_s = stage.tile([P, HALF], U8, name="w_s", align_bytes=64, offset=14208)
+        w_s = stage.tile([P, HALF], U8, name="w_s", align_bytes=64, offset=18496)
         nc.vector.tensor_copy(
             w_s[:].rearrange("p (t m e) -> p m t e", t=PACK, e=16),
             ws_raw[:].rearrange("p (m e t) -> p m t e", t=PACK, e=16),
         )
+
+        c_raw = [stage.tile([P, PACK, 256], F32, name=f"c_raw{u}", align_bytes=64, offset=(14336, 40064)[u])[:] for u in range(2)]
+        wc_at = ((22400, 26496), (30976, 35072))
+        wc_raw = [[stage.tile([P, PACK, 256], F32, name=f"wc_raw{g}{v}", align_bytes=64, offset=wc_at[g][v])[:] for v in range(2)] for g in range(2)]
+        nc.sync.dma_start(out=c_raw[0], in_=c_rows[:, :, 0 : J // 2])
+        for g in range(2):
+            for v in range(2):
+                nc.sync.dma_start(out=wc_raw[g][v], in_=wc_rows[:, :, HALF * g + 256 * v : HALF * g + 256 * (v + 1)])
+        nc.sync.dma_start(out=c_raw[1], in_=c_rows[:, :, J // 2 : J])
+
         w_w = keep.tile([P, R], I32, name="w_w", align_bytes=64)
 
         def gather_words(dst, a):
@@ -272,8 +274,6 @@ def tile_list_pnet_mix_none_kernel(
             nc.scalar.dma_start(out=out_rows[:, 1, JB * b : JB * (b + 1)], in_=res[1][:])
 
         round_c(0, "gpsimd")
-        c_raw.append(stage.tile([P, PACK, 256], F32, name="c_raw1", align_bytes=64, offset=18112)[:])
-        nc.sync.dma_start(out=c_raw[1], in_=c_rows[:, :, J // 2 : J])
         quantize_c(0)
         wd8_w = stage.tile([P, N], U32, name="wd8_w", align_bytes=64, offset=8192)
         wd4_w = stage.tile([P, 2 * N], U8, name="wd4_w", align_bytes=64, offset=9216)

@@ -44,7 +44,11 @@ def tile_list_pnet_mix_none_kernel(
         offsets = keep.tile([P, 2 * J // 16], U16, name="offsets")
         tab_w = keep.tile([P, T], U32, name="tab_w", align_bytes=64)
         tab_s = stage.tile([P, T], U8, name="tab_s", align_bytes=64, offset=18368)
-        w_raw = stage.tile([P, R], I32, name="w_raw", align_bytes=64, offset=10048)
+        w_raw = [
+            keep.tile([P, HALF], I32, name="w_raw0", tag="w_raw0", align_bytes=64),
+            stage.tile([P, HALF], I32, name="w_raw1", align_bytes=64, offset=16384),
+        ]
+        c_raw = [keep.tile([P, PACK, 256], F32, name="c_raw0", tag="c_raw0", align_bytes=64)[:]]
         ws_raw = stage.tile([P, HALF], U8, name="ws_raw", align_bytes=64, offset=30528)
 
         nc.vector.memset(ws_raw[:].bitcast(I32), 0)
@@ -67,7 +71,8 @@ def tile_list_pnet_mix_none_kernel(
         for q in range(4):
             nc.sync.dma_start(out=ws_raw[32 * q : 32 * q + 8, :].bitcast(I32), in_=ws_rows[:, 4 * q : 4 * q + 4, :])
         load_table(1)
-        nc.sync.dma_start(out=w_raw[:], in_=w_rows)
+        nc.sync.dma_start(out=w_raw[0][:], in_=w_rows[:, 0:HALF])
+        nc.sync.dma_start(out=c_raw[0], in_=c_rows[:, :, 0 : J // 2])
 
         nb_s = keep.tile([P, 2 * J], U8, name="nb_s", align_bytes=64)
         picked_s = stage.tile([P, 2 * J], U8, name="picked_s", align_bytes=64, offset=39104)
@@ -81,36 +86,39 @@ def tile_list_pnet_mix_none_kernel(
             ws_raw[:].rearrange("p (m e t) -> p m t e", t=PACK, e=16),
         )
 
-        c_raw = [stage.tile([P, PACK, 256], F32, name=f"c_raw{u}", align_bytes=64, offset=(14336, 40064)[u])[:] for u in range(2)]
+        c_raw.append(stage.tile([P, PACK, 256], F32, name="c_raw1", align_bytes=64, offset=40064)[:])
         wc_at = ((22400, 26496), (30976, 35072))
         wc_raw = [[stage.tile([P, PACK, 256], F32, name=f"wc_raw{g}{v}", align_bytes=64, offset=wc_at[g][v])[:] for v in range(2)] for g in range(2)]
-        nc.sync.dma_start(out=c_raw[0], in_=c_rows[:, :, 0 : J // 2])
+        nc.sync.dma_start(out=w_raw[1][:], in_=w_rows[:, HALF:R])
         for g in range(2):
             for v in range(2):
                 nc.sync.dma_start(out=wc_raw[g][v], in_=wc_rows[:, :, HALF * g + 256 * v : HALF * g + 256 * (v + 1)])
         nc.sync.dma_start(out=c_raw[1], in_=c_rows[:, :, J // 2 : J])
 
-        w_w = keep.tile([P, R], I32, name="w_w", align_bytes=64)
+        w_w = [keep.tile([P, HALF], I32, name=f"w_w{g}", align_bytes=64) for g in range(2)]
+
+        def order_words(g):
+            nc.vector.tensor_copy(
+                w_w[g][:].rearrange("p (t m e) -> p m t e", t=PACK, e=4),
+                w_raw[g][:].rearrange("p (m e t) -> p m t e", t=PACK, e=4),
+            )
 
         def gather_words(dst, a):
             nc.vector.tensor_copy(dst[:], tab_w[:].indirect(offsets[:, 32 * a : 32 * (a + 1)]))
 
         nb_w0 = keep.tile([P, J], U32, name="nb_w0", align_bytes=64)
         gather_words(nb_w0, 0)
-        for g in range(2):
-            nc.vector.tensor_copy(
-                w_w[:, HALF * g : HALF * (g + 1)].rearrange("p (t m e) -> p m t e", t=PACK, e=4),
-                w_raw[:, HALF * g : HALF * (g + 1)].rearrange("p (m e t) -> p m t e", t=PACK, e=4),
-            )
-        nb_w1 = stage.tile([P, J], U32, name="nb_w1", align_bytes=64, offset=12096)
+        order_words(0)
+        nb_w1 = keep.tile([P, J], U32, name="nb_w1", tag="w_raw0", align_bytes=64)
         gather_words(nb_w1, 1)
+        order_words(1)
         nb_w = [nb_w0, nb_w1]
 
         def neighbour_passes(bank, a, g, b, closed):
             for t in range(PACK):
                 nc.tensor.matmul_mx(
                     out=bank[:, t, :],
-                    lhsT=w_w[:, HALF * g + P * t : HALF * g + P * (t + 1)].bitcast(FP8X4),
+                    lhsT=w_w[g][:, P * t : P * (t + 1)].bitcast(FP8X4),
                     lhsT_scale=w_s[4 * g : P, P * t : P * (t + 1)],
                     rhs=nb_w[a][:, JB * b : JB * (b + 1)].bitcast(FP8X4),
                     rhs_scale=nb_s[NB_PLANE:P, J * a + JB * b : J * a + JB * (b + 1)],
@@ -129,15 +137,15 @@ def tile_list_pnet_mix_none_kernel(
         def first_neighbour(gb):
             a0 = psum.tile([P, PACK, JB], F32, tag=("a0", "ac")[plain.index(gb) // 2 % 2], name="a0")
             neighbour_passes(a0, 0, gb[0], gb[1], True)
-            firsts[gb] = keep.tile([P, JB, PACK], F32, name=f"first{gb[0]}{gb[1]}", tag=f"first{gb[0]}{gb[1]}", align_bytes=64)
-            nc.scalar.copy(firsts[gb][:], by_point(a0))
+            firsts[gb] = copies[:, plain.index(gb), :, :]
+            nc.scalar.copy(firsts[gb], by_point(a0))
 
         seconds = {}
         sums = {}
 
         def pool_neighbours(gb, tile):
             pooled[gb] = tile
-            nc.vector.tensor_tensor(tile[:], by_point(seconds[gb]), firsts[gb][:], ALU.max)
+            nc.vector.tensor_tensor(tile[:], by_point(seconds[gb]), firsts[gb], ALU.max)
 
         def second_neighbour(gb):
             a1 = psum.tile([P, PACK, JB], F32, tag=("y", "a1")[plain.index(gb) // 2 % 2], name="a1")
@@ -145,12 +153,6 @@ def tile_list_pnet_mix_none_kernel(
             seconds[gb] = a1
             if gb not in plain[-2:]:
                 pool_neighbours(gb, keep.tile([P, JB, PACK], F32, name=f"pooled{gb[0]}{gb[1]}"))
-
-        for s in range(len(plain)):
-            first_neighbour(plain[s])
-            if s >= 1:
-                second_neighbour(plain[s - 1])
-        second_neighbour(plain[-1])
 
         c_bf = [stage.tile([P, J // 2, PACK], BF16, name="c_bf0", align_bytes=64, offset=8064)]
         c_w = [keep.tile([P, J // 2], U32, name=f"c_w{u}", align_bytes=64) for u in range(2)]
@@ -273,8 +275,15 @@ def tile_list_pnet_mix_none_kernel(
             nc.vector.tensor_copy(res[1][:], last_y[1][:])
             nc.scalar.dma_start(out=out_rows[:, 1, JB * b : JB * (b + 1)], in_=res[1][:])
 
-        round_c(0, "gpsimd")
+        round_c(0, "scalar")
         quantize_c(0)
+        copies = keep.tile([P, len(plain), JB, PACK], F32, name="copies", tag="c_raw0", align_bytes=64)
+        for s in range(len(plain)):
+            first_neighbour(plain[s])
+            if s >= 1:
+                second_neighbour(plain[s - 1])
+        second_neighbour(plain[-1])
+
         wd8_w = stage.tile([P, N], U32, name="wd8_w", align_bytes=64, offset=8192)
         wd4_w = stage.tile([P, 2 * N], U8, name="wd4_w", align_bytes=64, offset=9216)
         wd_s = stage.tile([P, 2 * N], U8, name="wd_s", align_bytes=64, offset=9728)
@@ -287,7 +296,7 @@ def tile_list_pnet_mix_none_kernel(
         round_wc(0, 1, "gpsimd")
         quantize_wc(0)
         for n, gb in enumerate(plain[-2:]):
-            pool_neighbours(gb, stage.tile([P, JB, PACK], F32, name=f"pooled_late{n}", align_bytes=64, offset=4096 + 2048 * n))
+            pool_neighbours(gb, stage.tile([P, JB, PACK], F32, name=f"pooled_late{n}", align_bytes=64, offset=wc_at[0][1] + 2048 * n))
         wc_bf.append(stage.tile([P, PACK, P, PACK], BF16, name="wc_bf1", align_bytes=64, offset=0))
         round_wc(1, 0, "scalar")
         round_wc(1, 1, "gpsimd")

@@ -87,12 +87,16 @@ def tile_list_pnet_mix_none_kernel(
         )
 
         c_raw.append(stage.tile([P, PACK, 256], F32, name="c_raw1", align_bytes=64, offset=40064)[:])
-        wc_at = ((22400, 26496), (30976, 35072))
-        wc_raw = [[stage.tile([P, PACK, 256], F32, name=f"wc_raw{g}{v}", align_bytes=64, offset=wc_at[g][v])[:] for v in range(2)] for g in range(2)]
+        wc_at = ((22400, 26496), 30976)
+        wc_late = stage.tile([P, PACK, HALF], F32, name="wc_late", align_bytes=64, offset=wc_at[1])
+        wc_raw = [
+            [stage.tile([P, PACK, 256], F32, name=f"wc_raw0{v}", align_bytes=64, offset=wc_at[0][v])[:] for v in range(2)],
+            [wc_late[:, :, 256 * v : 256 * (v + 1)] for v in range(2)],
+        ]
         nc.sync.dma_start(out=w_raw[1][:], in_=w_rows[:, HALF:R])
-        for g in range(2):
-            for v in range(2):
-                nc.sync.dma_start(out=wc_raw[g][v], in_=wc_rows[:, :, HALF * g + 256 * v : HALF * g + 256 * (v + 1)])
+        for v in range(2):
+            nc.sync.dma_start(out=wc_raw[0][v], in_=wc_rows[:, :, 256 * v : 256 * (v + 1)])
+        nc.sync.dma_start(out=wc_late[:], in_=wc_rows[:, :, HALF:R])
         nc.sync.dma_start(out=c_raw[1], in_=c_rows[:, :, J // 2 : J])
 
         w_w = [keep.tile([P, HALF], I32, name=f"w_w{g}", align_bytes=64) for g in range(2)]

@@ -165,12 +165,8 @@ def tile_list_pnet_mix_none_kernel(
         wc_w = [keep.tile([P, HALF], U32, name=f"wc_w{g}", align_bytes=64) for g in range(2)]
         wc_s = [keep.tile([P, HALF], U8, name=f"wc_s{g}", align_bytes=64) for g in range(2)]
 
-        def round_c(u, engine):
-            src = c_raw[u].rearrange("p i j -> p j i")
-            if engine == "gpsimd":
-                nc.gpsimd.tensor_scalar(c_bf[u][:], src, 1.0, 0.0, ALU.mult, ALU.add)
-            else:
-                nc.scalar.copy(c_bf[u][:], src)
+        def round_c(u):
+            nc.scalar.copy(c_bf[u][:].rearrange("p (a j) i -> p a i j", j=PACK), c_raw[u].rearrange("p i (a j) -> p a i j", j=PACK))
 
         def round_wc(g, v, engine):
             dst = wc_bf[g][:, :, 64 * v : 64 * (v + 1), :].rearrange("p t m i -> p m t i")
@@ -279,7 +275,7 @@ def tile_list_pnet_mix_none_kernel(
             nc.vector.tensor_copy(res[1][:], last_y[1][:])
             nc.scalar.dma_start(out=out_rows[:, 1, JB * b : JB * (b + 1)], in_=res[1][:])
 
-        round_c(0, "scalar")
+        round_c(0)
         quantize_c(0)
         copies = keep.tile([P, len(plain), JB, PACK], F32, name="copies", tag="c_raw0", align_bytes=64)
         for s in range(len(plain)):
@@ -305,8 +301,8 @@ def tile_list_pnet_mix_none_kernel(
         round_wc(1, 0, "scalar")
         round_wc(1, 1, "gpsimd")
         add_own(order[0])
-        quantize_wc(1)
         add_own(order[1])
+        quantize_wc(1)
         for gb in FUSED:
             s0 = psum.tile([P, PACK, JB], F32, tag="a0", name="s0")
             s1 = psum.tile([P, PACK, JB], F32, tag="y", name="s1")
@@ -315,7 +311,7 @@ def tile_list_pnet_mix_none_kernel(
             sums[gb] = (s0, s1)
 
         c_bf.append(keep.tile([P, J // 2, PACK], BF16, name="c_bf1", align_bytes=64))
-        round_c(1, "scalar")
+        round_c(1)
         quantize_c(1)
         relu_on_scalar(order[0])
         relu_on_scalar(order[1])

@@ -101,10 +101,10 @@ def tile_list_pnet_mix_none_kernel(
 
         w_w = [keep.tile([P, HALF], I32, name=f"w_w{g}", align_bytes=64) for g in range(2)]
 
-        def order_words(g):
-            nc.vector.tensor_copy(
-                w_w[g][:].rearrange("p (t m e) -> p m t e", t=PACK, e=4),
-                w_raw[g][:].rearrange("p (m e t) -> p m t e", t=PACK, e=4),
+        def order_words(g, copy, dtype):
+            copy(
+                w_w[g][:].bitcast(dtype).rearrange("p (t m e) -> p m t e", t=PACK, e=4),
+                w_raw[g][:].bitcast(dtype).rearrange("p (m e t) -> p m t e", t=PACK, e=4),
             )
 
         def gather_words(dst, a):
@@ -112,10 +112,10 @@ def tile_list_pnet_mix_none_kernel(
 
         nb_w0 = keep.tile([P, J], U32, name="nb_w0", align_bytes=64)
         gather_words(nb_w0, 0)
-        order_words(0)
-        nb_w1 = keep.tile([P, J], U32, name="nb_w1", tag="w_raw0", align_bytes=64)
+        order_words(0, nc.scalar.copy, U32)
+        nb_w1 = keep.tile([P, J], U32, name="nb_w1", align_bytes=64)
         gather_words(nb_w1, 1)
-        order_words(1)
+        order_words(1, nc.vector.tensor_copy, I32)
         nb_w = [nb_w0, nb_w1]
 
         def neighbour_passes(bank, a, g, b, closed):

@@ -24,7 +24,7 @@ N_JB = J // JB
 TAB_CUTS = (0, 768, T)
 SCALE_ROWS = 48
 NB_PLANE = 12
-FUSED = ((0, 3), (1, 3))
+FUSED = ((1, 2), (1, 3))
 
 
 def load_scale_rows(queue, plane, rows):
@@ -75,7 +75,7 @@ def tile_list_pnet_mix_none_kernel(
         nc.sync.dma_start(out=c_raw[0], in_=c_rows[:, :, 0 : J // 2])
 
         nb_s = keep.tile([P, 2 * J], U8, name="nb_s", align_bytes=64)
-        picked_s = stage.tile([P, 2 * J], U8, name="picked_s", align_bytes=64, offset=39104)
+        picked_s = stage.tile([P, 2 * J], U8, name="picked_s", align_bytes=64, offset=35072)
         nc.vector.tensor_copy(picked_s[:], tab_s[:].indirect(offsets[:]))
         for r in range(4):
             nc.sync.dma_start(out=nb_s[NB_PLANE + r : P : 32, :].bitcast(I32), in_=picked_s[SCALE_ROWS + r : SCALE_ROWS + 16 : 4, :].bitcast(I32))
@@ -86,8 +86,8 @@ def tile_list_pnet_mix_none_kernel(
             ws_raw[:].rearrange("p (m e t) -> p m t e", t=PACK, e=16),
         )
 
-        c_raw.append(stage.tile([P, PACK, 256], F32, name="c_raw1", align_bytes=64, offset=40064)[:])
-        wc_at = ((22400, 26496), 30976)
+        c_raw.append(stage.tile([P, PACK, 256], F32, name="c_raw1", align_bytes=64, offset=30976)[:])
+        wc_at = ((22400, 26496), 36032)
         wc_late = stage.tile([P, PACK, HALF], F32, name="wc_late", align_bytes=64, offset=wc_at[1])
         wc_raw = [
             [stage.tile([P, PACK, 256], F32, name=f"wc_raw0{v}", align_bytes=64, offset=wc_at[0][v])[:] for v in range(2)],
@@ -96,15 +96,15 @@ def tile_list_pnet_mix_none_kernel(
         nc.sync.dma_start(out=w_raw[1][:], in_=w_rows[:, HALF:R])
         for v in range(2):
             nc.sync.dma_start(out=wc_raw[0][v], in_=wc_rows[:, :, 256 * v : 256 * (v + 1)])
-        nc.sync.dma_start(out=wc_late[:], in_=wc_rows[:, :, HALF:R])
         nc.sync.dma_start(out=c_raw[1], in_=c_rows[:, :, J // 2 : J])
+        nc.sync.dma_start(out=wc_late[:], in_=wc_rows[:, :, HALF:R])
 
         w_w = [keep.tile([P, HALF], I32, name=f"w_w{g}", align_bytes=64) for g in range(2)]
 
-        def order_words(g, copy, dtype):
-            copy(
-                w_w[g][:].bitcast(dtype).rearrange("p (t m e) -> p m t e", t=PACK, e=4),
-                w_raw[g][:].bitcast(dtype).rearrange("p (m e t) -> p m t e", t=PACK, e=4),
+        def order_words(g):
+            nc.vector.tensor_copy(
+                w_w[g][:].rearrange("p (t m e) -> p m t e", t=PACK, e=4),
+                w_raw[g][:].rearrange("p (m e t) -> p m t e", t=PACK, e=4),
             )
 
         def gather_words(dst, a):
@@ -112,10 +112,10 @@ def tile_list_pnet_mix_none_kernel(
 
         nb_w0 = keep.tile([P, J], U32, name="nb_w0", align_bytes=64)
         gather_words(nb_w0, 0)
-        order_words(0, nc.scalar.copy, U32)
-        nb_w1 = keep.tile([P, J], U32, name="nb_w1", align_bytes=64)
+        order_words(0)
+        nb_w1 = keep.tile([P, J], U32, name="nb_w1", tag="w_raw0", align_bytes=64)
         gather_words(nb_w1, 1)
-        order_words(1, nc.vector.tensor_copy, I32)
+        order_words(1)
         nb_w = [nb_w0, nb_w1]
 
         def neighbour_passes(bank, a, g, b, closed):
@@ -133,7 +133,7 @@ def tile_list_pnet_mix_none_kernel(
         def by_point(bank):
             return bank[:].rearrange("p t j -> p j t")
 
-        order = [(0, 0), (0, 1), (1, 0), (1, 1), (0, 2), (1, 2), (0, 3), (1, 3)]
+        order = [(0, 0), (0, 1), (1, 0), (1, 1), (0, 2), (0, 3), (1, 2), (1, 3)]
         plain = [gb for gb in order if gb not in FUSED]
         firsts = {}
         pooled = {}
@@ -204,7 +204,7 @@ def tile_list_pnet_mix_none_kernel(
 
         def add_own(gb):
             n, e = place[gb]
-            ac = psum.tile([P, PACK, JB], F32, tag="a0" if gb in order[:2] else "ac", name="ac")
+            ac = psum.tile([P, PACK, JB], F32, tag=("a0", "a1", "ac")[n], name="ac")
             own_passes(ac, gb[0], gb[1], True)
             nc.vector.tensor_tensor(pre[n][:, e, :].rearrange("p (j t) -> p j t", t=PACK), by_point(ac), pooled[gb][:], ALU.add)
 
@@ -251,7 +251,7 @@ def tile_list_pnet_mix_none_kernel(
             )
 
         def second_layer(b):
-            y = psum.tile([P, 2, JB], F32, tag="a1" if b < 2 else "ac", name="y")
+            y = psum.tile([P, 2, JB], F32, tag="ac" if b < 2 else "a1", name="y")
             for g in range(2):
                 for x in range(2):
                     second_passes(y[:, x, :], x, g, b, g == 0 and x == 0, g == 1 and x == 1)
@@ -278,7 +278,10 @@ def tile_list_pnet_mix_none_kernel(
         round_c(0)
         quantize_c(0)
         copies = keep.tile([P, len(plain), JB, PACK], F32, name="copies", tag="c_raw0", align_bytes=64)
+        c_bf.append(stage.tile([P, J // 2, PACK], BF16, name="c_bf1", align_bytes=64, offset=0))
         for s in range(len(plain)):
+            if s == len(plain) - 2:
+                round_c(1)
             first_neighbour(plain[s])
             if s >= 1:
                 second_neighbour(plain[s - 1])
@@ -295,14 +298,21 @@ def tile_list_pnet_mix_none_kernel(
         round_wc(0, 0, "gpsimd")
         round_wc(0, 1, "gpsimd")
         quantize_wc(0)
-        for n, gb in enumerate(plain[-2:]):
-            pool_neighbours(gb, stage.tile([P, JB, PACK], F32, name=f"pooled_late{n}", align_bytes=64, offset=wc_at[0][1] + 2048 * n))
+
+        def late_maximum(n):
+            pool_neighbours(plain[-2 + n], stage.tile([P, JB, PACK], F32, name=f"pooled_late{n}", align_bytes=64, offset=wc_at[0][1] + 2048 * n))
+
+        quantize_c(1)
+        late_maximum(0)
+        late_maximum(1)
         wc_bf.append(stage.tile([P, PACK, P, PACK], BF16, name="wc_bf1", align_bytes=64, offset=0))
         round_wc(1, 0, "scalar")
         round_wc(1, 1, "gpsimd")
         add_own(order[0])
         add_own(order[1])
+        add_own(order[4])
         quantize_wc(1)
+        add_own(order[5])
         for gb in FUSED:
             s0 = psum.tile([P, PACK, JB], F32, tag="a0", name="s0")
             s1 = psum.tile([P, PACK, JB], F32, tag="y", name="s1")
@@ -310,29 +320,22 @@ def tile_list_pnet_mix_none_kernel(
             neighbour_passes(s1, 1, gb[0], gb[1], False)
             sums[gb] = (s0, s1)
 
-        c_bf.append(keep.tile([P, J // 2, PACK], BF16, name="c_bf1", align_bytes=64))
-        round_c(1)
-        quantize_c(1)
-        relu_on_scalar(order[0])
-        relu_on_scalar(order[1])
+        for gb in order[0:2] + order[4:6]:
+            relu_on_scalar(gb)
+        quantize_h(0)
         add_own(order[2])
         add_own(order[3])
-        relu_on_scalar(order[2])
-        relu_on_scalar(order[3])
-        add_own(order[4])
         close_first(order[6])
-        quantize_h(0)
-        add_own(order[5])
         close_first(order[7])
+        quantize_h(2)
+        relu_pair_on_vector(1)
+        close_second(order[6])
         quantize_h(1)
         second_layer(0)
         second_layer(1)
-        relu_pair_on_vector(2)
-        close_second(order[6])
-        quantize_h(2)
-        second_layer(2)
         close_second(order[7])
         quantize_h(3)
+        second_layer(2)
         open_last(3)
         quantize_h(4)
         close_last(3)

@@ -222,9 +222,6 @@ def tile_list_pnet_mix_none_kernel(
                 h_bf[n][:, e, :].rearrange("p (j t) -> p j t", t=PACK), by_point(s1), 0.0, firsts[gb][:], ALU.max, ALU.max
             )
 
-        def relu_pair_on_vector(n):
-            nc.vector.tensor_scalar_max(h_bf[n][:].rearrange("p e x -> p (e x)"), pre[n][:].rearrange("p e x -> p (e x)"), 0.0)
-
         def relu_on_scalar(gb):
             n, e = place[gb]
             nc.scalar.activation(h_bf[n][:, e, :], pre[n][:, e, :], RELU)
@@ -326,9 +323,10 @@ def tile_list_pnet_mix_none_kernel(
         add_own(order[2])
         add_own(order[3])
         close_first(order[6])
+        relu_on_scalar(order[2])
         close_first(order[7])
         quantize_h(2)
-        relu_pair_on_vector(1)
+        nc.vector.tensor_scalar_max(h_bf[1][:, 1, :], pre[1][:, 1, :], 0.0)
         close_second(order[6])
         quantize_h(1)
         second_layer(0)

@@ -24,6 +24,7 @@ N_JB = J // JB
 TAB_CUTS = (0, 768, T)
 SCALE_ROWS = 48
 NB_PLANE = 12
+WC_CUT = 352
 FUSED = ((1, 2), (1, 3))
 
 
@@ -75,7 +76,7 @@ def tile_list_pnet_mix_none_kernel(
         nc.sync.dma_start(out=c_raw[0], in_=c_rows[:, :, 0 : J // 2])
 
         nb_s = keep.tile([P, 2 * J], U8, name="nb_s", align_bytes=64)
-        picked_s = stage.tile([P, 2 * J], U8, name="picked_s", align_bytes=64, offset=35072)
+        picked_s = stage.tile([P, 2 * J], U8, name="picked_s", align_bytes=64, offset=39168)
         nc.vector.tensor_copy(picked_s[:], tab_s[:].indirect(offsets[:]))
         for r in range(4):
             nc.sync.dma_start(out=nb_s[NB_PLANE + r : P : 32, :].bitcast(I32), in_=picked_s[SCALE_ROWS + r : SCALE_ROWS + 16 : 4, :].bitcast(I32))
@@ -87,17 +88,15 @@ def tile_list_pnet_mix_none_kernel(
         )
 
         c_raw.append(stage.tile([P, PACK, 256], F32, name="c_raw1", align_bytes=64, offset=30976)[:])
-        wc_at = ((22400, 26496), 36032)
-        wc_late = stage.tile([P, PACK, HALF], F32, name="wc_late", align_bytes=64, offset=wc_at[1])
-        wc_raw = [
-            [stage.tile([P, PACK, 256], F32, name=f"wc_raw0{v}", align_bytes=64, offset=wc_at[0][v])[:] for v in range(2)],
-            [wc_late[:, :, 256 * v : 256 * (v + 1)] for v in range(2)],
-        ]
+        wc_at = ((22400, 26496), (35136, 40128))
+        wc_late = [stage.tile([P, PACK, 256], F32, name=f"wc_late{v}", align_bytes=64, offset=wc_at[1][v]) for v in range(2)]
+        wc_raw = [stage.tile([P, PACK, 256], F32, name=f"wc_raw0{v}", align_bytes=64, offset=wc_at[0][v])[:] for v in range(2)]
         nc.sync.dma_start(out=w_raw[1][:], in_=w_rows[:, HALF:R])
         for v in range(2):
-            nc.sync.dma_start(out=wc_raw[0][v], in_=wc_rows[:, :, 256 * v : 256 * (v + 1)])
+            nc.sync.dma_start(out=wc_raw[v], in_=wc_rows[:, :, 256 * v : 256 * (v + 1)])
         nc.sync.dma_start(out=c_raw[1], in_=c_rows[:, :, J // 2 : J])
-        nc.sync.dma_start(out=wc_late[:], in_=wc_rows[:, :, HALF:R])
+        for v in range(2):
+            nc.sync.dma_start(out=wc_late[v][:], in_=wc_rows[:, :, HALF + 256 * v : HALF + 256 * (v + 1)])
 
         w_w = [keep.tile([P, HALF], I32, name=f"w_w{g}", align_bytes=64) for g in range(2)]
 
@@ -168,9 +167,9 @@ def tile_list_pnet_mix_none_kernel(
         def round_c(u):
             nc.scalar.copy(c_bf[u][:].rearrange("p (a j) i -> p a i j", j=PACK), c_raw[u].rearrange("p i (a j) -> p a i j", j=PACK))
 
-        def round_wc(g, v, engine):
-            dst = wc_bf[g][:, :, 64 * v : 64 * (v + 1), :].rearrange("p t m i -> p m t i")
-            src = wc_raw[g][v].rearrange("p i (m t) -> p m t i", t=PACK)
+        def round_wc(g, raw, first, engine):
+            dst = wc_bf[g][:, :, first // PACK : (first + raw.shape[2]) // PACK, :].rearrange("p t m i -> p m t i")
+            src = raw.rearrange("p i (m t) -> p m t i", t=PACK)
             if engine == "gpsimd":
                 nc.gpsimd.tensor_scalar(dst, src, 1.0, 0.0, ALU.mult, ALU.add)
             else:
@@ -275,7 +274,8 @@ def tile_list_pnet_mix_none_kernel(
         round_c(0)
         quantize_c(0)
         copies = keep.tile([P, len(plain), JB, PACK], F32, name="copies", tag="c_raw0", align_bytes=64)
-        c_bf.append(stage.tile([P, J // 2, PACK], BF16, name="c_bf1", align_bytes=64, offset=0))
+        late_bf = keep.tile([P, 1536 + WC_CUT + 1024], BF16, name="late_bf", align_bytes=64)
+        c_bf.append(late_bf[:, 1536 + WC_CUT :].rearrange("p (j i) -> p j i", i=PACK))
         for s in range(len(plain)):
             if s == len(plain) - 2:
                 round_c(1)
@@ -292,8 +292,8 @@ def tile_list_pnet_mix_none_kernel(
         load_scale_rows(nc.sync, wd_s[:, 0:N], wd8_scales[0])
         load_scale_rows(nc.sync, wd_s[:, N : 2 * N], wd4_scales[0])
         wc_bf.append(stage.tile([P, PACK, P, PACK], BF16, name="wc_bf0", align_bytes=64, offset=4032))
-        round_wc(0, 0, "gpsimd")
-        round_wc(0, 1, "gpsimd")
+        round_wc(0, wc_raw[0], 0, "gpsimd")
+        round_wc(0, wc_raw[1], 256, "gpsimd")
         quantize_wc(0)
 
         def late_maximum(n):
@@ -302,9 +302,10 @@ def tile_list_pnet_mix_none_kernel(
         quantize_c(1)
         late_maximum(0)
         late_maximum(1)
-        wc_bf.append(stage.tile([P, PACK, P, PACK], BF16, name="wc_bf1", align_bytes=64, offset=0))
-        round_wc(1, 0, "scalar")
-        round_wc(1, 1, "gpsimd")
+        wc_bf.append(late_bf[:, 0:2048].rearrange("p (t m i) -> p t m i", t=PACK, i=PACK))
+        round_wc(1, wc_late[0][:], 0, "scalar")
+        round_wc(1, wc_late[1][:, :, 0 : WC_CUT - 256], 256, "scalar")
+        round_wc(1, wc_late[1][:, :, WC_CUT - 256 : 256], WC_CUT, "gpsimd")
         add_own(order[0])
         add_own(order[1])
         add_own(order[4])

@@ -50,9 +50,9 @@ def tile_list_pnet_mix_none_kernel(
             stage.tile([P, HALF], I32, name="w_raw1", align_bytes=64, offset=16384),
         ]
         c_raw = [keep.tile([P, PACK, 256], F32, name="c_raw0", tag="c_raw0", align_bytes=64)[:]]
-        ws_raw = stage.tile([P, HALF], U8, name="ws_raw", align_bytes=64, offset=30528)
+        ws_raw = stage.tile([P, 12736], U8, name="ws_room", align_bytes=64, offset=30528)[:, 0:HALF]
 
-        nc.vector.memset(ws_raw[:].bitcast(I32), 0)
+        nc.vector.memset(ws_raw.bitcast(I32), 0)
         nc.vector.memset(tab_s[0:SCALE_ROWS, :].bitcast(I32), 0)
         nc.vector.memset(tab_s[SCALE_ROWS + 16 : P, :].bitcast(I32), 0)
 
@@ -76,7 +76,7 @@ def tile_list_pnet_mix_none_kernel(
         nc.sync.dma_start(out=c_raw[0], in_=c_rows[:, :, 0 : J // 2])
 
         nb_s = keep.tile([P, 2 * J], U8, name="nb_s", align_bytes=64)
-        picked_s = stage.tile([P, 2 * J], U8, name="picked_s", align_bytes=64, offset=39168)
+        picked_s = keep.tile([P, 2 * J], U8, name="picked_s", align_bytes=64)
         nc.vector.tensor_copy(picked_s[:], tab_s[:].indirect(offsets[:]))
         for r in range(4):
             nc.sync.dma_start(out=nb_s[NB_PLANE + r : P : 32, :].bitcast(I32), in_=picked_s[SCALE_ROWS + r : SCALE_ROWS + 16 : 4, :].bitcast(I32))
@@ -84,11 +84,11 @@ def tile_list_pnet_mix_none_kernel(
         w_s = stage.tile([P, HALF], U8, name="w_s", align_bytes=64, offset=18496)
         nc.vector.tensor_copy(
             w_s[:].rearrange("p (t m e) -> p m t e", t=PACK, e=16),
-            ws_raw[:].rearrange("p (m e t) -> p m t e", t=PACK, e=16),
+            ws_raw.rearrange("p (m e t) -> p m t e", t=PACK, e=16),
         )
 
         c_raw.append(stage.tile([P, PACK, 256], F32, name="c_raw1", align_bytes=64, offset=30976)[:])
-        wc_at = ((22400, 26496), (35136, 40128))
+        wc_at = ((22400, 26496), (35072, 39168))
         wc_late = [stage.tile([P, PACK, 256], F32, name=f"wc_late{v}", align_bytes=64, offset=wc_at[1][v]) for v in range(2)]
         wc_raw = [stage.tile([P, PACK, 256], F32, name=f"wc_raw0{v}", align_bytes=64, offset=wc_at[0][v])[:] for v in range(2)]
         nc.sync.dma_start(out=w_raw[1][:], in_=w_rows[:, HALF:R])
@@ -100,10 +100,10 @@ def tile_list_pnet_mix_none_kernel(
 
         w_w = [keep.tile([P, HALF], I32, name=f"w_w{g}", align_bytes=64) for g in range(2)]
 
-        def order_words(g):
-            nc.vector.tensor_copy(
-                w_w[g][:].rearrange("p (t m e) -> p m t e", t=PACK, e=4),
-                w_raw[g][:].rearrange("p (m e t) -> p m t e", t=PACK, e=4),
+        def order_words(g, copy, dtype):
+            copy(
+                w_w[g][:].bitcast(dtype).rearrange("p (t m e) -> p m t e", t=PACK, e=4),
+                w_raw[g][:].bitcast(dtype).rearrange("p (m e t) -> p m t e", t=PACK, e=4),
             )
 
         def gather_words(dst, a):
@@ -111,10 +111,10 @@ def tile_list_pnet_mix_none_kernel(
 
         nb_w0 = keep.tile([P, J], U32, name="nb_w0", align_bytes=64)
         gather_words(nb_w0, 0)
-        order_words(0)
-        nb_w1 = keep.tile([P, J], U32, name="nb_w1", tag="w_raw0", align_bytes=64)
+        order_words(0, nc.scalar.copy, U32)
+        nb_w1 = keep.tile([P, J], U32, name="nb_w1", align_bytes=64)
         gather_words(nb_w1, 1)
-        order_words(1)
+        order_words(1, nc.vector.tensor_copy, I32)
         nb_w = [nb_w0, nb_w1]
 
         def neighbour_passes(bank, a, g, b, closed):
@@ -284,9 +284,9 @@ def tile_list_pnet_mix_none_kernel(
                 second_neighbour(plain[s - 1])
         second_neighbour(plain[-1])
 
-        wd8_w = stage.tile([P, N], U32, name="wd8_w", align_bytes=64, offset=8192)
-        wd4_w = stage.tile([P, 2 * N], U8, name="wd4_w", align_bytes=64, offset=9216)
-        wd_s = stage.tile([P, 2 * N], U8, name="wd_s", align_bytes=64, offset=9728)
+        wd8_w = stage.tile([P, N], U32, name="wd8_w", align_bytes=64, offset=22464)
+        wd4_w = stage.tile([P, 2 * N], U8, name="wd4_w", align_bytes=64, offset=23488)
+        wd_s = stage.tile([P, 2 * N], U8, name="wd_s", align_bytes=64, offset=24000)
         nc.sync.dma_start(out=wd8_w[:].bitcast(I32), in_=wd8_words[0].rearrange("p n i -> p (n i)").bitcast(I32))
         nc.sync.dma_start(out=wd4_w[:].bitcast(I32), in_=wd4_words[0].bitcast(I32))
         load_scale_rows(nc.sync, wd_s[:, 0:N], wd8_scales[0])

@@ -20,17 +20,15 @@ P = 128
 PACK = 4
 HALF = P * PACK
 JB = 128
-N_JB = J // JB
-TAB_CUTS = (0, 768, T)
+QUARTER = 256
+TAB_CUT = 1792
 SCALE_ROWS = 48
-NB_PLANE = 12
+PLANE = 12
 WC_CUT = 352
+PLAIN = ((0, 0), (0, 1), (1, 0), (1, 1), (0, 2), (0, 3))
+FIRST_BANK = (0, 1, 4, 5, 0, 1)
+SECOND_BANK = (2, 3, 6, 7, 2, 3)
 FUSED = ((1, 2), (1, 3))
-
-
-def load_scale_rows(queue, plane, rows):
-    for r in range(4):
-        queue.dma_start(out=plane[r:P:32, :].bitcast(I32), in_=rows[r:16:4, :].bitcast(I32))
 
 
 def tile_list_pnet_mix_none_kernel(
@@ -40,152 +38,153 @@ def tile_list_pnet_mix_none_kernel(
     with ExitStack() as ctx:
         keep = ctx.enter_context(tc.tile_pool(name="keep", bufs=1))
         stage = ctx.enter_context(tc.tile_pool(name="stage", bufs=1))
-        psum = ctx.enter_context(tc.psum_pool(name="psum", bufs=2))
+        psum = ctx.enter_context(tc.psum_pool(name="psum", bufs=1))
+
+        def bank(n, shape):
+            return psum.tile(shape, F32, tag=f"bank{n}", name=f"bank{n}")
+
+        def staged(name, shape, dtype, offset):
+            return stage.tile(shape, dtype, name=name, align_bytes=64, offset=offset)
 
         offsets = keep.tile([P, 2 * J // 16], U16, name="offsets")
         tab_w = keep.tile([P, T], U32, name="tab_w", align_bytes=64)
-        tab_s = stage.tile([P, T], U8, name="tab_s", align_bytes=64, offset=18368)
-        w_raw = [
-            keep.tile([P, HALF], I32, name="w_raw0", tag="w_raw0", align_bytes=64),
-            stage.tile([P, HALF], I32, name="w_raw1", align_bytes=64, offset=16384),
-        ]
-        c_raw = [keep.tile([P, PACK, 256], F32, name="c_raw0", tag="c_raw0", align_bytes=64)[:]]
-        ws_raw = stage.tile([P, 12736], U8, name="ws_room", align_bytes=64, offset=30528)[:, 0:HALF]
-
+        tab_s = staged("tab_s", [P, T], U8, 49152)
+        ws_raw = staged("ws_raw", [P, 28672], U8, 0)[:, 0:HALF]
         nc.vector.memset(ws_raw.bitcast(I32), 0)
         nc.vector.memset(tab_s[0:SCALE_ROWS, :].bitcast(I32), 0)
-        nc.vector.memset(tab_s[SCALE_ROWS + 16 : P, :].bitcast(I32), 0)
+        nc.gpsimd.memset(tab_s[SCALE_ROWS + 16 : P, :].bitcast(I32), 0)
 
         tab_rows = tab_words[0].rearrange("p t i -> p (t i)").bitcast(I32)
         w_rows = w_words[0].rearrange("p r i -> p (r i)").bitcast(I32)
         wc_rows = wc.rearrange("(p i) r -> p i r", i=PACK)
         c_rows = c.rearrange("(p i) j -> p i j", i=PACK)
 
-        def load_table(n):
-            cols = slice(TAB_CUTS[n], TAB_CUTS[n + 1])
-            nc.sync.dma_start(out=tab_w[:, cols].bitcast(I32), in_=tab_rows[:, cols])
-
+        w_raw = [keep.tile([P, HALF], I32, name="w_raw0", align_bytes=64)]
+        ws_rows = w_scales[0].bitcast(I32).rearrange("q (g r) -> g q r", g=2)
         nc.sync.dma_start(out=tab_s[SCALE_ROWS : SCALE_ROWS + 16, :].bitcast(I32), in_=tab_scales[0].bitcast(I32))
         nc.sync.dma_start(offsets[:], offs)
-        load_table(0)
-        ws_rows = w_scales[0].bitcast(I32).rearrange("q (g r) -> g q r", g=2)
+        nc.sync.dma_start(out=tab_w[:, 0:TAB_CUT].bitcast(I32), in_=tab_rows[:, 0:TAB_CUT])
         for q in range(4):
             nc.sync.dma_start(out=ws_raw[32 * q : 32 * q + 8, :].bitcast(I32), in_=ws_rows[:, 4 * q : 4 * q + 4, :])
-        load_table(1)
         nc.sync.dma_start(out=w_raw[0][:], in_=w_rows[:, 0:HALF])
-        nc.sync.dma_start(out=c_raw[0], in_=c_rows[:, :, 0 : J // 2])
+        nc.sync.dma_start(out=tab_w[:, TAB_CUT:T].bitcast(I32), in_=tab_rows[:, TAB_CUT:T])
 
+        picked = keep.tile([P, 2 * J], U8, name="picked", align_bytes=64)
         nb_s = keep.tile([P, 2 * J], U8, name="nb_s", align_bytes=64)
-        picked_s = keep.tile([P, 2 * J], U8, name="picked_s", align_bytes=64)
-        nc.vector.tensor_copy(picked_s[:], tab_s[:].indirect(offsets[:]))
-        for r in range(4):
-            nc.sync.dma_start(out=nb_s[NB_PLANE + r : P : 32, :].bitcast(I32), in_=picked_s[SCALE_ROWS + r : SCALE_ROWS + 16 : 4, :].bitcast(I32))
-
-        w_s = stage.tile([P, HALF], U8, name="w_s", align_bytes=64, offset=18496)
+        nc.vector.tensor_copy(picked[:], tab_s[:].indirect(offsets[:]))
+        for q in range(4):
+            nc.sync.dma_start(
+                out=nb_s[32 * q + PLANE : 32 * q + PLANE + 4, :].bitcast(I32),
+                in_=picked[SCALE_ROWS + 4 * q : SCALE_ROWS + 4 * q + 4, :].bitcast(I32),
+            )
+        w_s = staged("w_s", [P, HALF], U8, 49152)
         nc.vector.tensor_copy(
             w_s[:].rearrange("p (t m e) -> p m t e", t=PACK, e=16),
             ws_raw.rearrange("p (m e t) -> p m t e", t=PACK, e=16),
         )
 
-        c_raw.append(stage.tile([P, PACK, 256], F32, name="c_raw1", align_bytes=64, offset=30976)[:])
-        wc_at = ((22400, 26496), (35072, 39168))
-        wc_late = [stage.tile([P, PACK, 256], F32, name=f"wc_late{v}", align_bytes=64, offset=wc_at[1][v]) for v in range(2)]
-        wc_raw = [stage.tile([P, PACK, 256], F32, name=f"wc_raw0{v}", align_bytes=64, offset=wc_at[0][v])[:] for v in range(2)]
+        c_raw = [staged("c_raw0", [P, PACK, QUARTER], F32, 49152 + 4032), staged("c_raw1", [P, PACK, QUARTER], F32, 4096)]
+        w_raw.append(staged("w_raw1", [P, HALF], I32, 24576))
+        wc_raw = [staged(f"wc_raw{v}", [P, PACK, QUARTER], F32, 8192 + 4096 * v) for v in range(4)]
+        wd8_w = staged("wd8_w", [P, N], U32, 26624)
+        wd4_w = staged("wd4_w", [P, 2 * N], U8, 27648)
+        wd_s = staged("wd_s", [P, 2 * N], U8, 28160)
+
+        def load_c(u):
+            nc.sync.dma_start(out=c_raw[u][:], in_=c_rows[:, :, QUARTER * u : QUARTER * (u + 1)])
+
+        def load_wc(v):
+            nc.sync.dma_start(out=wc_raw[v][:], in_=wc_rows[:, :, QUARTER * v : QUARTER * (v + 1)])
+
+        load_c(0)
         nc.sync.dma_start(out=w_raw[1][:], in_=w_rows[:, HALF:R])
-        for v in range(2):
-            nc.sync.dma_start(out=wc_raw[v], in_=wc_rows[:, :, 256 * v : 256 * (v + 1)])
-        nc.sync.dma_start(out=c_raw[1], in_=c_rows[:, :, J // 2 : J])
-        for v in range(2):
-            nc.sync.dma_start(out=wc_late[v][:], in_=wc_rows[:, :, HALF + 256 * v : HALF + 256 * (v + 1)])
+        load_wc(0)
+        load_wc(1)
+        load_c(1)
+        load_wc(2)
+        load_wc(3)
+        nc.sync.dma_start(out=wd8_w[:].bitcast(I32), in_=wd8_words[0].rearrange("p n i -> p (n i)").bitcast(I32))
+        nc.sync.dma_start(out=wd4_w[:].bitcast(I32), in_=wd4_words[0].bitcast(I32))
+        for g, scales in enumerate((wd8_scales, wd4_scales)):
+            for r in range(4):
+                nc.sync.dma_start(out=wd_s[r:P:32, N * g : N * (g + 1)].bitcast(I32), in_=scales[0][r:16:4, :].bitcast(I32))
 
-        w_w = [keep.tile([P, HALF], I32, name=f"w_w{g}", align_bytes=64) for g in range(2)]
+        nb_w = {}
+        for u in range(2):
+            for a in range(2):
+                nb_w[a, u] = keep.tile([P, QUARTER], U32, name=f"nb_w{a}{u}", align_bytes=64)
+                first = (J * a + QUARTER * u) // 16
+                nc.vector.tensor_copy(nb_w[a, u][:], tab_w[:].indirect(offsets[:, first : first + QUARTER // 16]))
 
-        def order_words(g, copy, dtype):
+        w_w = [keep.tile([P, HALF], U32, name=f"w_w{g}", align_bytes=64) for g in range(2)]
+
+        def order_words(g, copy):
             copy(
-                w_w[g][:].bitcast(dtype).rearrange("p (t m e) -> p m t e", t=PACK, e=4),
-                w_raw[g][:].bitcast(dtype).rearrange("p (m e t) -> p m t e", t=PACK, e=4),
+                w_w[g][:].rearrange("p (t m e) -> p m t e", t=PACK, e=4),
+                w_raw[g][:].bitcast(U32).rearrange("p (m e t) -> p m t e", t=PACK, e=4),
             )
 
-        def gather_words(dst, a):
-            nc.vector.tensor_copy(dst[:], tab_w[:].indirect(offsets[:, 32 * a : 32 * (a + 1)]))
-
-        nb_w0 = keep.tile([P, J], U32, name="nb_w0", align_bytes=64)
-        gather_words(nb_w0, 0)
-        order_words(0, nc.scalar.copy, U32)
-        nb_w1 = keep.tile([P, J], U32, name="nb_w1", align_bytes=64)
-        gather_words(nb_w1, 1)
-        order_words(1, nc.vector.tensor_copy, I32)
-        nb_w = [nb_w0, nb_w1]
-
-        def neighbour_passes(bank, a, g, b, closed):
+        def neighbour_passes(sums, a, gb, closed):
+            g, b = gb
+            u, v = divmod(b, 2)
             for t in range(PACK):
                 nc.tensor.matmul_mx(
-                    out=bank[:, t, :],
+                    out=sums[:, t, :],
                     lhsT=w_w[g][:, P * t : P * (t + 1)].bitcast(FP8X4),
                     lhsT_scale=w_s[4 * g : P, P * t : P * (t + 1)],
-                    rhs=nb_w[a][:, JB * b : JB * (b + 1)].bitcast(FP8X4),
-                    rhs_scale=nb_s[NB_PLANE:P, J * a + JB * b : J * a + JB * (b + 1)],
+                    rhs=nb_w[a, u][:, JB * v : JB * (v + 1)].bitcast(FP8X4),
+                    rhs_scale=nb_s[PLANE:P, J * a + JB * b : J * a + JB * (b + 1)],
                     start=closed or t == 0,
                     stop=closed,
                 )
 
-        def by_point(bank):
-            return bank[:].rearrange("p t j -> p j t")
+        def by_point(sums):
+            return sums[:].rearrange("p t j -> p j t")
 
-        order = [(0, 0), (0, 1), (1, 0), (1, 1), (0, 2), (0, 3), (1, 2), (1, 3)]
-        plain = [gb for gb in order if gb not in FUSED]
-        firsts = {}
-        pooled = {}
-
-        def first_neighbour(gb):
-            a0 = psum.tile([P, PACK, JB], F32, tag=("a0", "ac")[plain.index(gb) // 2 % 2], name="a0")
-            neighbour_passes(a0, 0, gb[0], gb[1], True)
-            firsts[gb] = copies[:, plain.index(gb), :, :]
-            nc.scalar.copy(firsts[gb], by_point(a0))
-
-        seconds = {}
-        sums = {}
-
-        def pool_neighbours(gb, tile):
-            pooled[gb] = tile
-            nc.vector.tensor_tensor(tile[:], by_point(seconds[gb]), firsts[gb], ALU.max)
-
-        def second_neighbour(gb):
-            a1 = psum.tile([P, PACK, JB], F32, tag=("y", "a1")[plain.index(gb) // 2 % 2], name="a1")
-            neighbour_passes(a1, 1, gb[0], gb[1], True)
-            seconds[gb] = a1
-            if gb not in plain[-2:]:
-                pool_neighbours(gb, keep.tile([P, JB, PACK], F32, name=f"pooled{gb[0]}{gb[1]}"))
-
-        c_bf = [stage.tile([P, J // 2, PACK], BF16, name="c_bf0", align_bytes=64, offset=8064)]
-        c_w = [keep.tile([P, J // 2], U32, name=f"c_w{u}", align_bytes=64) for u in range(2)]
-        c_s = [keep.tile([P, J // 2], U8, name=f"c_s{u}", align_bytes=64) for u in range(2)]
-        wc_bf = []
+        BF_AT = 32768
+        late_bf = keep.tile([P, 1536 + WC_CUT + 1024], BF16, name="late_bf", align_bytes=64)
+        c_bf = [staged("c_bf0", [P, QUARTER, PACK], BF16, BF_AT), late_bf[:, 1536 + WC_CUT :].rearrange("p (j i) -> p j i", i=PACK)]
+        c_w = [keep.tile([P, QUARTER], U32, name=f"c_w{u}", align_bytes=64) for u in range(2)]
+        c_s = [keep.tile([P, QUARTER], U8, name=f"c_s{u}", align_bytes=64) for u in range(2)]
+        wc_bf = {}
         wc_w = [keep.tile([P, HALF], U32, name=f"wc_w{g}", align_bytes=64) for g in range(2)]
         wc_s = [keep.tile([P, HALF], U8, name=f"wc_s{g}", align_bytes=64) for g in range(2)]
 
-        def round_c(u):
-            nc.scalar.copy(c_bf[u][:].rearrange("p (a j) i -> p a i j", j=PACK), c_raw[u].rearrange("p i (a j) -> p a i j", j=PACK))
-
-        def round_wc(g, raw, first, engine):
-            dst = wc_bf[g][:, :, first // PACK : (first + raw.shape[2]) // PACK, :].rearrange("p t m i -> p m t i")
-            src = raw.rearrange("p i (m t) -> p m t i", t=PACK)
+        def round_with(engine, dst, src):
             if engine == "gpsimd":
                 nc.gpsimd.tensor_scalar(dst, src, 1.0, 0.0, ALU.mult, ALU.add)
             else:
                 nc.scalar.copy(dst, src)
 
+        def round_c(u, engine):
+            round_with(
+                engine,
+                c_bf[u][:].rearrange("p (a j) i -> p a i j", j=PACK),
+                c_raw[u][:].rearrange("p i (a j) -> p a i j", j=PACK),
+            )
+
+        def round_wc(v, lo, hi, engine):
+            g, first = divmod(QUARTER * v, HALF)
+            dst = wc_bf[g][:, :, (first + lo) // PACK : (first + hi) // PACK, :].rearrange("p t m i -> p m t i")
+            round_with(engine, dst, wc_raw[v][:, :, lo:hi].rearrange("p i (m t) -> p m t i", t=PACK))
+
+        def quantize(words, scales, values):
+            nc.vector.quantize_mx(out=words[:].bitcast(FP8X4), scales=scales[:], in_=values)
+
         def quantize_c(u):
-            nc.vector.quantize_mx(out=c_w[u][:].bitcast(FP8X4), scales=c_s[u][:], in_=c_bf[u][:].rearrange("p j i -> p (j i)"))
+            quantize(c_w[u], c_s[u], c_bf[u][:].rearrange("p j i -> p (j i)"))
 
         def quantize_wc(g):
-            nc.vector.quantize_mx(out=wc_w[g][:].bitcast(FP8X4), scales=wc_s[g][:], in_=wc_bf[g][:].rearrange("p t m i -> p (t m i)"))
+            for lo in (0, 2):
+                cols = slice(P * lo, P * (lo + 2))
+                quantize(wc_w[g][:, cols], wc_s[g][:, cols], wc_bf[g][:, lo : lo + 2, :, :].rearrange("p t m i -> p (t m i)"))
 
-        def own_passes(bank, g, b, closed):
+        def own_passes(sums, gb, closed):
+            g, b = gb
             u, v = divmod(b, 2)
             for t in range(PACK):
                 nc.tensor.matmul_mx(
-                    out=bank[:, t, :],
+                    out=sums[:, t, :],
                     lhsT=wc_w[g][:, P * t : P * (t + 1)].bitcast(FP8X4),
                     lhsT_scale=wc_s[g][:, P * t : P * (t + 1)],
                     rhs=c_w[u][:, JB * v : JB * (v + 1)].bitcast(FP8X4),
@@ -194,43 +193,65 @@ def tile_list_pnet_mix_none_kernel(
                     stop=closed or t == PACK - 1,
                 )
 
-        pairs = [order[0:2], order[2:4], order[4:6], order[6:7], order[7:8]]
-        place = {gb: (n, pair.index(gb)) for n, pair in enumerate(pairs) for gb in pair}
-        pre = [keep.tile([P, len(pair), HALF], BF16, name=f"pre{n}") for n, pair in enumerate(pairs[:3])]
-        h_bf = {n: keep.tile([P, len(pair), HALF], BF16, name=f"h_bf{n}", align_bytes=64) for n, pair in enumerate(pairs)}
-        h_w = [keep.tile([P, len(pair) * JB], U32, name=f"h_w{n}", align_bytes=64) for n, pair in enumerate(pairs)]
-        h_s = [keep.tile([P, len(pair) * JB], U8, name=f"h_s{n}", align_bytes=64) for n, pair in enumerate(pairs)]
+        firsts, seconds, pooled = {}, {}, {}
 
-        def add_own(gb):
+        def first_neighbour(n):
+            gb = PLAIN[n]
+            a0 = bank(FIRST_BANK[n], [P, PACK, JB])
+            neighbour_passes(a0, 0, gb, True)
+            firsts[gb] = copies[:, n, :, :]
+            nc.scalar.copy(firsts[gb], by_point(a0))
+
+        def second_neighbour(n):
+            gb = PLAIN[n]
+            seconds[gb] = bank(SECOND_BANK[n], [P, PACK, JB])
+            neighbour_passes(seconds[gb], 1, gb, True)
+
+        def pool_neighbours(gb, tile):
+            pooled[gb] = tile
+            nc.vector.tensor_tensor(tile[:], by_point(seconds[gb]), firsts[gb], ALU.max)
+
+        groups = [PLAIN[0:2], PLAIN[4:6], PLAIN[2:4], FUSED[0:1], FUSED[1:2]]
+        place = {gb: (n, group.index(gb)) for n, group in enumerate(groups) for gb in group}
+        pre = {n: keep.tile([P, 2, HALF], BF16, name=f"pre{n}") for n in (1, 2)}
+        h_bf = [keep.tile([P, len(group), HALF], BF16, name=f"h_bf{n}", align_bytes=64) for n, group in enumerate(groups)]
+        h_w = [keep.tile([P, len(group) * JB], U32, name=f"h_w{n}", align_bytes=64) for n, group in enumerate(groups)]
+        h_s = [keep.tile([P, len(group) * JB], U8, name=f"h_s{n}", align_bytes=64) for n, group in enumerate(groups)]
+
+        def add_own(gb, at):
             n, e = place[gb]
-            ac = psum.tile([P, PACK, JB], F32, tag=("a0", "a1", "ac")[n], name="ac")
-            own_passes(ac, gb[0], gb[1], True)
+            ac = bank(at, [P, PACK, JB])
+            own_passes(ac, gb, True)
             nc.vector.tensor_tensor(pre[n][:, e, :].rearrange("p (j t) -> p j t", t=PACK), by_point(ac), pooled[gb][:], ALU.add)
-
-        def close_first(gb):
-            s0 = sums[gb][0]
-            own_passes(s0, gb[0], gb[1], False)
-            firsts[gb] = keep.tile([P, JB, PACK], F32, name=f"first{gb[0]}{gb[1]}")
-            nc.scalar.copy(firsts[gb][:], by_point(s0))
-
-        def close_second(gb):
-            n, e = place[gb]
-            s1 = sums[gb][1]
-            own_passes(s1, gb[0], gb[1], False)
-            nc.vector.scalar_tensor_tensor(
-                h_bf[n][:, e, :].rearrange("p (j t) -> p j t", t=PACK), by_point(s1), 0.0, firsts[gb][:], ALU.max, ALU.max
-            )
 
         def relu_on_scalar(gb):
             n, e = place[gb]
             nc.scalar.activation(h_bf[n][:, e, :], pre[n][:, e, :], RELU)
 
         def quantize_h(n):
-            nc.vector.quantize_mx(out=h_w[n][:].bitcast(FP8X4), scales=h_s[n][:], in_=h_bf[n][:].rearrange("p e x -> p (e x)"))
+            quantize(h_w[n], h_s[n], h_bf[n][:].rearrange("p e x -> p (e x)"))
+
+        fused_sums = {}
+
+        def open_fused(gb, a, at):
+            fused_sums[gb, a] = bank(at, [P, PACK, JB])
+            neighbour_passes(fused_sums[gb, a], a, gb, False)
+
+        def close_first(gb):
+            own_passes(fused_sums[gb, 0], gb, False)
+            firsts[gb] = keep.tile([P, JB, PACK], F32, name=f"first{gb[0]}{gb[1]}")
+            nc.scalar.copy(firsts[gb][:], by_point(fused_sums[gb, 0]))
+
+        def close_second(gb):
+            n, e = place[gb]
+            own_passes(fused_sums[gb, 1], gb, False)
+            nc.vector.scalar_tensor_tensor(
+                h_bf[n][:, e, :].rearrange("p (j t) -> p j t", t=PACK), by_point(fused_sums[gb, 1]), 0.0, firsts[gb][:], ALU.max, ALU.max
+            )
 
         out_rows = out.rearrange("(x p) j -> p x j", p=P)
 
-        def second_passes(y, x, g, b, start, stop):
+        def second_pass(y, x, g, b, start, stop):
             n, e = place[(g, b)]
             if g == 0:
                 lhsT = wd8_w[:, P * x : P * (x + 1)].bitcast(FP8X4)
@@ -246,95 +267,81 @@ def tile_list_pnet_mix_none_kernel(
                 stop=stop,
             )
 
-        def second_layer(b):
-            y = psum.tile([P, 2, JB], F32, tag="ac" if b < 2 else "a1", name="y")
+        def second_layer(b, at):
+            y = bank(at, [P, 2, JB])
             for g in range(2):
                 for x in range(2):
-                    second_passes(y[:, x, :], x, g, b, g == 0 and x == 0, g == 1 and x == 1)
+                    second_pass(y[:, x, :], x, g, b, g == 0 and x == 0, g == 1 and x == 1)
             res = keep.tile([P, 2, JB], F32, name=f"res{b}")
             nc.scalar.copy(res[:], y[:])
             nc.sync.dma_start(out=out_rows[:, :, JB * b : JB * (b + 1)], in_=res[:])
 
         last_y = []
 
-        def open_last(b):
+        def open_last(b, at):
             for x in range(2):
-                last_y.append(psum.tile([P, JB], F32, tag="a0", name="last_y"))
-                second_passes(last_y[x][:], x, 0, b, True, False)
+                last_y.append(bank(at[x], [P, JB]))
+                second_pass(last_y[x][:], x, 0, b, True, False)
 
         def close_last(b):
             for x in range(2):
-                second_passes(last_y[x][:], x, 1, b, False, True)
+                second_pass(last_y[x][:], x, 1, b, False, True)
             res = [keep.tile([P, JB], F32, name=f"last_res{x}") for x in range(2)]
             nc.scalar.copy(res[0][:], last_y[0][:])
             nc.sync.dma_start(out=out_rows[:, 0, JB * b : JB * (b + 1)], in_=res[0][:])
             nc.vector.tensor_copy(res[1][:], last_y[1][:])
             nc.scalar.dma_start(out=out_rows[:, 1, JB * b : JB * (b + 1)], in_=res[1][:])
 
-        round_c(0)
+        order_words(0, nc.scalar.copy)
+        order_words(1, nc.vector.tensor_copy)
+        round_c(0, "scalar")
         quantize_c(0)
-        copies = keep.tile([P, len(plain), JB, PACK], F32, name="copies", tag="c_raw0", align_bytes=64)
-        late_bf = keep.tile([P, 1536 + WC_CUT + 1024], BF16, name="late_bf", align_bytes=64)
-        c_bf.append(late_bf[:, 1536 + WC_CUT :].rearrange("p (j i) -> p j i", i=PACK))
-        for s in range(len(plain)):
-            if s == len(plain) - 2:
-                round_c(1)
-            first_neighbour(plain[s])
-            if s >= 1:
-                second_neighbour(plain[s - 1])
-        second_neighbour(plain[-1])
-
-        wd8_w = stage.tile([P, N], U32, name="wd8_w", align_bytes=64, offset=22464)
-        wd4_w = stage.tile([P, 2 * N], U8, name="wd4_w", align_bytes=64, offset=23488)
-        wd_s = stage.tile([P, 2 * N], U8, name="wd_s", align_bytes=64, offset=24000)
-        nc.sync.dma_start(out=wd8_w[:].bitcast(I32), in_=wd8_words[0].rearrange("p n i -> p (n i)").bitcast(I32))
-        nc.sync.dma_start(out=wd4_w[:].bitcast(I32), in_=wd4_words[0].bitcast(I32))
-        load_scale_rows(nc.sync, wd_s[:, 0:N], wd8_scales[0])
-        load_scale_rows(nc.sync, wd_s[:, N : 2 * N], wd4_scales[0])
-        wc_bf.append(stage.tile([P, PACK, P, PACK], BF16, name="wc_bf0", align_bytes=64, offset=4032))
-        round_wc(0, wc_raw[0], 0, "gpsimd")
-        round_wc(0, wc_raw[1], 256, "gpsimd")
+        copies = staged("copies", [P, len(PLAIN), JB, PACK], F32, 49152 + 4096)
+        for n in range(len(PLAIN) + 1):
+            if n < len(PLAIN):
+                first_neighbour(n)
+            if n >= 1:
+                second_neighbour(n - 1)
+                if n < len(PLAIN):
+                    pool_neighbours(PLAIN[n - 1], keep.tile([P, JB, PACK], F32, name=f"pooled{n}"))
+        round_c(1, "scalar")
+        wc_bf[0] = staged("wc_bf0", [P, PACK, P, PACK], BF16, BF_AT + 1984)
+        round_wc(0, 0, QUARTER, "gpsimd")
+        round_wc(1, 0, QUARTER, "gpsimd")
         quantize_wc(0)
-
-        def late_maximum(n):
-            pool_neighbours(plain[-2 + n], stage.tile([P, JB, PACK], F32, name=f"pooled_late{n}", align_bytes=64, offset=wc_at[0][1] + 2048 * n))
-
+        pool_neighbours(PLAIN[-1], staged("pooled_late", [P, JB, PACK], F32, 8192 + 4096))
         quantize_c(1)
-        late_maximum(0)
-        late_maximum(1)
-        wc_bf.append(late_bf[:, 0:2048].rearrange("p (t m i) -> p t m i", t=PACK, i=PACK))
-        round_wc(1, wc_late[0][:], 0, "scalar")
-        round_wc(1, wc_late[1][:, :, 0 : WC_CUT - 256], 256, "scalar")
-        round_wc(1, wc_late[1][:, :, WC_CUT - 256 : 256], WC_CUT, "gpsimd")
-        add_own(order[0])
-        add_own(order[1])
-        add_own(order[4])
+        pre[0] = staged("pre0", [P, 2, HALF], BF16, 4096)
+        add_own((0, 0), 0)
+        wc_bf[1] = late_bf[:, 0:2048].rearrange("p (t m i) -> p t m i", t=PACK, i=PACK)
+        round_wc(2, 0, QUARTER, "scalar")
+        round_wc(3, 0, WC_CUT - QUARTER, "scalar")
+        round_wc(3, WC_CUT - QUARTER, QUARTER, "gpsimd")
+        add_own((0, 1), 1)
+        add_own((0, 2), 4)
         quantize_wc(1)
-        add_own(order[5])
-        for gb in FUSED:
-            s0 = psum.tile([P, PACK, JB], F32, tag="a0", name="s0")
-            s1 = psum.tile([P, PACK, JB], F32, tag="y", name="s1")
-            neighbour_passes(s0, 0, gb[0], gb[1], False)
-            neighbour_passes(s1, 1, gb[0], gb[1], False)
-            sums[gb] = (s0, s1)
-
-        for gb in order[0:2] + order[4:6]:
-            relu_on_scalar(gb)
+        add_own((0, 3), 5)
+        open_fused(FUSED[0], 0, 0)
+        open_fused(FUSED[0], 1, 2)
+        open_fused(FUSED[1], 0, 1)
+        open_fused(FUSED[1], 1, 4)
+        for b in range(4):
+            relu_on_scalar((0, b))
         quantize_h(0)
-        add_own(order[2])
-        add_own(order[3])
-        close_first(order[6])
-        relu_on_scalar(order[2])
-        close_first(order[7])
-        quantize_h(2)
-        nc.vector.tensor_scalar_max(h_bf[1][:, 1, :], pre[1][:, 1, :], 0.0)
-        close_second(order[6])
+        add_own((1, 0), 6)
+        add_own((1, 1), 7)
+        close_first(FUSED[0])
+        relu_on_scalar((1, 0))
+        close_first(FUSED[1])
         quantize_h(1)
-        second_layer(0)
-        second_layer(1)
-        close_second(order[7])
+        nc.vector.tensor_scalar_max(h_bf[2][:, 1, :], pre[2][:, 1, :], 0.0)
+        close_second(FUSED[0])
+        quantize_h(2)
+        second_layer(0, 3)
+        second_layer(1, 5)
+        close_second(FUSED[1])
         quantize_h(3)
-        second_layer(2)
-        open_last(3)
+        second_layer(2, 6)
+        open_last(3, (0, 1))
         quantize_h(4)
         close_last(3)

@@ -339,9 +339,9 @@ def tile_list_pnet_mix_none_kernel(
         quantize_h(2)
         second_layer(0, 3)
         second_layer(1, 5)
-        close_second(FUSED[1])
         quantize_h(3)
         second_layer(2, 6)
+        close_second(FUSED[1])
         open_last(3, (0, 1))
         quantize_h(4)
         close_last(3)

@@ -304,6 +304,7 @@ def tile_list_pnet_mix_none_kernel(
                 second_neighbour(n - 1)
                 if n < len(PLAIN):
                     pool_neighbours(PLAIN[n - 1], keep.tile([P, JB, PACK], F32, name=f"pooled{n}"))
+        open_fused(FUSED[1], 0, 7)
         round_c(1, "scalar")
         wc_bf[0] = staged("wc_bf0", [P, PACK, P, PACK], BF16, BF_AT + 1984)
         round_wc(0, 0, QUARTER, "gpsimd")
@@ -323,13 +324,12 @@ def tile_list_pnet_mix_none_kernel(
         add_own((0, 3), 5)
         open_fused(FUSED[0], 0, 0)
         open_fused(FUSED[0], 1, 2)
-        open_fused(FUSED[1], 0, 1)
         open_fused(FUSED[1], 1, 4)
         for b in range(4):
             relu_on_scalar((0, b))
         quantize_h(0)
         add_own((1, 0), 6)
-        add_own((1, 1), 7)
+        add_own((1, 1), 1)
         close_first(FUSED[0])
         relu_on_scalar((1, 0))
         close_first(FUSED[1])
@@ -342,6 +342,6 @@ def tile_list_pnet_mix_none_kernel(
         quantize_h(3)
         second_layer(2, 6)
         close_second(FUSED[1])
-        open_last(3, (0, 1))
+        open_last(3, (0, 7))
         quantize_h(4)
         close_last(3)

@@ -24,10 +24,9 @@ QUARTER = 256
 TAB_CUT = 1792
 SCALE_ROWS = 48
 PLANE = 12
-WC_CUT = 352
-PLAIN = ((0, 0), (0, 1), (1, 0), (1, 1), (0, 2), (0, 3))
-FIRST_BANK = (0, 1, 4, 5, 0, 1)
-SECOND_BANK = (2, 3, 6, 7, 2, 3)
+SHARE = 128
+BF16_MAX = 3.3895313892515355e38
+PLAIN = ((0, 0), (0, 1), (0, 2), (1, 0), (1, 1), (0, 3))
 FUSED = ((1, 2), (1, 3))
 
 
@@ -49,7 +48,7 @@ def tile_list_pnet_mix_none_kernel(
         offsets = keep.tile([P, 2 * J // 16], U16, name="offsets")
         tab_w = keep.tile([P, T], U32, name="tab_w", align_bytes=64)
         tab_s = staged("tab_s", [P, T], U8, 49152)
-        ws_raw = staged("ws_raw", [P, 28672], U8, 0)[:, 0:HALF]
+        ws_raw = staged("ws_raw", [P, 30720], U8, 0)[:, 0:R]
         nc.vector.memset(ws_raw.bitcast(I32), 0)
         nc.vector.memset(tab_s[0:SCALE_ROWS, :].bitcast(I32), 0)
         nc.gpsimd.memset(tab_s[SCALE_ROWS + 16 : P, :].bitcast(I32), 0)
@@ -60,14 +59,13 @@ def tile_list_pnet_mix_none_kernel(
         c_rows = c.rearrange("(p i) j -> p i j", i=PACK)
 
         w_raw = [keep.tile([P, HALF], I32, name="w_raw0", align_bytes=64)]
-        ws_rows = w_scales[0].bitcast(I32).rearrange("q (g r) -> g q r", g=2)
         nc.sync.dma_start(out=tab_s[SCALE_ROWS : SCALE_ROWS + 16, :].bitcast(I32), in_=tab_scales[0].bitcast(I32))
         nc.sync.dma_start(offsets[:], offs)
         nc.sync.dma_start(out=tab_w[:, 0:TAB_CUT].bitcast(I32), in_=tab_rows[:, 0:TAB_CUT])
         for q in range(4):
-            nc.sync.dma_start(out=ws_raw[32 * q : 32 * q + 8, :].bitcast(I32), in_=ws_rows[:, 4 * q : 4 * q + 4, :])
-        nc.sync.dma_start(out=w_raw[0][:], in_=w_rows[:, 0:HALF])
+            nc.sync.dma_start(out=ws_raw[32 * q : 32 * q + 4, :].bitcast(I32), in_=w_scales[0][4 * q : 4 * q + 4, :].bitcast(I32))
         nc.sync.dma_start(out=tab_w[:, TAB_CUT:T].bitcast(I32), in_=tab_rows[:, TAB_CUT:T])
+        nc.sync.dma_start(out=w_raw[0][:], in_=w_rows[:, 0:HALF])
 
         picked = keep.tile([P, 2 * J], U8, name="picked", align_bytes=64)
         nb_s = keep.tile([P, 2 * J], U8, name="nb_s", align_bytes=64)
@@ -77,18 +75,18 @@ def tile_list_pnet_mix_none_kernel(
                 out=nb_s[32 * q + PLANE : 32 * q + PLANE + 4, :].bitcast(I32),
                 in_=picked[SCALE_ROWS + 4 * q : SCALE_ROWS + 4 * q + 4, :].bitcast(I32),
             )
-        w_s = staged("w_s", [P, HALF], U8, 49152)
+        w_s = staged("w_s", [P, R], U8, 49152)
         nc.vector.tensor_copy(
-            w_s[:].rearrange("p (t m e) -> p m t e", t=PACK, e=16),
-            ws_raw.rearrange("p (m e t) -> p m t e", t=PACK, e=16),
+            w_s[:].rearrange("p (g t m e) -> p g m t e", g=2, t=PACK, e=16),
+            ws_raw.rearrange("p (g m e t) -> p g m t e", g=2, t=PACK, e=16),
         )
 
-        c_raw = [staged("c_raw0", [P, PACK, QUARTER], F32, 49152 + 4032), staged("c_raw1", [P, PACK, QUARTER], F32, 4096)]
-        w_raw.append(staged("w_raw1", [P, HALF], I32, 24576))
+        c_raw = [staged("c_raw0", [P, PACK, QUARTER], F32, 24576), staged("c_raw1", [P, PACK, QUARTER], F32, 4096)]
+        w_raw.append(staged("w_raw1", [P, HALF], I32, 49152 + 4032))
         wc_raw = [staged(f"wc_raw{v}", [P, PACK, QUARTER], F32, 8192 + 4096 * v) for v in range(4)]
-        wd8_w = staged("wd8_w", [P, N], U32, 26624)
-        wd4_w = staged("wd4_w", [P, 2 * N], U8, 27648)
-        wd_s = staged("wd_s", [P, 2 * N], U8, 28160)
+        wd8_w = staged("wd8_w", [P, N], U32, 28672)
+        wd4_w = staged("wd4_w", [P, 2 * N], U8, 29696)
+        wd_s = staged("wd_s", [P, 2 * N], U8, 30208)
 
         def load_c(u):
             nc.sync.dma_start(out=c_raw[u][:], in_=c_rows[:, :, QUARTER * u : QUARTER * (u + 1)])
@@ -96,8 +94,8 @@ def tile_list_pnet_mix_none_kernel(
         def load_wc(v):
             nc.sync.dma_start(out=wc_raw[v][:], in_=wc_rows[:, :, QUARTER * v : QUARTER * (v + 1)])
 
-        load_c(0)
         nc.sync.dma_start(out=w_raw[1][:], in_=w_rows[:, HALF:R])
+        load_c(0)
         load_wc(0)
         load_wc(1)
         load_c(1)
@@ -116,12 +114,13 @@ def tile_list_pnet_mix_none_kernel(
                 first = (J * a + QUARTER * u) // 16
                 nc.vector.tensor_copy(nb_w[a, u][:], tab_w[:].indirect(offsets[:, first : first + QUARTER // 16]))
 
-        w_w = [keep.tile([P, HALF], U32, name=f"w_w{g}", align_bytes=64) for g in range(2)]
+        CODES_AT = 36864
+        w_w = [staged("w_w0", [P, HALF], U32, CODES_AT), keep.tile([P, HALF], U32, name="w_w1", align_bytes=64)]
 
-        def order_words(g, copy):
-            copy(
-                w_w[g][:].rearrange("p (t m e) -> p m t e", t=PACK, e=4),
-                w_raw[g][:].bitcast(U32).rearrange("p (m e t) -> p m t e", t=PACK, e=4),
+        def order_words(g, lo, hi):
+            nc.scalar.copy(
+                w_w[g][:].rearrange("p (t m e) -> p m t e", t=PACK, e=4)[:, :, lo:hi, :],
+                w_raw[g][:].bitcast(U32).rearrange("p (m e t) -> p m t e", t=PACK, e=4)[:, :, lo:hi, :],
             )
 
         def neighbour_passes(sums, a, gb, closed):
@@ -131,7 +130,7 @@ def tile_list_pnet_mix_none_kernel(
                 nc.tensor.matmul_mx(
                     out=sums[:, t, :],
                     lhsT=w_w[g][:, P * t : P * (t + 1)].bitcast(FP8X4),
-                    lhsT_scale=w_s[4 * g : P, P * t : P * (t + 1)],
+                    lhsT_scale=w_s[:, HALF * g + P * t : HALF * g + P * (t + 1)],
                     rhs=nb_w[a, u][:, JB * v : JB * (v + 1)].bitcast(FP8X4),
                     rhs_scale=nb_s[PLANE:P, J * a + JB * b : J * a + JB * (b + 1)],
                     start=closed or t == 0,
@@ -141,38 +140,42 @@ def tile_list_pnet_mix_none_kernel(
         def by_point(sums):
             return sums[:].rearrange("p t j -> p j t")
 
-        BF_AT = 32768
-        late_bf = keep.tile([P, 1536 + WC_CUT + 1024], BF16, name="late_bf", align_bytes=64)
-        c_bf = [staged("c_bf0", [P, QUARTER, PACK], BF16, BF_AT), late_bf[:, 1536 + WC_CUT :].rearrange("p (j i) -> p j i", i=PACK)]
+        def as_points(flat):
+            return flat.rearrange("p (j t) -> p j t", t=PACK)
+
+        early = keep.tile([P, 5376], BF16, name="early", align_bytes=64)
+        late = early[:, 2944:5376]
+        CHAIN_AT = CODES_AT + 1024
+        firsts = {gb: keep.tile([P, HALF], F32, name=f"first{gb[0]}{gb[1]}")[:] for gb in PLAIN + FUSED}
+        c_bf = [early[:, 0:1024]]
         c_w = [keep.tile([P, QUARTER], U32, name=f"c_w{u}", align_bytes=64) for u in range(2)]
         c_s = [keep.tile([P, QUARTER], U8, name=f"c_s{u}", align_bytes=64) for u in range(2)]
-        wc_bf = {}
-        wc_w = [keep.tile([P, HALF], U32, name=f"wc_w{g}", align_bytes=64) for g in range(2)]
+        wc_bf = [
+            early[:, 960:3008].rearrange("p (t m i) -> p t m i", t=PACK, i=PACK),
+            late[:, 0:2048].rearrange("p (t m i) -> p t m i", t=PACK, i=PACK),
+        ]
+        wc_w = {1: keep.tile([P, HALF], U32, name="wc_w1", align_bytes=64)}
         wc_s = [keep.tile([P, HALF], U8, name=f"wc_s{g}", align_bytes=64) for g in range(2)]
 
-        def round_with(engine, dst, src):
-            if engine == "gpsimd":
-                nc.gpsimd.tensor_scalar(dst, src, 1.0, 0.0, ALU.mult, ALU.add)
-            else:
-                nc.scalar.copy(dst, src)
+        def round_on_gpsimd(dst, src):
+            nc.gpsimd.tensor_scalar(dst, src, 1.0, 0.0, ALU.mult, ALU.add)
 
-        def round_c(u, engine):
-            round_with(
-                engine,
-                c_bf[u][:].rearrange("p (a j) i -> p a i j", j=PACK),
-                c_raw[u][:].rearrange("p i (a j) -> p a i j", j=PACK),
+        def round_c(u, lo, hi, copy):
+            copy(
+                c_bf[u][:, PACK * lo : PACK * hi].rearrange("p (a j i) -> p a i j", j=PACK, i=PACK),
+                c_raw[u][:, :, lo:hi].rearrange("p i (a j) -> p a i j", j=PACK),
             )
 
-        def round_wc(v, lo, hi, engine):
+        def round_wc(v, lo, hi, copy):
             g, first = divmod(QUARTER * v, HALF)
             dst = wc_bf[g][:, :, (first + lo) // PACK : (first + hi) // PACK, :].rearrange("p t m i -> p m t i")
-            round_with(engine, dst, wc_raw[v][:, :, lo:hi].rearrange("p i (m t) -> p m t i", t=PACK))
+            copy(dst, wc_raw[v][:, :, lo:hi].rearrange("p i (m t) -> p m t i", t=PACK))
 
         def quantize(words, scales, values):
-            nc.vector.quantize_mx(out=words[:].bitcast(FP8X4), scales=scales[:], in_=values)
+            nc.vector.quantize_mx(out=words.bitcast(FP8X4), scales=scales, in_=values)
 
-        def quantize_c(u):
-            quantize(c_w[u], c_s[u], c_bf[u][:].rearrange("p j i -> p (j i)"))
+        def quantize_c(u, lo, hi):
+            quantize(c_w[u][:, lo:hi], c_s[u][:, lo:hi], c_bf[u][:, PACK * lo : PACK * hi])
 
         def quantize_wc(g):
             for lo in (0, 2):
@@ -193,43 +196,47 @@ def tile_list_pnet_mix_none_kernel(
                     stop=closed or t == PACK - 1,
                 )
 
-        firsts, seconds, pooled = {}, {}, {}
+        seconds, pooled = {}, {}
 
         def first_neighbour(n):
             gb = PLAIN[n]
-            a0 = bank(FIRST_BANK[n], [P, PACK, JB])
+            a0 = bank(n % 2, [P, PACK, JB])
             neighbour_passes(a0, 0, gb, True)
-            firsts[gb] = copies[:, n, :, :]
-            nc.scalar.copy(firsts[gb], by_point(a0))
+            nc.scalar.copy(as_points(firsts[gb]), by_point(a0))
 
         def second_neighbour(n):
             gb = PLAIN[n]
-            seconds[gb] = bank(SECOND_BANK[n], [P, PACK, JB])
+            seconds[gb] = bank(2 + n, [P, PACK, JB])
             neighbour_passes(seconds[gb], 1, gb, True)
 
         def pool_neighbours(gb, tile):
             pooled[gb] = tile
-            nc.vector.tensor_tensor(tile[:], by_point(seconds[gb]), firsts[gb], ALU.max)
+            nc.vector.tensor_tensor(tile[:], by_point(seconds[gb]), as_points(firsts[gb]), ALU.max)
 
-        groups = [PLAIN[0:2], PLAIN[4:6], PLAIN[2:4], FUSED[0:1], FUSED[1:2]]
+        groups = [[(0, 0)], [(0, 2), (0, 3)], [(1, 0), (1, 1)], [(1, 2)], [(1, 3)], [(0, 1)]]
         place = {gb: (n, group.index(gb)) for n, group in enumerate(groups) for gb in group}
-        pre = {n: keep.tile([P, 2, HALF], BF16, name=f"pre{n}") for n in (1, 2)}
-        h_bf = [keep.tile([P, len(group), HALF], BF16, name=f"h_bf{n}", align_bytes=64) for n, group in enumerate(groups)]
+        pre = {gb: keep.tile([P, HALF], BF16, name=f"pre{gb[0]}{gb[1]}")[:] for gb in PLAIN[1:6]}
+        pre[0, 0] = late[:, 1920:2432]
+        h_bf = {n: keep.tile([P, 1, HALF], BF16, name=f"h_bf{n}", align_bytes=64) for n in (3, 4)}
         h_w = [keep.tile([P, len(group) * JB], U32, name=f"h_w{n}", align_bytes=64) for n, group in enumerate(groups)]
         h_s = [keep.tile([P, len(group) * JB], U8, name=f"h_s{n}", align_bytes=64) for n, group in enumerate(groups)]
 
         def add_own(gb, at):
-            n, e = place[gb]
             ac = bank(at, [P, PACK, JB])
             own_passes(ac, gb, True)
-            nc.vector.tensor_tensor(pre[n][:, e, :].rearrange("p (j t) -> p j t", t=PACK), by_point(ac), pooled[gb][:], ALU.add)
+            nc.vector.tensor_tensor(as_points(pre[gb]), by_point(ac), pooled[gb][:], ALU.add)
 
-        def relu_on_scalar(gb):
+        def relu(gb, engine):
             n, e = place[gb]
-            nc.scalar.activation(h_bf[n][:, e, :], pre[n][:, e, :], RELU)
+            if engine == "scalar":
+                nc.scalar.activation(h_bf[n][:, e, :], pre[gb], RELU)
+            elif engine == "vector":
+                nc.vector.tensor_scalar_max(h_bf[n][:, e, :], pre[gb], 0.0)
+            else:
+                nc.gpsimd.tensor_scalar(h_bf[n][:, e, :], pre[gb], BF16_MAX, 0.0, ALU.min, ALU.max)
 
         def quantize_h(n):
-            quantize(h_w[n], h_s[n], h_bf[n][:].rearrange("p e x -> p (e x)"))
+            quantize(h_w[n][:], h_s[n][:], h_bf[n][:].rearrange("p e x -> p (e x)"))
 
         fused_sums = {}
 
@@ -239,14 +246,13 @@ def tile_list_pnet_mix_none_kernel(
 
         def close_first(gb):
             own_passes(fused_sums[gb, 0], gb, False)
-            firsts[gb] = keep.tile([P, JB, PACK], F32, name=f"first{gb[0]}{gb[1]}")
-            nc.scalar.copy(firsts[gb][:], by_point(fused_sums[gb, 0]))
+            nc.scalar.copy(as_points(firsts[gb]), by_point(fused_sums[gb, 0]))
 
         def close_second(gb):
             n, e = place[gb]
             own_passes(fused_sums[gb, 1], gb, False)
             nc.vector.scalar_tensor_tensor(
-                h_bf[n][:, e, :].rearrange("p (j t) -> p j t", t=PACK), by_point(fused_sums[gb, 1]), 0.0, firsts[gb][:], ALU.max, ALU.max
+                as_points(h_bf[n][:, e, :]), by_point(fused_sums[gb, 1]), 0.0, as_points(firsts[gb]), ALU.max, ALU.max
             )
 
         out_rows = out.rearrange("(x p) j -> p x j", p=P)
@@ -292,56 +298,64 @@ def tile_list_pnet_mix_none_kernel(
             nc.vector.tensor_copy(res[1][:], last_y[1][:])
             nc.scalar.dma_start(out=out_rows[:, 1, JB * b : JB * (b + 1)], in_=res[1][:])
 
-        order_words(0, nc.scalar.copy)
-        order_words(1, nc.vector.tensor_copy)
-        round_c(0, "scalar")
-        quantize_c(0)
-        copies = staged("copies", [P, len(PLAIN), JB, PACK], F32, 49152 + 4096)
-        for n in range(len(PLAIN) + 1):
-            if n < len(PLAIN):
-                first_neighbour(n)
-            if n >= 1:
-                second_neighbour(n - 1)
-                if n < len(PLAIN):
-                    pool_neighbours(PLAIN[n - 1], keep.tile([P, JB, PACK], F32, name=f"pooled{n}"))
-        open_fused(FUSED[1], 0, 7)
-        round_c(1, "scalar")
-        wc_bf[0] = staged("wc_bf0", [P, PACK, P, PACK], BF16, BF_AT + 1984)
-        round_wc(0, 0, QUARTER, "gpsimd")
-        round_wc(1, 0, QUARTER, "gpsimd")
+        order_words(0, 0, 2)
+        order_words(0, 2, 4)
+        for lo in (0, JB):
+            round_c(0, lo, lo + JB, nc.vector.tensor_copy)
+        for lo in (0, JB):
+            quantize_c(0, lo, lo + JB)
+        order_words(1, 0, 4)
+        for n in range(len(PLAIN)):
+            first_neighbour(n)
+            second_neighbour(n)
+            if n < 2:
+                pool_neighbours(PLAIN[n], staged(f"pooled{n}", [P, JB, PACK], F32, 24576 + 2048 * n))
+            elif n < len(PLAIN) - 1:
+                pool_neighbours(PLAIN[n], keep.tile([P, JB, PACK], F32, name=f"pooled{n}"))
+        open_fused(FUSED[0], 0, 4)
+        round_wc(0, 0, QUARTER, round_on_gpsimd)
+        round_wc(1, 0, QUARTER, round_on_gpsimd)
+        wc_w[0] = staged("wc_w0", [P, HALF], U32, CODES_AT - 1024)
         quantize_wc(0)
         pool_neighbours(PLAIN[-1], staged("pooled_late", [P, JB, PACK], F32, 8192 + 4096))
-        quantize_c(1)
-        pre[0] = staged("pre0", [P, 2, HALF], BF16, 4096)
         add_own((0, 0), 0)
-        wc_bf[1] = late_bf[:, 0:2048].rearrange("p (t m i) -> p t m i", t=PACK, i=PACK)
-        round_wc(2, 0, QUARTER, "scalar")
-        round_wc(3, 0, WC_CUT - QUARTER, "scalar")
-        round_wc(3, WC_CUT - QUARTER, QUARTER, "gpsimd")
+        c_bf.append(staged("c_bf1", [P, PACK * QUARTER], BF16, CHAIN_AT)[:])
+        round_c(1, 0, QUARTER, nc.scalar.copy)
+        quantize_c(1, 0, QUARTER)
         add_own((0, 1), 1)
-        add_own((0, 2), 4)
+        open_fused(FUSED[0], 1, 0)
+        h_bf[0] = staged("h_bf0", [P, 1, HALF], BF16, CHAIN_AT)
+        relu((0, 0), "gpsimd")
+        add_own((0, 2), 2)
+        add_own((0, 3), 3)
+        open_fused(FUSED[1], 0, 1)
+        open_fused(FUSED[1], 1, 2)
+        round_wc(2, 0, QUARTER, nc.scalar.copy)
+        round_wc(3, 0, SHARE, nc.scalar.copy)
+        round_wc(3, SHARE, QUARTER, round_on_gpsimd)
         quantize_wc(1)
-        add_own((0, 3), 5)
-        open_fused(FUSED[0], 0, 0)
-        open_fused(FUSED[0], 1, 2)
-        open_fused(FUSED[1], 1, 4)
-        for b in range(4):
-            relu_on_scalar((0, b))
+        h_bf[1] = staged("h_bf1", [P, 2, HALF], BF16, 8192 + 3 * 4096)
+        h_bf[5] = staged("h_bf5", [P, 1, HALF], BF16, 8192 + 3 * 4096 + 2048)
+        relu((0, 1), "scalar")
+        relu((0, 2), "scalar")
+        relu((0, 3), "vector")
         quantize_h(0)
-        add_own((1, 0), 6)
-        add_own((1, 1), 1)
+        quantize_h(5)
+        add_own((1, 0), 5)
+        add_own((1, 1), 6)
+        h_bf[2] = keep.tile([P, 2, HALF], BF16, name="h_bf2", align_bytes=64)
         close_first(FUSED[0])
-        relu_on_scalar((1, 0))
+        relu((1, 0), "scalar")
         close_first(FUSED[1])
         quantize_h(1)
-        nc.vector.tensor_scalar_max(h_bf[2][:, 1, :], pre[2][:, 1, :], 0.0)
+        relu((1, 1), "vector")
         close_second(FUSED[0])
         quantize_h(2)
-        second_layer(0, 3)
-        second_layer(1, 5)
+        second_layer(0, 7)
+        second_layer(1, 3)
         quantize_h(3)
-        second_layer(2, 6)
+        second_layer(2, 5)
         close_second(FUSED[1])
-        open_last(3, (0, 7))
+        open_last(3, (6, 4))
         quantize_h(4)
         close_last(3)

@@ -24,9 +24,12 @@ QUARTER = 256
 TAB_CUT = 1792
 SCALE_ROWS = 48
 PLANE = 12
-SHARE = 128
-BF16_MAX = 3.3895313892515355e38
-PLAIN = ((0, 0), (0, 1), (0, 2), (1, 0), (1, 1), (0, 3))
+SHARE = 48
+PLAIN = ((0, 0), (0, 1), (0, 2), (0, 3), (1, 0), (1, 1))
+PAIRS = ((0, 0), (1, 0), (0, 1))
+UNITS = tuple((g, u, s) for g, u in PAIRS for s in range(2))
+FIRST_BANK = (0, 1, 7, 0, 1, 7)
+SECOND_BANK = (2, 3, 4, 5, 6, 2)
 FUSED = ((1, 2), (1, 3))
 
 
@@ -81,18 +84,24 @@ def tile_list_pnet_mix_none_kernel(
             ws_raw.rearrange("p (g m e t) -> p g m t e", g=2, t=PACK, e=16),
         )
 
-        c_raw = [staged("c_raw0", [P, PACK, QUARTER], F32, 24576), staged("c_raw1", [P, PACK, QUARTER], F32, 4096)]
+        c_raw = [staged("c_raw0", [P, PACK, QUARTER], F32, 26624), staged("c_raw1", [P, PACK, QUARTER], F32, 1024)]
         w_raw.append(staged("w_raw1", [P, HALF], I32, 49152 + 4032))
-        wc_raw = [staged(f"wc_raw{v}", [P, PACK, QUARTER], F32, 8192 + 4096 * v) for v in range(4)]
-        wd8_w = staged("wd8_w", [P, N], U32, 28672)
-        wd4_w = staged("wd4_w", [P, 2 * N], U8, 29696)
-        wd_s = staged("wd_s", [P, 2 * N], U8, 30208)
+        shared = staged("shared", [P, 3 * HALF], F32, 9216)
+        wc_raw = [
+            staged("wc_raw0", [P, PACK, QUARTER], F32, 5120)[:],
+            shared[:, HALF : 3 * HALF].rearrange("p (i r) -> p i r", i=PACK),
+            staged("wc_raw2", [P, PACK, QUARTER], F32, 16384)[:],
+            staged("wc_raw3", [P, PACK, QUARTER], F32, 20480)[:],
+        ]
+        wd8_w = staged("wd8_w", [P, N], U32, 24576)
+        wd4_w = staged("wd4_w", [P, 2 * N], U8, 25600)
+        wd_s = staged("wd_s", [P, 2 * N], U8, 26112)
 
         def load_c(u):
             nc.sync.dma_start(out=c_raw[u][:], in_=c_rows[:, :, QUARTER * u : QUARTER * (u + 1)])
 
         def load_wc(v):
-            nc.sync.dma_start(out=wc_raw[v][:], in_=wc_rows[:, :, QUARTER * v : QUARTER * (v + 1)])
+            nc.sync.dma_start(out=wc_raw[v], in_=wc_rows[:, :, QUARTER * v : QUARTER * (v + 1)])
 
         nc.sync.dma_start(out=w_raw[1][:], in_=w_rows[:, HALF:R])
         load_c(0)
@@ -114,7 +123,7 @@ def tile_list_pnet_mix_none_kernel(
                 first = (J * a + QUARTER * u) // 16
                 nc.vector.tensor_copy(nb_w[a, u][:], tab_w[:].indirect(offsets[:, first : first + QUARTER // 16]))
 
-        CODES_AT = 36864
+        CODES_AT = 38912
         w_w = [staged("w_w0", [P, HALF], U32, CODES_AT), keep.tile([P, HALF], U32, name="w_w1", align_bytes=64)]
 
         def order_words(g, lo, hi):
@@ -123,7 +132,7 @@ def tile_list_pnet_mix_none_kernel(
                 w_raw[g][:].bitcast(U32).rearrange("p (m e t) -> p m t e", t=PACK, e=4)[:, :, lo:hi, :],
             )
 
-        def neighbour_passes(sums, a, gb, closed):
+        def neighbour_passes(sums, a, gb):
             g, b = gb
             u, v = divmod(b, 2)
             for t in range(PACK):
@@ -133,8 +142,22 @@ def tile_list_pnet_mix_none_kernel(
                     lhsT_scale=w_s[:, HALF * g + P * t : HALF * g + P * (t + 1)],
                     rhs=nb_w[a, u][:, JB * v : JB * (v + 1)].bitcast(FP8X4),
                     rhs_scale=nb_s[PLANE:P, J * a + JB * b : J * a + JB * (b + 1)],
-                    start=closed or t == 0,
-                    stop=closed,
+                    start=t == 0,
+                    stop=False,
+                )
+
+        def unit_passes(sums, a, unit):
+            g, u, s = unit
+            for e in range(2):
+                t = 2 * s + e
+                nc.tensor.matmul_mx(
+                    out=sums[:, e, :],
+                    lhsT=w_w[g][:, P * t : P * (t + 1)].bitcast(FP8X4),
+                    lhsT_scale=w_s[:, HALF * g + P * t : HALF * g + P * (t + 1)],
+                    rhs=nb_w[a, u][:].bitcast(FP8X4),
+                    rhs_scale=nb_s[PLANE:P, J * a + QUARTER * u : J * a + QUARTER * (u + 1)],
+                    start=True,
+                    stop=True,
                 )
 
         def by_point(sums):
@@ -143,16 +166,22 @@ def tile_list_pnet_mix_none_kernel(
         def as_points(flat):
             return flat.rearrange("p (j t) -> p j t", t=PACK)
 
-        early = keep.tile([P, 5376], BF16, name="early", align_bytes=64)
-        late = early[:, 2944:5376]
-        CHAIN_AT = CODES_AT + 1024
-        firsts = {gb: keep.tile([P, HALF], F32, name=f"first{gb[0]}{gb[1]}")[:] for gb in PLAIN + FUSED}
-        c_bf = [early[:, 0:1024]]
+        rounded = keep.tile([P, 3008], BF16, name="rounded", align_bytes=64)
+        late = keep.tile([P, 3904], BF16, name="late", align_bytes=64)
+        firsts = {key: keep.tile([P, HALF], F32, name=f"first{n}")[:] for n, key in enumerate(UNITS[0:3] + UNITS[4:5] + FUSED)}
+        firsts[UNITS[3]] = late[:, 2880:3904].bitcast(F32)
+        firsts[UNITS[5]] = late[:, 0:1024].bitcast(F32)
+        pooled = {
+            PAIRS[0]: staged("pooled00", [P, 2 * HALF], F32, 26624)[:],
+            PAIRS[1]: keep.tile([P, 2 * HALF], F32, name="pooled10")[:],
+            PAIRS[2]: shared[:, 0 : 2 * HALF],
+        }
+        c_bf = [rounded[:, 0:1024], late[:, 2880:3904]]
         c_w = [keep.tile([P, QUARTER], U32, name=f"c_w{u}", align_bytes=64) for u in range(2)]
         c_s = [keep.tile([P, QUARTER], U8, name=f"c_s{u}", align_bytes=64) for u in range(2)]
         wc_bf = [
-            early[:, 960:3008].rearrange("p (t m i) -> p t m i", t=PACK, i=PACK),
-            late[:, 0:2048].rearrange("p (t m i) -> p t m i", t=PACK, i=PACK),
+            rounded[:, 960:3008].rearrange("p (t m i) -> p t m i", t=PACK, i=PACK),
+            late[:, 960:3008].rearrange("p (t m i) -> p t m i", t=PACK, i=PACK),
         ]
         wc_w = {1: keep.tile([P, HALF], U32, name="wc_w1", align_bytes=64)}
         wc_s = [keep.tile([P, HALF], U8, name=f"wc_s{g}", align_bytes=64) for g in range(2)]
@@ -196,53 +225,60 @@ def tile_list_pnet_mix_none_kernel(
                     stop=closed or t == PACK - 1,
                 )
 
-        seconds, pooled = {}, {}
+        seconds = {}
+
+        def as_pairs(flat):
+            return flat.rearrange("p (j e) -> p j e", e=2)
 
         def first_neighbour(n):
-            gb = PLAIN[n]
-            a0 = bank(n % 2, [P, PACK, JB])
-            neighbour_passes(a0, 0, gb, True)
-            nc.scalar.copy(as_points(firsts[gb]), by_point(a0))
+            unit = UNITS[n]
+            a0 = bank(FIRST_BANK[n], [P, 2, QUARTER])
+            unit_passes(a0, 0, unit)
+            nc.scalar.copy(as_pairs(firsts[unit]), by_point(a0))
 
         def second_neighbour(n):
-            gb = PLAIN[n]
-            seconds[gb] = bank(2 + n, [P, PACK, JB])
-            neighbour_passes(seconds[gb], 1, gb, True)
+            unit = UNITS[n]
+            seconds[unit] = bank(SECOND_BANK[n], [P, 2, QUARTER])
+            unit_passes(seconds[unit], 1, unit)
 
-        def pool_neighbours(gb, tile):
-            pooled[gb] = tile
-            nc.vector.tensor_tensor(tile[:], by_point(seconds[gb]), as_points(firsts[gb]), ALU.max)
+        def pool_neighbours(unit):
+            g, u, s = unit
+            nc.vector.tensor_tensor(
+                as_pairs(pooled[g, u][:, HALF * s : HALF * (s + 1)]), by_point(seconds[unit]), as_pairs(firsts[unit]), ALU.max
+            )
 
-        groups = [[(0, 0)], [(0, 2), (0, 3)], [(1, 0), (1, 1)], [(1, 2)], [(1, 3)], [(0, 1)]]
+        groups = [[(0, 0), (0, 1)], [(0, 2), (0, 3)], [(1, 0), (1, 1)], [(1, 2)], [(1, 3)]]
         place = {gb: (n, group.index(gb)) for n, group in enumerate(groups) for gb in group}
-        pre = {gb: keep.tile([P, HALF], BF16, name=f"pre{gb[0]}{gb[1]}")[:] for gb in PLAIN[1:6]}
-        pre[0, 0] = late[:, 1920:2432]
+        pre = {gb: keep.tile([P, HALF], BF16, name=f"pre{gb[0]}{gb[1]}")[:] for gb in ((0, 2), (1, 0), (1, 1))}
         h_bf = {n: keep.tile([P, 1, HALF], BF16, name=f"h_bf{n}", align_bytes=64) for n in (3, 4)}
+        h_bf[2] = keep.tile([P, 2, HALF], BF16, name="h_bf2", align_bytes=64)
         h_w = [keep.tile([P, len(group) * JB], U32, name=f"h_w{n}", align_bytes=64) for n, group in enumerate(groups)]
         h_s = [keep.tile([P, len(group) * JB], U8, name=f"h_s{n}", align_bytes=64) for n, group in enumerate(groups)]
 
         def add_own(gb, at):
             ac = bank(at, [P, PACK, JB])
             own_passes(ac, gb, True)
-            nc.vector.tensor_tensor(as_points(pre[gb]), by_point(ac), pooled[gb][:], ALU.add)
+            g, b = gb
+            u, v = divmod(b, 2)
+            nc.vector.tensor_tensor(
+                pre[gb].rearrange("p (j s e) -> p j s e", s=2, e=2),
+                ac[:].rearrange("p (s e) j -> p j s e", s=2),
+                pooled[g, u].rearrange("p (s j e) -> p j s e", s=2, e=2)[:, JB * v : JB * (v + 1), :, :],
+                ALU.add,
+            )
 
-        def relu(gb, engine):
+        def relu(gb):
             n, e = place[gb]
-            if engine == "scalar":
-                nc.scalar.activation(h_bf[n][:, e, :], pre[gb], RELU)
-            elif engine == "vector":
-                nc.vector.tensor_scalar_max(h_bf[n][:, e, :], pre[gb], 0.0)
-            else:
-                nc.gpsimd.tensor_scalar(h_bf[n][:, e, :], pre[gb], BF16_MAX, 0.0, ALU.min, ALU.max)
+            nc.scalar.activation(h_bf[n][:, e, :], pre[gb], RELU)
 
         def quantize_h(n):
-            quantize(h_w[n][:], h_s[n][:], h_bf[n][:].rearrange("p e x -> p (e x)"))
+            quantize(h_w[n][:], h_s[n][:], h_bf[n][:, :, :].rearrange("p e x -> p (e x)"))
 
         fused_sums = {}
 
         def open_fused(gb, a, at):
             fused_sums[gb, a] = bank(at, [P, PACK, JB])
-            neighbour_passes(fused_sums[gb, a], a, gb, False)
+            neighbour_passes(fused_sums[gb, a], a, gb)
 
         def close_first(gb):
             own_passes(fused_sums[gb, 0], gb, False)
@@ -273,13 +309,17 @@ def tile_list_pnet_mix_none_kernel(
                 stop=stop,
             )
 
+        ys = {}
+
         def second_layer(b, at):
-            y = bank(at, [P, 2, JB])
+            ys[b] = bank(at, [P, 2, JB])
             for g in range(2):
                 for x in range(2):
-                    second_pass(y[:, x, :], x, g, b, g == 0 and x == 0, g == 1 and x == 1)
+                    second_pass(ys[b][:, x, :], x, g, b, g == 0 and x == 0, g == 1 and x == 1)
+
+        def store(b, copy):
             res = keep.tile([P, 2, JB], F32, name=f"res{b}")
-            nc.scalar.copy(res[:], y[:])
+            copy(res[:], ys[b][:])
             nc.sync.dma_start(out=out_rows[:, :, JB * b : JB * (b + 1)], in_=res[:])
 
         last_y = []
@@ -305,57 +345,59 @@ def tile_list_pnet_mix_none_kernel(
         for lo in (0, JB):
             quantize_c(0, lo, lo + JB)
         order_words(1, 0, 4)
-        for n in range(len(PLAIN)):
-            first_neighbour(n)
+        first_neighbour(0)
+        for n in range(len(UNITS)):
+            if n < len(UNITS) - 1:
+                first_neighbour(n + 1)
             second_neighbour(n)
-            if n < 2:
-                pool_neighbours(PLAIN[n], staged(f"pooled{n}", [P, JB, PACK], F32, 24576 + 2048 * n))
-            elif n < len(PLAIN) - 1:
-                pool_neighbours(PLAIN[n], keep.tile([P, JB, PACK], F32, name=f"pooled{n}"))
-        open_fused(FUSED[0], 0, 4)
+            if n < len(UNITS) - 1:
+                pool_neighbours(UNITS[n])
+        open_fused(FUSED[0], 0, 3)
         round_wc(0, 0, QUARTER, round_on_gpsimd)
         round_wc(1, 0, QUARTER, round_on_gpsimd)
-        wc_w[0] = staged("wc_w0", [P, HALF], U32, CODES_AT - 1024)
+        wc_w[0] = staged("wc_w0", [P, HALF], U32, CODES_AT)
         quantize_wc(0)
-        pool_neighbours(PLAIN[-1], staged("pooled_late", [P, JB, PACK], F32, 8192 + 4096))
-        add_own((0, 0), 0)
-        c_bf.append(staged("c_bf1", [P, PACK * QUARTER], BF16, CHAIN_AT)[:])
+        pool_neighbours(UNITS[-1])
         round_c(1, 0, QUARTER, nc.scalar.copy)
         quantize_c(1, 0, QUARTER)
+        pre[0, 0] = staged("pre00", [P, HALF], BF16, 1024)[:]
+        pre[0, 1] = staged("pre01", [P, HALF], BF16, 2048)[:]
+        add_own((0, 0), 0)
         add_own((0, 1), 1)
         open_fused(FUSED[0], 1, 0)
-        h_bf[0] = staged("h_bf0", [P, 1, HALF], BF16, CHAIN_AT)
-        relu((0, 0), "gpsimd")
-        add_own((0, 2), 2)
-        add_own((0, 3), 3)
+        add_own((0, 2), 4)
         open_fused(FUSED[1], 0, 1)
-        open_fused(FUSED[1], 1, 2)
         round_wc(2, 0, QUARTER, nc.scalar.copy)
         round_wc(3, 0, SHARE, nc.scalar.copy)
         round_wc(3, SHARE, QUARTER, round_on_gpsimd)
         quantize_wc(1)
-        h_bf[1] = staged("h_bf1", [P, 2, HALF], BF16, 8192 + 3 * 4096)
-        h_bf[5] = staged("h_bf5", [P, 1, HALF], BF16, 8192 + 3 * 4096 + 2048)
-        relu((0, 1), "scalar")
-        relu((0, 2), "scalar")
-        relu((0, 3), "vector")
+        pre[0, 3] = staged("pre03", [P, HALF], BF16, 20480 - 960)[:]
+        add_own((0, 3), 5)
+        open_fused(FUSED[1], 1, 4)
+        h_bf[0] = staged("h_bf0", [P, 2, HALF], BF16, 16384)
+        h_bf[1] = keep.tile([P, 2, HALF], BF16, name="h_bf1", align_bytes=64)
+        relu((0, 0))
+        relu((0, 1))
+        relu((0, 2))
+        relu((0, 3))
         quantize_h(0)
-        quantize_h(5)
-        add_own((1, 0), 5)
-        add_own((1, 1), 6)
-        h_bf[2] = keep.tile([P, 2, HALF], BF16, name="h_bf2", align_bytes=64)
+        add_own((1, 0), 6)
+        add_own((1, 1), 7)
         close_first(FUSED[0])
-        relu((1, 0), "scalar")
+        relu((1, 0))
         close_first(FUSED[1])
         quantize_h(1)
-        relu((1, 1), "vector")
+        nc.vector.tensor_scalar_max(h_bf[2][:, 1, :], pre[1, 1], 0.0)
         close_second(FUSED[0])
         quantize_h(2)
-        second_layer(0, 7)
-        second_layer(1, 3)
+        second_layer(0, 2)
+        second_layer(1, 5)
+        store(0, nc.scalar.copy)
+        store(1, nc.scalar.copy)
         quantize_h(3)
-        second_layer(2, 5)
+        second_layer(2, 6)
+        store(2, nc.scalar.copy)
         close_second(FUSED[1])
-        open_last(3, (6, 4))
+        open_last(3, (7, 3))
         quantize_h(4)
         close_last(3)

@@ -86,10 +86,9 @@ def tile_list_pnet_mix_none_kernel(
 
         c_raw = [staged("c_raw0", [P, PACK, QUARTER], F32, 26624), staged("c_raw1", [P, PACK, QUARTER], F32, 1024)]
         w_raw.append(staged("w_raw1", [P, HALF], I32, 49152 + 4032))
-        shared = staged("shared", [P, 3 * HALF], F32, 9216)
         wc_raw = [
             staged("wc_raw0", [P, PACK, QUARTER], F32, 5120)[:],
-            shared[:, HALF : 3 * HALF].rearrange("p (i r) -> p i r", i=PACK),
+            staged("wc_raw1", [P, PACK, QUARTER], F32, 9216)[:],
             staged("wc_raw2", [P, PACK, QUARTER], F32, 16384)[:],
             staged("wc_raw3", [P, PACK, QUARTER], F32, 20480)[:],
         ]
@@ -174,7 +173,7 @@ def tile_list_pnet_mix_none_kernel(
         pooled = {
             PAIRS[0]: staged("pooled00", [P, 2 * HALF], F32, 26624)[:],
             PAIRS[1]: keep.tile([P, 2 * HALF], F32, name="pooled10")[:],
-            PAIRS[2]: shared[:, 0 : 2 * HALF],
+            PAIRS[2]: keep.tile([P, 2 * HALF], F32, name="pooled01")[:],
         }
         c_bf = [rounded[:, 0:1024], late[:, 2880:3904]]
         c_w = [keep.tile([P, QUARTER], U32, name=f"c_w{u}", align_bytes=64) for u in range(2)]
@@ -350,14 +349,12 @@ def tile_list_pnet_mix_none_kernel(
             if n < len(UNITS) - 1:
                 first_neighbour(n + 1)
             second_neighbour(n)
-            if n < len(UNITS) - 1:
-                pool_neighbours(UNITS[n])
+            pool_neighbours(UNITS[n])
         open_fused(FUSED[0], 0, 3)
         round_wc(0, 0, QUARTER, round_on_gpsimd)
         round_wc(1, 0, QUARTER, round_on_gpsimd)
         wc_w[0] = staged("wc_w0", [P, HALF], U32, CODES_AT)
         quantize_wc(0)
-        pool_neighbours(UNITS[-1])
         round_c(1, 0, QUARTER, nc.scalar.copy)
         quantize_c(1, 0, QUARTER)
         pre[0, 0] = staged("pre00", [P, HALF], BF16, 1024)[:]

@@ -351,6 +351,8 @@ def tile_list_pnet_mix_none_kernel(
             second_neighbour(n)
             pool_neighbours(UNITS[n])
         open_fused(FUSED[0], 0, 3)
+        open_fused(FUSED[0], 1, 4)
+        open_fused(FUSED[1], 0, 5)
         round_wc(0, 0, QUARTER, round_on_gpsimd)
         round_wc(1, 0, QUARTER, round_on_gpsimd)
         wc_w[0] = staged("wc_w0", [P, HALF], U32, CODES_AT)
@@ -361,16 +363,14 @@ def tile_list_pnet_mix_none_kernel(
         pre[0, 1] = staged("pre01", [P, HALF], BF16, 2048)[:]
         add_own((0, 0), 0)
         add_own((0, 1), 1)
-        open_fused(FUSED[0], 1, 0)
-        add_own((0, 2), 4)
-        open_fused(FUSED[1], 0, 1)
+        open_fused(FUSED[1], 1, 0)
+        add_own((0, 2), 7)
         round_wc(2, 0, QUARTER, nc.scalar.copy)
         round_wc(3, 0, SHARE, nc.scalar.copy)
         round_wc(3, SHARE, QUARTER, round_on_gpsimd)
         quantize_wc(1)
         pre[0, 3] = staged("pre03", [P, HALF], BF16, 20480 - 960)[:]
-        add_own((0, 3), 5)
-        open_fused(FUSED[1], 1, 4)
+        add_own((0, 3), 2)
         h_bf[0] = staged("h_bf0", [P, 2, HALF], BF16, 16384)
         h_bf[1] = keep.tile([P, 2, HALF], BF16, name="h_bf1", align_bytes=64)
         relu((0, 0))
@@ -379,7 +379,7 @@ def tile_list_pnet_mix_none_kernel(
         relu((0, 3))
         quantize_h(0)
         add_own((1, 0), 6)
-        add_own((1, 1), 7)
+        add_own((1, 1), 1)
         close_first(FUSED[0])
         relu((1, 0))
         close_first(FUSED[1])
@@ -387,14 +387,14 @@ def tile_list_pnet_mix_none_kernel(
         nc.vector.tensor_scalar_max(h_bf[2][:, 1, :], pre[1, 1], 0.0)
         close_second(FUSED[0])
         quantize_h(2)
-        second_layer(0, 2)
-        second_layer(1, 5)
+        second_layer(0, 7)
+        second_layer(1, 2)
         store(0, nc.scalar.copy)
         store(1, nc.scalar.copy)
         quantize_h(3)
         second_layer(2, 6)
         store(2, nc.scalar.copy)
         close_second(FUSED[1])
-        open_last(3, (7, 3))
+        open_last(3, (1, 3))
         quantize_h(4)
         close_last(3)

from contextlib import ExitStack

import concourse.mybir as mybir

K, R, N, T, J = 512, 1024, 256, 4096, 512
FLOPS = 3 * 2 * K * R * J + 2 * R * N * J

F32 = mybir.dt.float32
BF16 = mybir.dt.bfloat16
I32 = mybir.dt.int32
U32 = mybir.dt.uint32
U16 = mybir.dt.uint16
U8 = mybir.dt.uint8
FP8X4 = mybir.dt.float8_e4m3fn_x4
FP4X4 = mybir.dt.float4_e2m1fn_x4
ALU = mybir.AluOpType
RELU = mybir.ActivationFunctionType.Relu

P = 128
PACK = 4
HALF = P * PACK
JB = 128
QUARTER = 256
TAB_CUT = 1792
SCALE_ROWS = 48
PLANE = 12
SHARE = 48
PLAIN = ((0, 0), (0, 1), (0, 2), (0, 3), (1, 0), (1, 1))
PAIRS = ((0, 0), (1, 0), (0, 1))
UNITS = tuple((g, u, s) for g, u in PAIRS for s in range(2))
FIRST_BANK = (0, 1, 7, 0, 1, 7)
SECOND_BANK = (2, 3, 4, 5, 6, 2)
FUSED = ((1, 2), (1, 3))


def tile_list_pnet_mix_none_kernel(
    tc, tab_words, tab_scales, c, w_words, w_scales, wc, wd8_words, wd8_scales, wd4_words, wd4_scales, offs, out
):
    nc = tc.nc
    with ExitStack() as ctx:
        keep = ctx.enter_context(tc.tile_pool(name="keep", bufs=1))
        stage = ctx.enter_context(tc.tile_pool(name="stage", bufs=1))
        psum = ctx.enter_context(tc.psum_pool(name="psum", bufs=1))

        def bank(n, shape):
            return psum.tile(shape, F32, tag=f"bank{n}", name=f"bank{n}")

        def staged(name, shape, dtype, offset):
            return stage.tile(shape, dtype, name=name, align_bytes=64, offset=offset)

        offsets = keep.tile([P, 2 * J // 16], U16, name="offsets")
        tab_w = keep.tile([P, T], U32, name="tab_w", align_bytes=64)
        tab_s = staged("tab_s", [P, T], U8, 49152)
        ws_raw = staged("ws_raw", [P, 30720], U8, 0)[:, 0:R]
        nc.vector.memset(ws_raw.bitcast(I32), 0)
        nc.vector.memset(tab_s[0:SCALE_ROWS, :].bitcast(I32), 0)
        nc.gpsimd.memset(tab_s[SCALE_ROWS + 16 : P, :].bitcast(I32), 0)

        tab_rows = tab_words[0].rearrange("p t i -> p (t i)").bitcast(I32)
        w_rows = w_words[0].rearrange("p r i -> p (r i)").bitcast(I32)
        wc_rows = wc.rearrange("(p i) r -> p i r", i=PACK)
        c_rows = c.rearrange("(p i) j -> p i j", i=PACK)

        w_raw = [keep.tile([P, HALF], I32, name="w_raw0", align_bytes=64)]
        nc.sync.dma_start(out=tab_s[SCALE_ROWS : SCALE_ROWS + 16, :].bitcast(I32), in_=tab_scales[0].bitcast(I32))
        nc.sync.dma_start(offsets[:], offs)
        nc.sync.dma_start(out=tab_w[:, 0:TAB_CUT].bitcast(I32), in_=tab_rows[:, 0:TAB_CUT])
        for q in range(4):
            nc.sync.dma_start(out=ws_raw[32 * q : 32 * q + 4, :].bitcast(I32), in_=w_scales[0][4 * q : 4 * q + 4, :].bitcast(I32))
        nc.sync.dma_start(out=tab_w[:, TAB_CUT:T].bitcast(I32), in_=tab_rows[:, TAB_CUT:T])
        nc.sync.dma_start(out=w_raw[0][:], in_=w_rows[:, 0:HALF])

        picked = keep.tile([P, 2 * J], U8, name="picked", align_bytes=64)
        nb_s = keep.tile([P, 2 * J], U8, name="nb_s", align_bytes=64)
        nc.vector.tensor_copy(picked[:], tab_s[:].indirect(offsets[:]))
        for q in range(4):
            nc.sync.dma_start(
                out=nb_s[32 * q + PLANE : 32 * q + PLANE + 4, :].bitcast(I32),
                in_=picked[SCALE_ROWS + 4 * q : SCALE_ROWS + 4 * q + 4, :].bitcast(I32),
            )
        w_s = staged("w_s", [P, R], U8, 49152)
        nc.vector.tensor_copy(
            w_s[:].rearrange("p (g t m e) -> p g m t e", g=2, t=PACK, e=16),
            ws_raw.rearrange("p (g m e t) -> p g m t e", g=2, t=PACK, e=16),
        )

        c_raw = [staged("c_raw0", [P, PACK, QUARTER], F32, 26624), staged("c_raw1", [P, PACK, QUARTER], F32, 1024)]
        w_raw.append(staged("w_raw1", [P, HALF], I32, 49152 + 4032))
        wc_raw = [
            staged("wc_raw0", [P, PACK, QUARTER], F32, 5120)[:],
            staged("wc_raw1", [P, PACK, QUARTER], F32, 9216)[:],
            staged("wc_raw2", [P, PACK, QUARTER], F32, 16384)[:],
            staged("wc_raw3", [P, PACK, QUARTER], F32, 20480)[:],
        ]
        wd8_w = staged("wd8_w", [P, N], U32, 24576)
        wd4_w = staged("wd4_w", [P, 2 * N], U8, 25600)
        wd_s = staged("wd_s", [P, 2 * N], U8, 26112)

        def load_c(u):
            nc.sync.dma_start(out=c_raw[u][:], in_=c_rows[:, :, QUARTER * u : QUARTER * (u + 1)])

        def load_wc(v):
            nc.sync.dma_start(out=wc_raw[v], in_=wc_rows[:, :, QUARTER * v : QUARTER * (v + 1)])

        nc.sync.dma_start(out=w_raw[1][:], in_=w_rows[:, HALF:R])
        load_c(0)
        load_wc(0)
        load_wc(1)
        load_c(1)
        load_wc(2)
        load_wc(3)
        nc.sync.dma_start(out=wd8_w[:].bitcast(I32), in_=wd8_words[0].rearrange("p n i -> p (n i)").bitcast(I32))
        nc.sync.dma_start(out=wd4_w[:].bitcast(I32), in_=wd4_words[0].bitcast(I32))
        for g, scales in enumerate((wd8_scales, wd4_scales)):
            for r in range(4):
                nc.sync.dma_start(out=wd_s[r:P:32, N * g : N * (g + 1)].bitcast(I32), in_=scales[0][r:16:4, :].bitcast(I32))

        nb_w = {}
        for u in range(2):
            for a in range(2):
                nb_w[a, u] = keep.tile([P, QUARTER], U32, name=f"nb_w{a}{u}", align_bytes=64)
                first = (J * a + QUARTER * u) // 16
                nc.vector.tensor_copy(nb_w[a, u][:], tab_w[:].indirect(offsets[:, first : first + QUARTER // 16]))

        CODES_AT = 38912
        w_w = [staged("w_w0", [P, HALF], U32, CODES_AT), keep.tile([P, HALF], U32, name="w_w1", align_bytes=64)]

        def order_words(g, lo, hi):
            nc.scalar.copy(
                w_w[g][:].rearrange("p (t m e) -> p m t e", t=PACK, e=4)[:, :, lo:hi, :],
                w_raw[g][:].bitcast(U32).rearrange("p (m e t) -> p m t e", t=PACK, e=4)[:, :, lo:hi, :],
            )

        def neighbour_passes(sums, a, gb):
            g, b = gb
            u, v = divmod(b, 2)
            for t in range(PACK):
                nc.tensor.matmul_mx(
                    out=sums[:, t, :],
                    lhsT=w_w[g][:, P * t : P * (t + 1)].bitcast(FP8X4),
                    lhsT_scale=w_s[:, HALF * g + P * t : HALF * g + P * (t + 1)],
                    rhs=nb_w[a, u][:, JB * v : JB * (v + 1)].bitcast(FP8X4),
                    rhs_scale=nb_s[PLANE:P, J * a + JB * b : J * a + JB * (b + 1)],
                    start=t == 0,
                    stop=False,
                )

        def unit_passes(sums, a, unit):
            g, u, s = unit
            for e in range(2):
                t = 2 * s + e
                nc.tensor.matmul_mx(
                    out=sums[:, e, :],
                    lhsT=w_w[g][:, P * t : P * (t + 1)].bitcast(FP8X4),
                    lhsT_scale=w_s[:, HALF * g + P * t : HALF * g + P * (t + 1)],
                    rhs=nb_w[a, u][:].bitcast(FP8X4),
                    rhs_scale=nb_s[PLANE:P, J * a + QUARTER * u : J * a + QUARTER * (u + 1)],
                    start=True,
                    stop=True,
                )

        def by_point(sums):
            return sums[:].rearrange("p t j -> p j t")

        def as_points(flat):
            return flat.rearrange("p (j t) -> p j t", t=PACK)

        rounded = keep.tile([P, 3008], BF16, name="rounded", align_bytes=64)
        late = keep.tile([P, 3904], BF16, name="late", align_bytes=64)
        firsts = {key: keep.tile([P, HALF], F32, name=f"first{n}")[:] for n, key in enumerate(UNITS[0:3] + UNITS[4:5] + FUSED)}
        firsts[UNITS[3]] = late[:, 2880:3904].bitcast(F32)
        firsts[UNITS[5]] = late[:, 0:1024].bitcast(F32)
        pooled = {
            PAIRS[0]: staged("pooled00", [P, 2 * HALF], F32, 26624)[:],
            PAIRS[1]: keep.tile([P, 2 * HALF], F32, name="pooled10")[:],
            PAIRS[2]: keep.tile([P, 2 * HALF], F32, name="pooled01")[:],
        }
        c_bf = [rounded[:, 0:1024], late[:, 2880:3904]]
        c_w = [keep.tile([P, QUARTER], U32, name=f"c_w{u}", align_bytes=64) for u in range(2)]
        c_s = [keep.tile([P, QUARTER], U8, name=f"c_s{u}", align_bytes=64) for u in range(2)]
        wc_bf = [
            rounded[:, 960:3008].rearrange("p (t m i) -> p t m i", t=PACK, i=PACK),
            late[:, 960:3008].rearrange("p (t m i) -> p t m i", t=PACK, i=PACK),
        ]
        wc_w = {1: keep.tile([P, HALF], U32, name="wc_w1", align_bytes=64)}
        wc_s = [keep.tile([P, HALF], U8, name=f"wc_s{g}", align_bytes=64) for g in range(2)]

        def round_on_gpsimd(dst, src):
            nc.gpsimd.tensor_scalar(dst, src, 1.0, 0.0, ALU.mult, ALU.add)

        def round_c(u, lo, hi, copy):
            copy(
                c_bf[u][:, PACK * lo : PACK * hi].rearrange("p (a j i) -> p a i j", j=PACK, i=PACK),
                c_raw[u][:, :, lo:hi].rearrange("p i (a j) -> p a i j", j=PACK),
            )

        def round_wc(v, lo, hi, copy):
            g, first = divmod(QUARTER * v, HALF)
            dst = wc_bf[g][:, :, (first + lo) // PACK : (first + hi) // PACK, :].rearrange("p t m i -> p m t i")
            copy(dst, wc_raw[v][:, :, lo:hi].rearrange("p i (m t) -> p m t i", t=PACK))

        def quantize(words, scales, values):
            nc.vector.quantize_mx(out=words.bitcast(FP8X4), scales=scales, in_=values)

        def quantize_c(u, lo, hi):
            quantize(c_w[u][:, lo:hi], c_s[u][:, lo:hi], c_bf[u][:, PACK * lo : PACK * hi])

        def quantize_wc(g):
            for lo in (0, 2):
                cols = slice(P * lo, P * (lo + 2))
                quantize(wc_w[g][:, cols], wc_s[g][:, cols], wc_bf[g][:, lo : lo + 2, :, :].rearrange("p t m i -> p (t m i)"))

        def own_passes(sums, gb, closed):
            g, b = gb
            u, v = divmod(b, 2)
            for t in range(PACK):
                nc.tensor.matmul_mx(
                    out=sums[:, t, :],
                    lhsT=wc_w[g][:, P * t : P * (t + 1)].bitcast(FP8X4),
                    lhsT_scale=wc_s[g][:, P * t : P * (t + 1)],
                    rhs=c_w[u][:, JB * v : JB * (v + 1)].bitcast(FP8X4),
                    rhs_scale=c_s[u][:, JB * v : JB * (v + 1)],
                    start=closed,
                    stop=closed or t == PACK - 1,
                )

        seconds = {}

        def as_pairs(flat):
            return flat.rearrange("p (j e) -> p j e", e=2)

        def first_neighbour(n):
            unit = UNITS[n]
            a0 = bank(FIRST_BANK[n], [P, 2, QUARTER])
            unit_passes(a0, 0, unit)
            nc.scalar.copy(as_pairs(firsts[unit]), by_point(a0))

        def second_neighbour(n):
            unit = UNITS[n]
            seconds[unit] = bank(SECOND_BANK[n], [P, 2, QUARTER])
            unit_passes(seconds[unit], 1, unit)

        def pool_neighbours(unit):
            g, u, s = unit
            nc.vector.tensor_tensor(
                as_pairs(pooled[g, u][:, HALF * s : HALF * (s + 1)]), by_point(seconds[unit]), as_pairs(firsts[unit]), ALU.max
            )

        groups = [[(0, 0), (0, 1)], [(0, 2), (0, 3)], [(1, 0), (1, 1)], [(1, 2)], [(1, 3)]]
        place = {gb: (n, group.index(gb)) for n, group in enumerate(groups) for gb in group}
        pre = {gb: keep.tile([P, HALF], BF16, name=f"pre{gb[0]}{gb[1]}")[:] for gb in ((0, 2), (1, 0), (1, 1))}
        h_bf = {n: keep.tile([P, 1, HALF], BF16, name=f"h_bf{n}", align_bytes=64) for n in (3, 4)}
        h_bf[2] = keep.tile([P, 2, HALF], BF16, name="h_bf2", align_bytes=64)
        h_w = [keep.tile([P, len(group) * JB], U32, name=f"h_w{n}", align_bytes=64) for n, group in enumerate(groups)]
        h_s = [keep.tile([P, len(group) * JB], U8, name=f"h_s{n}", align_bytes=64) for n, group in enumerate(groups)]

        def add_own(gb, at):
            ac = bank(at, [P, PACK, JB])
            own_passes(ac, gb, True)
            g, b = gb
            u, v = divmod(b, 2)
            nc.vector.tensor_tensor(
                pre[gb].rearrange("p (j s e) -> p j s e", s=2, e=2),
                ac[:].rearrange("p (s e) j -> p j s e", s=2),
                pooled[g, u].rearrange("p (s j e) -> p j s e", s=2, e=2)[:, JB * v : JB * (v + 1), :, :],
                ALU.add,
            )

        def relu(gb):
            n, e = place[gb]
            nc.scalar.activation(h_bf[n][:, e, :], pre[gb], RELU)

        def quantize_h(n):
            quantize(h_w[n][:], h_s[n][:], h_bf[n][:, :, :].rearrange("p e x -> p (e x)"))

        fused_sums = {}

        def open_fused(gb, a, at):
            fused_sums[gb, a] = bank(at, [P, PACK, JB])
            neighbour_passes(fused_sums[gb, a], a, gb)

        def close_first(gb):
            own_passes(fused_sums[gb, 0], gb, False)
            nc.scalar.copy(as_points(firsts[gb]), by_point(fused_sums[gb, 0]))

        def close_second(gb):
            n, e = place[gb]
            own_passes(fused_sums[gb, 1], gb, False)
            nc.vector.scalar_tensor_tensor(
                as_points(h_bf[n][:, e, :]), by_point(fused_sums[gb, 1]), 0.0, as_points(firsts[gb]), ALU.max, ALU.max
            )

        out_rows = out.rearrange("(x p) j -> p x j", p=P)

        def second_pass(y, x, g, b, start, stop):
            n, e = place[(g, b)]
            if g == 0:
                lhsT = wd8_w[:, P * x : P * (x + 1)].bitcast(FP8X4)
            else:
                lhsT = wd4_w[:, 2 * P * x : 2 * P * (x + 1)].bitcast(FP4X4)
            nc.tensor.matmul_mx(
                out=y,
                lhsT=lhsT,
                lhsT_scale=wd_s[:, N * g + P * x : N * g + P * (x + 1)],
                rhs=h_w[n][:, JB * e : JB * (e + 1)].bitcast(FP8X4),
                rhs_scale=h_s[n][:, JB * e : JB * (e + 1)],
                start=start,
                stop=stop,
            )

        ys = {}

        def second_layer(b, at):
            ys[b] = bank(at, [P, 2, JB])
            for g in range(2):
                for x in range(2):
                    second_pass(ys[b][:, x, :], x, g, b, g == 0 and x == 0, g == 1 and x == 1)

        def store(b, copy):
            res = keep.tile([P, 2, JB], F32, name=f"res{b}")
            copy(res[:], ys[b][:])
            nc.sync.dma_start(out=out_rows[:, :, JB * b : JB * (b + 1)], in_=res[:])

        last_y = []

        def open_last(b, at):
            for x in range(2):
                last_y.append(bank(at[x], [P, JB]))
                second_pass(last_y[x][:], x, 0, b, True, False)

        def close_last(b):
            for x in range(2):
                second_pass(last_y[x][:], x, 1, b, False, True)
            res = [keep.tile([P, JB], F32, name=f"last_res{x}") for x in range(2)]
            nc.scalar.copy(res[0][:], last_y[0][:])
            nc.sync.dma_start(out=out_rows[:, 0, JB * b : JB * (b + 1)], in_=res[0][:])
            nc.vector.tensor_copy(res[1][:], last_y[1][:])
            nc.scalar.dma_start(out=out_rows[:, 1, JB * b : JB * (b + 1)], in_=res[1][:])

        order_words(0, 0, 2)
        order_words(0, 2, 4)
        for lo in (0, JB):
            round_c(0, lo, lo + JB, nc.vector.tensor_copy)
        for lo in (0, JB):
            quantize_c(0, lo, lo + JB)
        order_words(1, 0, 4)
        first_neighbour(0)
        for n in range(len(UNITS)):
            if n < len(UNITS) - 1:
                first_neighbour(n + 1)
            second_neighbour(n)
            pool_neighbours(UNITS[n])
        open_fused(FUSED[0], 0, 3)
        open_fused(FUSED[0], 1, 4)
        open_fused(FUSED[1], 0, 5)
        round_wc(0, 0, QUARTER, round_on_gpsimd)
        round_wc(1, 0, QUARTER, round_on_gpsimd)
        wc_w[0] = staged("wc_w0", [P, HALF], U32, CODES_AT)
        quantize_wc(0)
        round_c(1, 0, QUARTER, nc.scalar.copy)
        quantize_c(1, 0, QUARTER)
        pre[0, 0] = staged("pre00", [P, HALF], BF16, 1024)[:]
        pre[0, 1] = staged("pre01", [P, HALF], BF16, 2048)[:]
        add_own((0, 0), 0)
        add_own((0, 1), 1)
        open_fused(FUSED[1], 1, 0)
        add_own((0, 2), 7)
        round_wc(2, 0, QUARTER, nc.scalar.copy)
        round_wc(3, 0, SHARE, nc.scalar.copy)
        round_wc(3, SHARE, QUARTER, round_on_gpsimd)
        quantize_wc(1)
        pre[0, 3] = staged("pre03", [P, HALF], BF16, 20480 - 960)[:]
        add_own((0, 3), 2)
        h_bf[0] = staged("h_bf0", [P, 2, HALF], BF16, 16384)
        h_bf[1] = keep.tile([P, 2, HALF], BF16, name="h_bf1", align_bytes=64)
        relu((0, 0))
        relu((0, 1))
        relu((0, 2))
        relu((0, 3))
        quantize_h(0)
        add_own((1, 0), 6)
        add_own((1, 1), 1)
        close_first(FUSED[0])
        relu((1, 0))
        close_first(FUSED[1])
        quantize_h(1)
        nc.vector.tensor_scalar_max(h_bf[2][:, 1, :], pre[1, 1], 0.0)
        close_second(FUSED[0])
        quantize_h(2)
        second_layer(0, 7)
        second_layer(1, 2)
        store(0, nc.scalar.copy)
        store(1, nc.scalar.copy)
        quantize_h(3)
        second_layer(2, 6)
        store(2, nc.scalar.copy)
        close_second(FUSED[1])
        open_last(3, (1, 3))
        quantize_h(4)
        close_last(3)
